import numpy as np, ml_dtypes
CORES = [35,38,43,46]
N = 4
import mx_ref
BF = ml_dtypes.bfloat16
def gentries(a):
    return np.ascontiguousarray(a.reshape(8, 16, -1).transpose(0, 2, 1)).reshape(8, -1)
def gtable(e):
    e = np.asarray(e); return np.ascontiguousarray(e.reshape(8, -1, 16).transpose(0, 2, 1)).reshape(128, -1).astype(np.int32)
def gcols(t, e):
    v = np.concatenate([t.reshape(8, 16, -1, 4), np.zeros((8, 16, 1, 4), BF)], axis=2)
    return np.ascontiguousarray(np.stack([v[g][:, e[g]] for g in range(8)])).reshape(128, -1)
def tile(rs):
    return np.stack(rs, axis=2).reshape(128, -1).astype(BF)
def pick(q, e):
    c = np.concatenate([q[0].reshape(128, -1, 4), np.zeros((128, 1, 4), np.uint8)], axis=1); s = np.concatenate([q[1], np.ones((16, 1), np.uint8)], axis=1)
    return (np.ascontiguousarray(c[:, e].reshape(128, -1)), np.ascontiguousarray(s[:, e]))
def join(*qs):
    return (np.concatenate([q[0] for q in qs], axis=1), np.concatenate([q[1] for q in qs], axis=1))
def put(q, e, v):
    c, s = q[0].reshape(128, -1, 4).copy(), q[1].copy(); c[:, e] = v[0].reshape(128, -1, 4); s[:, e] = v[1]
    return (c.reshape(128, -1), s)
def pk(c, s):
    return (np.ascontiguousarray(c), mx_ref.live(s))
def emit(q):
    return q[0], q[1]
def packed(v, rng):
    q = [mx_ref.quantize(np.ascontiguousarray(v[r])) for r in range(N)]
    return np.stack([a for a, b in q]), np.stack([mx_ref.plane(b, rng) for a, b in q])
def values_of_codes():
    e, c = np.zeros((128, 128, 4), np.float32), np.zeros((128, 2, 4), np.uint8)
    e[np.arange(128), np.arange(128), 0] = 1
    c[:127, :, 0] = np.arange(256).reshape(2, 128).T[:127]
    return mx_ref.matmul(mx_ref.quantize(e.reshape(128, 512).astype(BF)), (c.reshape(128, 8), np.full((16, 2), 127, np.uint8))).T.reshape(-1).astype(np.float64)
CODE_VALUE, SCALE_VALUE = values_of_codes(), 2.0 ** (np.arange(256) - 127.0)
def decode(q):
    return (CODE_VALUE[q[0]].reshape(16, 8, -1, 4) * SCALE_VALUE[q[1]][:, None, :, None] + 0.0).reshape(128, -1).astype(np.float32)
def f(rng, *shape):
    return mx_ref.flush((rng.standard_normal(shape, dtype=np.float32) * np.exp2(rng.integers(-2, 3, shape[:-1] + (1,)))).astype(BF))
def wide(rng, *shape, cols=0):
    v = rng.standard_normal(shape, dtype=np.float32) * np.exp2(rng.integers(-12, 13, shape)).astype(np.float32)
    if cols: v *= np.repeat(np.exp2(rng.integers(-cols, cols + 1, shape[:-2] + (1, shape[-1] // 4))) * (rng.random(shape[:-2] + (1, shape[-1] // 4)) > 0.0625), 4, axis=-1).astype(np.float32)
    return mx_ref.flush(v.astype(BF))
C, S, R, SWEEPS = 320, 160, 3, 8
def big(v):
    v = v.astype(np.float32)
    v[np.abs(v) < np.float32(2.0 ** -16)] = 0
    return v
def numbers_of(rng):
    return big(f(rng, N, 128, 4 * C)).reshape(N, 8, 16, C, 4), f(rng, N, 128, 512).astype(np.float32).reshape(N, 128, 128, 4), f(rng, N, 128, 512).astype(np.float32)
def ring(rng, e):
    s, i, n = rng.permutation(C), np.arange(C), np.zeros((3, C), np.int64)
    n[0, s] = s[i ^ 1]
    n[1, s] = s[(((i + 1) ^ 1) - 1) % C]
    n[2, s[e]] = s[e[i ^ 1]]
    return n[rng.permutation(3)], s
def beside(a, b):
    return (a - b) % C in (1, C - 1)
def chords(rng):
    e = rng.permutation(C)
    for i in range(0, C, 2):
        if beside(e[i], e[i + 1]):
            for j in range(0, C, 2):
                if j != i and not beside(e[i], e[j + 1]) and not beside(e[j], e[i + 1]):
                    e[i + 1], e[j + 1] = e[j + 1], e[i + 1]
                    break
    return e
def opposite():
    i = np.arange(S)
    return np.stack([i, i + S], axis=1).reshape(-1)
def crossed(rng):
    i = 2 * np.arange(S)
    return np.stack([i, (i + 2 * rng.integers(1, S - 1) + 1) % C], axis=1).reshape(-1)
def fours(rng):
    s, i, n = rng.permutation(C), np.arange(C), np.zeros((3, C), np.int64)
    for k in range(3): n[k, s] = s[i ^ (k + 1)]
    return n
def graphs(rng):
    return np.stack([np.stack([ring(rng, chords(rng))[0] for g in range(8)]) for r in range(N)])
def layers(rng, still=()):
    w = (big(f(rng, N, 128, 2048)) * np.float32(0.03125)).reshape(N, 128, 512, 4)
    w *= np.where(np.sum(np.abs(w), axis=(1, 3), keepdims=True) > 28.0, 0.5, 1.0)
    w = w.reshape(N, 8, 16, 4, 8, 16, 4)
    for i in still:
        w[:, :, i] = 0
        w[:, :, :, :, :, i] = 0
    return w
def drawn(rng, x, u, v, n, w):
    c, s = packed(np.ascontiguousarray(w).reshape(N, 128, 2048).astype(np.float32).astype(BF), rng)
    e = [np.stack([gtable(n[r, :, k]) for r in range(N)]) for k in range(3)]
    return {"x": x.reshape(N, 128, 4 * C).astype(np.float32).astype(BF), "u": u.reshape(N, 128, 512).astype(np.float32).astype(BF), "v": v.reshape(N, 128, 512).astype(np.float32).astype(BF), "n0": e[0], "n1": e[1], "n2": e[2], "wc": c, "ws": s}
def whole(x, u, s, i, k):
    for m in range(3):
        x[:, i + m] = ((s[:, :, None] >> (4 * m + np.arange(4))) & 1) * (2.0 ** (4 * m + np.arange(4)) * k)
        for h in range(0, 128, 16): u[h + i + m, h] = 1.0
def setup_inputs(rng):
    x, u, v = numbers_of(rng)
    return drawn(rng, x, u, v, graphs(rng), layers(rng))
def setup_inputs_ties(rng):
    x, u, v = numbers_of(rng)
    n, o = graphs(rng), rng.permutation(N)
    u[:, :, ::16] = 0
    for r in range(N):
        whole(x[r], u[r], rng.integers(0, 3, (8, C)), 0, 1.0)
        if o[r] == 0: u[r][:, ::16] = 0
        if o[r] == 1: u[r][:, ::16] *= -1
        if o[r] == 2: n[r] = np.stack([fours(rng) for g in range(8)])
    return drawn(rng, x, u, v, n, layers(rng, (0, 1, 2)))
def setup_inputs_near(rng):
    x, u, v = numbers_of(rng)
    o = rng.permutation(N) % 4
    x[:, :, 0] = 0
    x[:, :, 8:] = 0
    u[:, :, ::16] = 0
    for r in range(N):
        b, k = rng.integers(0, 2, (8, C)), rng.permutation(8)
        x[r, :, 0, :, 0] = [1.0, -1.0, 1.0, 0.0][o[r]]
        if o[r] < 3:
            whole(x[r], u[r], rng.integers(0, 256, (8, C)), 8, 2.0 ** -23)
            x[r, :, 11, :, 0] = 2.0 ** -10
        else:
            x[r, :, 12, :, 0] = 2.0 ** -28 * (1 - b)
            x[r, :, 13, :, 0] = 1.125 * 2.0 ** -28 * b
            for g in k[2:6]: x[r, g, 14, :, 0] = 2.0 ** -28
        for g in k[:4]: x[r, g, 0, rng.integers(C), 0] = rng.choice([-1.0, 1.0]) * 2.0 ** 26
        for h in range(0, 128, 16):
            u[r, h, h, 0] = 1.0
            u[r, h + 11, h, 0] = 1.0
            u[r, h + 12, h, 0] = 1.25
            u[r, h + 13, h, 0] = 1.125
            u[r, h + 14, h, 0] = -1.25
        if o[r] >= 2: u[r][:, ::16] *= 2.0 ** -30
    return drawn(rng, x, u, v, graphs(rng), layers(rng, (0, 8, 9, 10, 11, 12, 13, 14, 15)))
def setup_inputs_long(rng):
    x, u, v = numbers_of(rng)
    k = (N, 8, 8, C, 4)
    x[:, :, 8:] = rng.choice([-1.0, 1.0], k) * (1.0078125 + 0.015625 * rng.integers(0, 64, k)) * 2.0 ** -rng.integers(8, 15, k)
    x[:, :, 8, :, 0] = 1.96875
    u[:, :, ::16] = 0
    n, o, t = np.zeros((N, 8, 3, C), np.int64), (np.arange(N) + rng.integers(N)) % N // (N // 2), np.arange(C)
    for r in range(N):
        s = np.zeros((8, C), np.int64)
        for g in range(8):
            n[r, g], a = ring(rng, crossed(rng) if o[r] else opposite())
            s[g, a] = 512 * (1 - t % 2) + rng.permutation(C) if o[r] else C - 1 - t
        whole(x[r], u[r], s, 0, 1.0)
    return drawn(rng, x, u, v, n, layers(rng, (0, 1, 2)))
def setup_inputs_ends(rng):
    x, u, v = numbers_of(rng)
    o, k, h = rng.permutation(N) % 4, rng.permutation(N) % 2, rng.permutation(8)
    sg = rng.choice([-1.0, 1.0], (8, 16, 4))
    sg[h[:4]] = rng.choice([-1.0, 1.0])
    row, i = sg.reshape(128, 4), np.arange(128)
    n, w = graphs(rng), np.zeros((N, 128, 4, 128, 4), np.float32)
    for r in range(N):
        c = rng.permutation(C) % 2 == 0
        size, turn = 2.0 ** 30, np.ones((8, 16, 1, 1))
        if o[r] == 0:
            m, s = ring(rng, crossed(rng))
            n[r] = m
            a = 0.9 + 0.1 * rng.random((8, 16, C, 4))
            a[:, :, s[::2]] -= 0.15
            a *= 2.0 ** 26
        elif o[r] == 1:
            n[r] = np.stack([fours(rng) for g in range(8)])
            a = np.ones((8, 16, C, 4)) * np.where(c, 2.0 ** 26, 2.0 ** 25)[:, None]
            a[h[4:]] = np.where(c, 2.0 ** 25, 2.0 ** 26)[:, None]
            turn[h[4:]] = -1
        elif o[r] == 2: a, size = 2.0 ** -30, 2.0 ** -30
        else: a = np.where(c, 2.0 ** 26, 2.0 ** -30)[:, None]
        x[r] = a * sg[:, :, None]
        u[r] = size * row[:, None] * (turn * np.ones((1, 16, 1, 1))).reshape(128, 1, 1) * rng.choice([-1.0, 1.0], (1, 128, 1))
        v[r] = (size * row[:, None] * rng.choice([-1.0, 1.0], (1, 128, 1))).reshape(128, 512)
        if k[r]:
            for b in range(4): w[r, i, b, i, b] = 32
        else: w[r] = 0.0625 * row[:, None, None] * row.T[None, :, :, None]
    return drawn(rng, x, u, v, n, w)
def setup_inputs_spread(rng):
    x, u, v = numbers_of(rng)
    return drawn(rng, big(wide(rng, N, 128, 4 * C, cols=6)), u, v, graphs(rng), layers(rng))
def check_inputs(d):
    b = []
    for k, t in (("x", 26), ("u", 30), ("v", 30)):
        a = np.abs(d[k].astype(np.float32))
        if not (np.isfinite(a).all() and ((a == 0) | (a >= 2.0 ** -30) & (a <= 2.0 ** t)).all()): b.append("a value of " + k)
    none, least, most = [emit(mx_ref.quantize(np.full((128, 16), k, np.float32).astype(BF)))[1][0, 0] for k in (0.0, 2.0 ** -30, 2.0 ** 30)]
    i = np.arange(C)
    for r in range(N):
        n = [gentries(d[k][r]) for k in ("n0", "n1", "n2")]
        if not all([((e >= 0) & (e < C)).all() for e in n]): b.append("an entry of n0, n1 or n2")
        else:
            if any([(np.take_along_axis(e, e, axis=1) != i).any() or (e == i).any() for e in n]): b.append("n0, n1, n2: nodes not in pairs")
            if ((n[0] == n[1]) | (n[0] == n[2]) | (n[1] == n[2])).any(): b.append("n0, n1, n2: equal neighbours")
        if ((d["wc"][r] & 0x7F) == 0x7F).any(): b.append("wc: a code that is no number")
        s = mx_ref.live(d["ws"][r])
        if ((s != none) & ((s < least) | (s > most))).any(): b.append("ws: a scale out of range")
        if not (np.sum(np.abs(decode(pk(d["wc"][r], d["ws"][r]))).reshape(128, 512, 4), axis=(0, 2), dtype=np.float64) <= 32).all(): b.append("W: the sizes of a column")
    return b
def look(t, e):
    return np.where(e < 0, -1, np.take_along_axis(t, np.maximum(e, 0), axis=2))
def around(t, nb):
    return np.stack([np.take_along_axis(t, e, axis=2) for e in nb])
def best(t, nb):
    a = around(t, nb)
    return np.where(np.max(a, axis=0) < 0, -1, np.take_along_axis(nb, np.argmax(a, axis=0)[None], axis=0)[0])
def reference(x, u, v, n0, n1, n2, wc, ws):
    qu = [mx_ref.quantize(u[r]) for r in range(N)]
    lay = [pk(wc[r], ws[r]) for r in range(N)]
    now = [x[r] for r in range(N)]
    nb = np.stack([np.stack([gentries(n[r]) for r in range(N)]) for n in (n0, n1, n2)]).astype(np.int64)
    node = np.arange(C)
    for t in range(R):
        qx = [mx_ref.quantize(now[r]) for r in range(N)]
        full = [decode(qx[r]).astype(BF) for r in range(N)]
        score = np.stack([mx_ref.matmul(qu[r], qx[r])[::16] for r in range(N)]) + np.float32(0.0)
        z = C - 1 - np.argsort(np.argsort(-score, axis=2, kind="stable"), axis=2)
        state = np.zeros((N, 8, C), np.int64)
        for i in range(SWEEPS):
            key = np.where(state == 0, 512 * np.count_nonzero(around(state, nb) == 2, axis=0) + z, -1)
            win = key > np.max(around(key, nb), axis=0)
            state[win] = 1
            state[(state == 0) & np.any(around(win, nb), axis=0)] = 2
        coarse = state == 1
        o = np.argsort(~coarse, axis=2, kind="stable")
        slot, head = np.argsort(o, axis=2), o[:, :, :S]
        c = np.where(np.take_along_axis(coarse, head, axis=2), head, -1)
        fine = best(np.where(coarse, -1, z), nb)
        p1 = np.where(coarse, node, best(np.where(coarse, z, -1), nb))
        p2 = np.where(coarse, node, np.where(fine < 0, p1, look(p1, fine)))
        cf, s1, s2 = look(fine, c), look(slot, p1), look(slot, p2)
        qe = []
        for r in range(N):
            e = (gcols(full[r], c[r]).astype(np.float32) + gcols(full[r], cf[r]).astype(np.float32)) * np.float32(0.5)
            qe.append(mx_ref.quantize(e.astype(BF)))
        for r in range(N):
            h = tile([mx_ref.matmul(pick(lay[r], np.arange(128 * b, 128 * b + 128)), qe[r - 1]) * np.float32(0.03125) for b in range(4)])
            add = ((gcols(h, s1[r]).astype(np.float32) + gcols(h, s2[r]).astype(np.float32)) * np.float32(0.5)).astype(BF)
            now[r] = (full[r].astype(np.float32) + add.astype(np.float32)).astype(BF)
    y, op = np.zeros((N, 128, C), np.float32), np.zeros((N, 8, C), np.float32)
    oc, osc = np.zeros((N, 128, 4 * C), np.uint8), np.zeros((N, 16, C), np.uint8)
    for r in range(N):
        q = mx_ref.quantize(now[r])
        y[r] = mx_ref.matmul(mx_ref.quantize(v[r]), q)
        op[r] = p1[r]
        oc[r], osc[r] = emit(q)
    return {"y": y, "op": op, "oc": oc, "osc": osc}

@@ -1,0 +1,529 @@
+from concourse.mybir import dt, AluOpType, ActivationFunctionType
+
+ALU = AluOpType
+ACT = ActivationFunctionType
+C, S, ROUNDS, SWEEPS = 320, 160, 3, 8
+FW, HW = 336, 176
+BIG = 512.0
+TINY = 2.0 ** -110
+HOP1_S, HOP2_S, HOP3_S = True, False, False
+HALVES = False
+
+F32, B16, I32, U16, Q8, U8 = "float32", "bfloat16", "int32", "uint16", "float8_e4m3fn_x4", "uint8"
+SCRATCH = {}
+
+
+def _sb(names, n, d):
+    for k in names.split():
+        SCRATCH[k] = ("sbuf", [128, n], d)
+
+
+_sb("xin xa", 4 * C, B16)
+_sb("uin vin", 512, B16)
+_sb("eb", 2048, B16)
+_sb("one", 512, B16)
+_sb("mone isa inc yy jm nmask e1", C, B16)
+_sb("mask keep mx x1g ex", 3 * C, B16)
+_sb("qx", C, Q8)
+_sb("sx", C, U8)
+_sb("qu qv qup", 128, Q8)
+_sb("su sv sup", 128, U8)
+_sb("qw qeb", 512, Q8)
+_sb("sw seb", 512, U8)
+for _r in range(ROUNDS):
+    _sb("qe%d lq%d" % (_r, _r), S, Q8)
+    _sb("se%d ls%d" % (_r, _r), S, U8)
+_sb("nin", 64, I32)
+_sb("pidx pmi", 8, I32)
+_sb("mi mj", 64, I32)
+_sb("nu lu sl mu", 64, U16)
+_sb("upk mnu posu cu destu cposu topu", 32, U16)
+_sb("s12u", 48, U16)
+_sb("iota pi1 pos1", FW, F32)
+_sb("nrep posn gp exf", 2 * C, F32)
+_sb("sc prep yo", C, F32)
+_sb("sg sgx", 3 * C, F32)
+_sb("win", 3 * S, F32)
+_sb("tabp", HW, F32)
+_sb("pc", 8, F32)
+_sb("i16 own k2 off t20", 32, F32)
+_sb("nw xn cz wp wm tp tf", 80, F32)
+_sb("nf mw tau tauo dd bb do eo ww l1 l2 t40 t41", 64, F32)
+_sb("kw ci", 2 * C, B16)
+_sb("cc gg g2 lo2 a1 a2 a3 n2g u1 uu k1 x1 r1 r2", C, B16)
+_sb("sp", S, B16)
+_sb("tabx", 3 * S, B16)
+_sb("fn f2", 4 * FW, B16)
+_sb("et e2", 4 * S, B16)
+_sb("hh", 4 * HW, B16)
+_sb("t2 tt", 4 * C, B16)
+SCRATCH["pd"] = ("psum", [128, 2048], F32)
+SCRATCH["ph"] = ("psum", [128, 2048], F32)
+
+SEMAPHORES = ["cv", "cs", "ct", "cg", "sent", "arr0", "arr1", "arr2"] + ["d%d" % _k for _k in range(24)]
+
+
+def rank_program(g, core, T, topo):
+    rank = T.rank_of(core)
+    if rank is None:
+        return
+    nr = len(T.cores)
+    nxt, prv = T.cores[(rank + 1) % nr], T.cores[(rank - 1) % nr]
+    ops = []
+
+    def A(name, a, b, st=1):
+        ap = T[name][:, a:b:st] if st != 1 else T[name][:, a:b]
+        if SCRATCH[name][0] == "psum":
+            a, b = a // 512 * 512, (b + 511) // 512 * 512
+        return (ap, [(name, a, b)])
+
+    def IND(w, o):
+        return (w[0].indirect(o[0]), w[1] + o[1])
+
+    def val(x):
+        return x[0] if isinstance(x, tuple) else x
+
+    def add(q, fn, outs, ins, sem=None, n=1):
+        rd, wr = [], []
+        for x in ins:
+            if isinstance(x, tuple):
+                rd += x[1]
+        for x in outs:
+            wr += x[1]
+        ops.append({"q": q, "fn": fn, "r": rd, "w": wr, "sem": sem, "n": n, "used": False})
+
+    def tt(o, a, b, op):
+        add("v", lambda: g.vector.tensor_tensor(o[0], a[0], b[0], op), [o], [a, b])
+
+    def ts(o, a, s1, op0, s2=None, op1=None):
+        if op1 is None:
+            add("v", lambda: g.vector.tensor_scalar(o[0], a[0], val(s1), None, op0), [o], [a, s1])
+        else:
+            add("v", lambda: g.vector.tensor_scalar(o[0], a[0], val(s1), val(s2), op0, op1), [o], [a, s1, s2])
+
+    def cp(o, a):
+        add("v", lambda: g.vector.tensor_copy(o[0], a[0]), [o], [a])
+
+    def scatter(w, off, a):
+        add("v", lambda: g.vector.tensor_copy(w[0].indirect(off[0]), a[0]), [w], [a, off])
+
+    def fill(o, c):
+        add("v", lambda: g.vector.memset(o[0], c), [o], [])
+
+    def scan(o, d0, d1, init, op0, op1):
+        add("v", lambda: g.vector.tensor_tensor_scan(o[0], d0[0], d1[0], init, op0, op1), [o], [d0, d1])
+
+    def pick(o, d, n):
+        scan(o, A("mx", 0, n), d, 0.0, ALU.mult, ALU.max)
+
+    def quant(q, s, a):
+        add("v", lambda: g.vector.quantize_mx(q[0], s[0], a[0]), [q, s], [a])
+
+    def act(o, a, scale=1.0, bias=0.0):
+        f = ACT.Copy if bias == 0.0 else ACT.Identity
+        add("s", lambda: g.scalar.activation(o[0], a[0], f, bias=bias, scale=scale), [o], [a])
+
+    def mm(o, wq, ws, xq, xs):
+        add("t", lambda: g.tensor.matmul_mx(o[0], wq[0], ws[0], xq[0], xs[0], True, True), [o], [wq, ws, xq, xs])
+
+    def iota(o, pat, base, cm, flag):
+        if flag:
+            add("g", lambda: g.iota(o[0], pat, base, cm, allow_small_or_imprecise_dtypes=True), [o], [])
+        else:
+            add("g", lambda: g.iota(o[0], pat, base, cm), [o], [])
+
+    nd = [0]
+
+    def dma(q, o, a, outs, ins):
+        e = {"y": g.sync, "s": g.scalar}[q]
+        add(q, lambda: e.dma_start(o, a), outs, ins, sem="d%d" % nd[0], n=16)
+        nd[0] += 1
+
+    def w16(name, a, b):
+        return A(name, 16 * a + 15, 16 * b, 16)
+
+    SCL = A("pc", 2, 3)
+
+    for k, t in enumerate((T.n0, T.n1, T.n2)):
+        dma("y", T.nin[:, 20 * k:20 * k + 20], t[:], [A("nin", 20 * k, 20 * k + 20)], [])
+    dma("s", T.xin[:], T.x[:], [A("xin", 0, 4 * C)], [])
+    dma("s", T.uin[:], T.u[:], [A("uin", 0, 512)], [])
+
+    iota(A("pidx", 0, 1), [[1, 1]], 0, 1, False)
+    iota(A("i16", 0, 20), [[16, 20]], 0, 0, True)
+    iota(A("iota", 0, FW), [[1, FW]], 0, 0, True)
+    iota(A("jm", 0, C), [[0, 20], [1, 16]], 0, 0, True)
+    fill(A("one", 0, 512), 1.0)
+    for b in range(4):
+        o, i = A("eb", 512 * b, 512 * b + 512), A("one", 0, 512)
+        add("g", (lambda o, i, b: lambda: g.affine_select(o[0], i[0], [[-1, 512]], ALU.is_equal, 0.0, b, 4))(o, i, b), [o], [i])
+    ts(A("pmi", 0, 1), A("pidx", 0, 1), 15, ALU.bitwise_and)
+    fill(A("mone", 0, C), -1.0)
+    cp(A("pc", 0, 1), A("pmi", 0, 1))
+    cp(A("upk", 0, 8), A("i16", 0, 8))
+    fill(A("wp", 0, 20), 8192.0)
+    ts(A("pc", 1, 2), A("pc", 0, 1), 1.0, ALU.add)
+    ts(SCL, A("pc", 0, 1), 15.0, ALU.is_equal, 1.0 / BIG, ALU.max)
+    ts(A("own", 0, 20), A("i16", 0, 20), A("pc", 0, 1), ALU.add)
+    fill(A("fn", C, 4 * FW, FW), 0.0)
+    ts(A("pc", 3, 4), SCL, -BIG, ALU.mult)
+    fill(A("f2", C, 4 * FW, FW), 0.0)
+    fill(A("hh", 0, 4 * HW, HW), 0.0)
+    fill(A("tabx", S, 3 * S), 1.0)
+    fill(A("tabp", 0, 1), -1.0)
+    ts(A("k2", 0, 20), A("own", 0, 20), float(S), ALU.add)
+    cp(A("mw", 0, 10), A("own", 10, 20))
+    cp(A("mw", 10, 20), A("own", 0, 10))
+    ts(A("tabx", 0, S), A("iota", 0, S), 2.0, ALU.add)
+
+    IO = A("iota", 0, C)
+    act(A("sc", 0, C), IO)
+    cp(A("nu", 0, 60), A("nin", 0, 60))
+    cp(A("nf", 0, 60), A("nin", 0, 60))
+    tt(A("isa", 0, C), IND(IO, A("nu", 0, 20)), A("sc", 0, C), ALU.is_gt)
+    act(A("nrep", 0, C), IND(IO, A("nu", 20, 40)), bias=1.0)
+    act(A("nrep", C, 2 * C), IND(IO, A("nu", 40, 60)), bias=1.0)
+    tt(A("t20", 0, 20), A("own", 0, 20), A("nf", 0, 20), ALU.min)
+    tt(A("off", 0, 20), A("own", 0, 20), A("nf", 0, 20), ALU.is_gt)
+    scan(A("inc", 0, C), A("one", 0, C), A("isa", 0, C), 0.0, ALU.mult, ALU.add)
+    cp(A("mnu", 0, 20), A("t20", 0, 20))
+    ts(A("nmask", 0, C), A("jm", 0, C), A("pc", 0, 1), ALU.not_equal)
+    ts(A("e1", 0, C), A("jm", 0, C), A("pc", 1, 2), ALU.is_equal, BIG, ALU.mult)
+    cp(A("yy", 0, C), IND(A("inc", 0, C), A("mnu", 0, 20)))
+    tt(A("mx", 0, C), A("nmask", 0, C), A("e1", 0, C), ALU.max)
+    ts(A("off", 0, 20), A("off", 0, 20), float(S), ALU.mult, -1.0, ALU.add)
+    act(A("mask", 0, C), A("nmask", 0, C), scale=-1.0, bias=1.0)
+    for k in (1, 2):
+        dma("y", T.mx[:, k * C:k * C + C], T.mx[:, 0:C], [A("mx", k * C, k * C + C)], [A("mx", 0, C)])
+    pick(A("ex", 0, C), A("yy", 0, C), C)
+    quant(A("qu", 0, 128), A("su", 0, 128), A("uin", 0, 512))
+    ts(A("keep", 0, C), A("jm", 0, C), 0.0, ALU.not_equal)
+    for nm in ("mask", "keep"):
+        for k in (1, 2):
+            dma("y", T[nm][:, k * C:k * C + C], T[nm][:, 0:C], [A(nm, k * C, k * C + C)], [A(nm, 0, C)])
+    dma("y", T.qw[:].bitcast(dt.uint8), T.wc[:], [A("qw", 0, 512)], [])
+    dma("y", T.sw[:], T.ws[:], [A("sw", 0, 512)], [])
+    dma("y", T.vin[:], T.v[:], [A("vin", 0, 512)], [])
+    ts(A("t20", 0, 20), w16("ex", 0, 20), SCL, ALU.mult)
+    up = A("upk", 0, 8)
+    add("v", lambda: g.vector.tensor_copy(T.qup[:, 0:128].bitcast(dt.uint32), T.qu[:, 0:128].bitcast(dt.uint32).indirect(up[0])),
+        [A("qup", 0, 128)], [A("qu", 0, 128), up])
+    add("s", lambda: g.scalar.activation(T.sup[:, 0:128], T.su[:, 0:128].indirect(up[0]), ACT.Copy),
+        [A("sup", 0, 128)], [A("su", 0, 128), up])
+    tt(A("t20", 0, 20), A("t20", 0, 20), A("off", 0, 20), ALU.add)
+    quant(A("qx", 0, C), A("sx", 0, C), A("xin", 0, 4 * C))
+    cp(A("posu", 0, 20), A("t20", 0, 20))
+    POS = A("posu", 0, 20)
+    scatter(A("pi1", 0, C), POS, A("iota", 1, C + 1))
+    act(A("pos1", 0, C), IND(IO, POS), bias=1.0)
+    act(A("posn", 0, C), IND(A("pos1", 0, C), A("nu", 20, 40)))
+    act(A("posn", C, 2 * C), IND(A("pos1", 0, C), A("nu", 40, 60)))
+    pick(A("exf", 0, C), A("pi1", 0, C), C)
+    ts(A("sl", 0, 20), w16("exf", 0, 20), SCL, ALU.mult, -1.0, ALU.add)
+    ts(A("nw", 0, 20), w16("exf", 0, 20), SCL, ALU.mult, -1.0, ALU.add)
+    PI = A("sl", 0, 20)
+    cp(A("gp", 0, C), IND(A("nrep", 0, C), PI))
+    cp(A("gp", C, 2 * C), IND(A("nrep", C, 2 * C), PI))
+    act(A("sgx", 0, C), IND(A("posn", 0, C), PI))
+    act(A("sgx", C, 2 * C), IND(A("posn", C, 2 * C), PI))
+    cp(A("nw", 20, 30), A("nw", 10, 20))
+    cp(A("nw", 30, 40), A("nw", 0, 10))
+    pick(A("exf", 0, 2 * C), A("gp", 0, 2 * C), 2 * C)
+    ts(A("sl", 20, 60), w16("exf", 0, 40), SCL, ALU.mult, -1.0, ALU.add)
+    ts(A("nw", 40, 80), w16("exf", 0, 40), SCL, ALU.mult, -1.0, ALU.add)
+    pick(A("gp", 0, 2 * C), A("sgx", 0, 2 * C), 2 * C)
+    for k in range(3):
+        tt(A("tau", 20 * k, 20 * k + 20), A("nw", 20 * k + 20, 20 * k + 40), A("nw", 0, 20), ALU.subtract)
+    ts(A("mu", 0, 40), w16("gp", 0, 40), SCL, ALU.mult, -1.0, ALU.add)
+    ts(A("mw", 20, 60), w16("gp", 0, 40), SCL, ALU.mult, -1.0, ALU.add)
+    ts(A("tau", 0, 60), A("tau", 0, 60), TINY, ALU.mult)
+
+    def late_setup():
+        for j, (lo, hi) in enumerate(((1, 2), (1, 3), (2, 3))):
+            tt(A("tauo", 20 * j, 20 * j + 20), A("nw", 20 * hi, 20 * hi + 20), A("nw", 20 * lo, 20 * lo + 20), ALU.subtract)
+        quant(A("qeb", 0, 512), A("seb", 0, 512), A("eb", 0, 2048))
+        ts(A("tauo", 0, 60), A("tauo", 0, 60), TINY, ALU.mult)
+
+    M1, M2 = A("mu", 0, 20), A("mu", 20, 40)
+    QX, SX = A("qx", 0, C), A("sx", 0, C)
+    CW, GW, KW = A("cc", 0, C), A("gg", 0, C), A("kw", 0, 2 * C)
+    parts = [(0, S), (S, C)] if HALVES else [(0, C)]
+
+    def L(name, base, a, b):
+        return A(name, base + a // 16, base + b // 16)
+
+    rid, pid = topo.addr(nxt)[0], topo.addr(nxt)[1]
+    omask = topo.mask(core, nxt)
+    n_out, n_in = len(topo.engines(core, nxt)), len(topo.engines(prv, core))
+
+    for r in range(ROUNDS):
+        last = r == ROUNDS - 1
+        mm(A("ph", 0, C), A("qup", 0, 128), A("sup", 0, 128), QX, SX)
+        if r == 0:
+            act(A("sc", 0, C), A("ph", 0, C))
+        else:
+            cp(A("sc", 0, C), A("ph", 0, C))
+        tt(A("sg", 0, 3 * C), IND(A("sc", 0, C), A("sl", 0, 60)), A("mask", 0, 3 * C), ALU.mult)
+        scan(A("sgx", 0, 3 * C), A("keep", 0, 3 * C), A("sg", 0, 3 * C), 0.0, ALU.mult, ALU.add)
+        tt(A("dd", 0, 10), w16("sgx", 10, 20), w16("sgx", 0, 10), ALU.subtract)
+        tt(A("dd", 10, 20), w16("sgx", 0, 10), w16("sgx", 10, 20), ALU.subtract)
+        tt(A("dd", 20, 40), w16("sgx", 20, 40), w16("sgx", 0, 20), ALU.subtract)
+        tt(A("dd", 40, 60), w16("sgx", 40, 60), w16("sgx", 0, 20), ALU.subtract)
+        tt(A("bb", 0, 60), A("dd", 0, 60), A("tau", 0, 60), ALU.is_lt)
+        tt(A("do", 0, 10), w16("sgx", 20, 30), w16("sgx", 10, 20), ALU.subtract)
+        tt(A("t20", 0, 20), A("bb", 0, 20), A("bb", 20, 40), ALU.mult)
+        tt(A("do", 10, 20), w16("sgx", 30, 40), w16("sgx", 0, 10), ALU.subtract)
+        tt(A("off", 0, 20), A("t20", 0, 20), A("bb", 40, 60), ALU.mult)
+        tt(A("do", 20, 30), w16("sgx", 40, 50), w16("sgx", 10, 20), ALU.subtract)
+        cp(A("cu", 0, 20), A("off", 0, 20))
+        tt(A("do", 30, 40), w16("sgx", 50, 60), w16("sgx", 0, 10), ALU.subtract)
+        cp(CW, IND(IO, A("cu", 0, 20)))
+        if r == 0:
+            late_setup()
+        for b in range(4):
+            mm(A("pd", 512 * b, 512 * b + C), A("qeb", 128 * b, 128 * b + 128), A("seb", 128 * b, 128 * b + 128), QX, SX)
+        small = [
+            lambda: tt(A("do", 40, 60), w16("sgx", 40, 60), w16("sgx", 20, 40), ALU.subtract),
+            lambda: ts(A("l1", 0, 60), A("bb", 0, 60), float(C), ALU.mult),
+            lambda: tt(A("eo", 0, 60), A("do", 0, 60), A("tauo", 0, 60), ALU.is_lt),
+            lambda: tt(A("l2", 0, 60), A("l1", 0, 60), A("mw", 0, 60), ALU.add),
+            lambda: tt(A("ww", 0, 20), A("eo", 0, 20), A("eo", 20, 40), ALU.add),
+            lambda: cp(A("lu", 0, 60), A("l2", 0, 60)),
+            lambda: tt(A("ww", 20, 40), A("eo", 40, 60), A("eo", 0, 20), ALU.subtract),
+            lambda: ts(A("ww", 40, 60), A("ww", 20, 40), 4.0, ALU.mult, 5.0, ALU.add),
+            lambda: tt(A("t20", 0, 20), A("ww", 0, 20), A("ww", 40, 60), ALU.add),
+            lambda: cp(A("cu", 0, 20), A("t20", 0, 20)),
+            lambda: (act(A("r1", 0, C), IND(IO, A("cu", 0, 20))), act(A("r2", 0, C), IND(A("r1", 0, C), POS))),
+            lambda: fill(A("win", 0, S), float(C + 1)),
+            None, None, None, None, None,
+            lambda: pick(A("ex", 0, C), A("r2", 0, C), C),
+            lambda: ts(A("mi", 0, 20), w16("ex", 0, 20), SCL, ALU.mult, -1.0, ALU.add),
+            lambda: ts(A("mj", 0, 20), A("mi", 0, 20), 3, ALU.bitwise_and),
+            lambda: ts(A("mj", 20, 40), A("mi", 0, 20), 12, ALU.bitwise_and),
+            lambda: ts(A("wp", 20, 40), A("mj", 0, 20), 1024.0, ALU.mult, 1024.0, ALU.add),
+            lambda: ts(A("wp", 40, 60), A("mj", 20, 40), 256.0, ALU.mult, 1024.0, ALU.add),
+            lambda: tt(A("t20", 0, 20), A("wp", 20, 40), A("wp", 40, 60), ALU.add),
+            lambda: ts(A("wp", 60, 80), A("t20", 0, 20), -1.0, ALU.mult, 6144.0, ALU.add),
+            lambda: tt(A("wm", 20, 80), A("wp", 20, 80), A("nf", 0, 60), ALU.add),
+            lambda: tt(A("t20", 0, 20), A("wm", 20, 40), A("wm", 40, 60), ALU.max),
+            lambda: tt(A("mi", 0, 20), A("t20", 0, 20), A("wm", 60, 80), ALU.max),
+            lambda: ts(A("mj", 0, 20), A("mi", 0, 20), 1023, ALU.bitwise_and),
+            lambda: cp(A("topu", 0, 20), A("mj", 0, 20)),
+        ]
+        bg = []
+        for b in range(4):
+            bg.append((lambda b: lambda: act(A("fn", FW * b, FW * b + C), A("pd", 512 * b, 512 * b + C), scale=0.5))(b))
+        for b in range(4):
+            bg.append((lambda b: lambda: act(A("f2", FW * b, FW * b + C), IND(A("fn", FW * b, FW * b + C), A("topu", 0, 20))))(b))
+
+        def ride(n=1):
+            for _ in range(n):
+                if small:
+                    step = small.pop(0)
+                    if step is not None:
+                        step()
+
+        def back(n=1):
+            for _ in range(n):
+                if bg and (len(bg) > 4 or not small):
+                    bg.pop(0)()
+
+        for sw in range(1, SWEEPS):
+            if HOP2_S:
+                act(A("n2g", 0, C), IND(CW, M2))
+            back()
+            tt(A("sp", 0, S), A("cc", S, C), A("cc", 0, S), ALU.subtract)
+            ride()
+            tt(A("u1", 0, S), IND(CW, A("mu", 0, 10)), A("sp", 0, S), ALU.add)
+            tt(A("u1", S, C), IND(CW, A("mu", 10, 20)), A("sp", 0, S), ALU.subtract)
+            ride()
+            for a, b in parts:
+                if HOP2_S:
+                    tt(A("uu", a, b), A("u1", a, b), A("n2g", a, b), ALU.add)
+                else:
+                    tt(A("uu", a, b), IND(CW, L("mu", 20, a, b)), A("u1", a, b), ALU.add)
+            ride()
+            for a, b in parts:
+                ts(A("gg", a, b), A("uu", a, b), 1.0, ALU.min, 1.0, ALU.add)
+            ts(A("g2", 0, C), A("uu", 0, C), 1.0, ALU.min, 1.0, ALU.add)
+            ride()
+            if HOP3_S:
+                act(A("n2g", 0, C), IND(GW, M2))
+            tt(A("k1", 0, S), IND(GW, A("mu", 0, 10)), A("g2", S, C), ALU.mult)
+            tt(A("k1", S, C), IND(GW, A("mu", 10, 20)), A("g2", 0, S), ALU.mult)
+            ride()
+            for a, b in parts:
+                if HOP3_S:
+                    tt(A("kw", a, b), A("k1", a, b), A("n2g", a, b), ALU.mult)
+                else:
+                    tt(A("kw", a, b), IND(GW, L("mu", 20, a, b)), A("k1", a, b), ALU.mult)
+            ride()
+            for a, b in parts:
+                ts(A("kw", C + a, C + b), A("kw", a, b), 0.5, ALU.mult)
+            ts(A("lo2", 0, C), A("kw", 0, C), 0.5, ALU.mult)
+            ride()
+            if HOP1_S:
+                act(A("a3", 0, C), IND(KW, A("lu", 40, 60)), scale=-1.0, bias=1.25)
+            back()
+            for a, b in parts:
+                tt(A("a1", a, b), IND(KW, L("lu", 0, a, b)), A("lo2", a, b), ALU.subtract)
+            ride()
+            for a, b in parts:
+                tt(A("a2", a, b), IND(KW, L("lu", 20, a, b)), A("a1", a, b), ALU.add)
+            ride()
+            if HOP1_S:
+                for a, b in parts:
+                    tt(A("cc", a, b), A("a2", a, b), A("a3", a, b), ALU.is_lt)
+            else:
+                for a, b in parts:
+                    tt(A("a3", a, b), IND(KW, L("lu", 40, a, b)), A("a2", a, b), ALU.add)
+                for a, b in parts:
+                    ts(A("cc", a, b), A("a3", a, b), 1.25, ALU.is_lt)
+            ride()
+        ride(99)
+        back(99)
+
+        ts(A("ci", 0, C), IND(CW, POS), 1.0, ALU.add)
+        scan(A("ci", C, 2 * C), A("mone", 0, C), A("ci", 0, C), 1.0, ALU.add, ALU.add)
+        pick(A("ex", 0, 2 * C), A("ci", 0, 2 * C), 2 * C)
+        ts(A("t40", 0, 20), w16("ex", 0, 20), A("pc", 3, 4), ALU.mult, 2.0 * BIG - 2.0, ALU.add)
+        ts(A("t40", 20, 40), w16("ex", 20, 40), SCL, ALU.mult)
+        tt(A("t20", 0, 20), A("t40", 0, 20), A("t40", 20, 40), ALU.add)
+        tt(A("off", 0, 20), A("t20", 0, 20), A("k2", 0, 20), ALU.min)
+        cp(A("destu", 0, 20), A("off", 0, 20))
+        ts(A("t41", 0, 20), A("t20", 0, 20), float(S), ALU.is_lt)
+        scatter(A("win", 0, 3 * S), A("destu", 0, 20), A("iota", 1, C + 1))
+        act(A("x1", 0, C), IND(A("tabx", 0, 3 * S), A("destu", 0, 20)))
+        act(A("x1g", 0, C), IND(A("x1", 0, C), A("nu", 0, 20)))
+        act(A("x1g", C, 2 * C), IND(A("x1", 0, C), A("nu", 20, 40)))
+        ts(A("t41", 20, 40), A("t20", 0, 20), 1.0, ALU.add)
+        pick(A("exf", 0, S), A("win", 0, S), S)
+        tt(A("xn", 0, 20), A("t41", 0, 20), A("t41", 20, 40), ALU.mult)
+        ts(A("cposu", 0, 10), w16("exf", 0, 10), SCL, ALU.mult, -1.0, ALU.add)
+        CP = A("cposu", 0, 10)
+        ts(A("t20", 0, 20), A("t41", 0, 20), 8192.0, ALU.mult)
+        for b in range(4):
+            act(A("e2", S * b, S * b + S), IND(A("f2", FW * b, FW * b + C + 1), CP))
+            if b == 0:
+                tt(A("tf", 0, 20), A("t20", 0, 20), A("own", 0, 20), ALU.add)
+            tt(A("et", b, 4 * S, 4), IND(A("fn", FW * b, FW * b + C + 1), CP), A("e2", S * b, S * b + S), ALU.add)
+        qe, se, lq, ls = "qe%d" % r, "se%d" % r, "lq%d" % r, "ls%d" % r
+        quant(A(qe, 0, S), A(se, 0, S), A("et", 0, 4 * S))
+        arr = T.sem["arr%d" % r]
+        add("g", (lambda qe, lq, arr: lambda: g.remote_dma(T[lq][:, 0:S].bitcast(dt.uint8), T[qe][:, 0:S].bitcast(dt.uint8), arr, T.sem.sent, pid, rid, omask))(qe, lq, arr),
+            [], [A(qe, 0, S)], sem="remote")
+        add("g", (lambda se, ls, arr: lambda: g.remote_dma(T[ls][:, 0:S], T[se][:, 0:S], arr, T.sem.sent, pid, rid, omask))(se, ls, arr),
+            [], [A(se, 0, S)], sem="remote")
+        add("far", None, [A(lq, 0, S), A(ls, 0, S)], [], sem="arr%d" % r, n=2 * n_in)
+
+        act(A("x1g", 2 * C, 3 * C), IND(A("x1", 0, C), A("nu", 40, 60)))
+        pick(A("ex", 0, 3 * C), A("x1g", 0, 3 * C), 3 * C)
+        ts(A("xn", 20, 80), w16("ex", 0, 60), SCL, ALU.mult, -1.0, ALU.add)
+        ts(A("cz", 0, 80), A("xn", 0, 80), 0.0, ALU.is_gt)
+        tt(A("tp", 0, 80), A("xn", 0, 80), A("wp", 0, 80), ALU.add)
+        ts(A("l2", 0, 60), A("xn", 20, 80), 0.0, ALU.is_le)
+        tt(A("tp", 0, 80), A("tp", 0, 80), A("cz", 0, 80), ALU.mult)
+        tt(A("tf", 20, 80), A("wm", 20, 80), A("l2", 0, 60), ALU.mult)
+        tt(A("t40", 0, 40), A("tp", 0, 40), A("tp", 40, 80), ALU.max)
+        tt(A("t41", 0, 40), A("tf", 0, 40), A("tf", 40, 80), ALU.max)
+        tt(A("mi", 0, 20), A("t40", 0, 20), A("t40", 20, 40), ALU.max)
+        tt(A("mi", 20, 40), A("t41", 0, 20), A("t41", 20, 40), ALU.max)
+        ts(A("mj", 0, 40), A("mi", 0, 40), 1023, ALU.bitwise_and)
+        cp(A("s12u", 0, 40), A("mj", 0, 40))
+        S1, FQ, S2 = A("s12u", 0, 20), A("s12u", 20, 40), A("mnu", 0, 20)
+        ts(A("r1", 0, C), IND(IO, S1), 1.0, ALU.add)
+        cp(A("r2", 0, C), IND(A("r1", 0, C), FQ))
+        pick(A("ex", 0, C), A("r2", 0, C), C)
+        ts(S2, w16("ex", 0, 20), SCL, ALU.mult, -1.0, ALU.add)
+
+        for b in range(4):
+            mm(A("ph", 512 * b, 512 * b + S), A("qw", 128 * b, 128 * b + 128), A("sw", 128 * b, 128 * b + 128), A(lq, 0, S), A(ls, 0, S))
+        act(A("hh", 1, S + 1), A("ph", 0, S), scale=2.0 ** -6)
+        for b in range(1, 4):
+            ts(A("hh", HW * b + 1, HW * b + S + 1), A("ph", 512 * b, 512 * b + S), 2.0 ** -6, ALU.mult)
+        for b in range(4):
+            act(A("t2", C * b, C * b + C), IND(A("hh", HW * b, HW * b + S + 1), S1))
+        for b in range(5):
+            if b < 4:
+                tt(A("tt", C * b, C * b + C), IND(A("hh", HW * b, HW * b + S + 1), S2), A("t2", C * b, C * b + C), ALU.add)
+            if b > 0:
+                a = b - 1
+                tt(A("xa", a, 4 * C, 4), A("pd", 512 * a, 512 * a + C), A("tt", C * a, C * a + C), ALU.add)
+            if last and b == 0:
+                quant(A("qv", 0, 128), A("sv", 0, 128), A("vin", 0, 512))
+        if last:
+            act(A("tabp", 1, S + 1), IND(A("iota", 0, C + 1), CP))
+            act(A("prep", 0, C), IND(A("tabp", 0, S + 1), S1))
+            dma("s", T.op[:], T.prep[0:128:16, 0:C], [], [A("prep", 0, C)])
+        quant(QX, SX, A("xa", 0, 4 * C))
+
+    dma("y", T.oc[:], T.qx[:, 0:C].bitcast(dt.uint8), [], [QX])
+    mm(A("ph", 0, S), A("qv", 0, 128), A("sv", 0, 128), A("qx", 0, S), A("sx", 0, S))
+    mm(A("ph", 512, 512 + S), A("qv", 0, 128), A("sv", 0, 128), A("qx", S, C), A("sx", S, C))
+    for k in range(4):
+        dma("y" if k % 2 else "s", T.osc[4 * k:4 * k + 4, :], T.sx[32 * k:32 * k + 4, 0:C], [], [SX])
+    cp(A("yo", 0, S), A("ph", 0, S))
+    act(A("yo", S, C), A("ph", 512, 512 + S))
+    dma("y", T.y[:, 0:S], T.yo[:, 0:S], [], [A("yo", 0, S)])
+    dma("s", T.y[:, S:C], T.yo[:, S:C], [], [A("yo", S, C)])
+
+    seen = {}
+    for i, o in enumerate(ops):
+        deps = set()
+        for kind, keys in (("r", o["r"]), ("w", o["w"])):
+            for (nm, a, b) in keys:
+                ps = SCRATCH[nm][0] == "psum"
+                for (j, kj, aj, bj) in seen.get(nm, []):
+                    if j == i or aj >= b or a >= bj:
+                        continue
+                    e = ops[j]
+                    if e["q"] == o["q"] and e["sem"] is None and o["sem"] is None:
+                        need = kj == "w" and kind == "r"
+                    else:
+                        need = kj == "w" or kind == "w" or ps
+                    if need and e["sem"] != "remote":
+                        deps.add(j)
+        for kind, keys in (("r", o["r"]), ("w", o["w"])):
+            for (nm, a, b) in keys:
+                seen.setdefault(nm, []).append((i, kind, a, b))
+        best = {}
+        for j in deps:
+            k = ops[j]["sem"] or ops[j]["q"]
+            best[k] = max(best.get(k, -1), j)
+        o["deps"] = sorted(best.values())
+    waited = {}
+    for o in ops:
+        keep = []
+        for j in o["deps"]:
+            k = (o["q"], ops[j]["sem"] or ops[j]["q"])
+            if waited.get(k, -1) < j:
+                waited[k] = j
+                keep.append(j)
+                ops[j]["used"] = True
+        o["deps"] = keep
+    qsem = {"v": "cv", "s": "cs", "t": "ct", "g": "cg"}
+    eng = {"v": g.vector, "s": g.scalar, "t": g.tensor, "g": g, "y": g.sync}
+    count = {}
+    for o in ops:
+        if o["sem"] is None:
+            o["sn"] = qsem[o["q"]]
+            if o["used"]:
+                count[o["sn"]] = count.get(o["sn"], 0) + 1
+            o["at"] = count.get(o["sn"], 0)
+        else:
+            o["sn"], o["at"] = o["sem"], o["n"]
+    for o in ops:
+        if o["fn"] is None:
+            continue
+        for j in o["deps"]:
+            eng[o["q"]].wait_ge(T.sem[ops[j]["sn"]], ops[j]["at"])
+        ins = o["fn"]()
+        if o["sem"] is None:
+            if o["used"]:
+                ins.then_inc(T.sem[o["sn"]], 1)
+        elif o["sem"] != "remote":
+            ins.then_inc(T.sem[o["sem"]], 16)
+    g.wait_ge(T.sem.sent, 2 * ROUNDS * n_out)
+    for o in ops:
+        if o["fn"] is not None and o["sem"] not in (None, "remote") and not o["used"]:
+            g.wait_ge(T.sem[o["sem"]], 16)

@@ -7,7 +7,7 @@ FW, HW = 336, 176
 BIG = 512.0
 TINY = 2.0 ** -110
 HOP1_S, HOP2_S, HOP3_S = True, False, False
-HALVES = False
+HALVES = True
 
 F32, B16, I32, U16, Q8, U8 = "float32", "bfloat16", "int32", "uint16", "float8_e4m3fn_x4", "uint8"
 SCRATCH = {}
@@ -248,6 +248,7 @@ def rank_program(g, core, T, topo):
     QX, SX = A("qx", 0, C), A("sx", 0, C)
     CW, GW, KW = A("cc", 0, C), A("gg", 0, C), A("kw", 0, 2 * C)
     parts = [(0, S), (S, C)] if HALVES else [(0, C)]
+    strap = parts[::-1]
 
     def L(name, base, a, b):
         return A(name, base + a // 16, base + b // 16)
@@ -263,45 +264,48 @@ def rank_program(g, core, T, topo):
             act(A("sc", 0, C), A("ph", 0, C))
         else:
             cp(A("sc", 0, C), A("ph", 0, C))
-        tt(A("sg", 0, 3 * C), IND(A("sc", 0, C), A("sl", 0, 60)), A("mask", 0, 3 * C), ALU.mult)
-        scan(A("sgx", 0, 3 * C), A("keep", 0, 3 * C), A("sg", 0, 3 * C), 0.0, ALU.mult, ALU.add)
+        tt(A("sg", 0, 2 * C), IND(A("sc", 0, C), A("sl", 0, 40)), A("mask", 0, 2 * C), ALU.mult)
+        tt(A("sg", 2 * C, 3 * C), IND(A("sc", 0, C), A("sl", 40, 60)), A("mask", 0, C), ALU.mult)
+        scan(A("sgx", 0, 2 * C), A("keep", 0, 2 * C), A("sg", 0, 2 * C), 0.0, ALU.mult, ALU.add)
+        scan(A("sgx", 2 * C, 3 * C), A("keep", 0, C), A("sg", 2 * C, 3 * C), 0.0, ALU.mult, ALU.add)
         tt(A("dd", 0, 10), w16("sgx", 10, 20), w16("sgx", 0, 10), ALU.subtract)
         tt(A("dd", 10, 20), w16("sgx", 0, 10), w16("sgx", 10, 20), ALU.subtract)
         tt(A("dd", 20, 40), w16("sgx", 20, 40), w16("sgx", 0, 20), ALU.subtract)
         tt(A("dd", 40, 60), w16("sgx", 40, 60), w16("sgx", 0, 20), ALU.subtract)
-        tt(A("bb", 0, 60), A("dd", 0, 60), A("tau", 0, 60), ALU.is_lt)
+        tt(A("bb", 0, 40), A("dd", 0, 40), A("tau", 0, 40), ALU.is_lt)
         tt(A("do", 0, 10), w16("sgx", 20, 30), w16("sgx", 10, 20), ALU.subtract)
+        tt(A("bb", 40, 60), A("dd", 40, 60), A("tau", 40, 60), ALU.is_lt)
         tt(A("t20", 0, 20), A("bb", 0, 20), A("bb", 20, 40), ALU.mult)
         tt(A("do", 10, 20), w16("sgx", 30, 40), w16("sgx", 0, 10), ALU.subtract)
-        tt(A("off", 0, 20), A("t20", 0, 20), A("bb", 40, 60), ALU.mult)
         tt(A("do", 20, 30), w16("sgx", 40, 50), w16("sgx", 10, 20), ALU.subtract)
-        cp(A("cu", 0, 20), A("off", 0, 20))
+        tt(A("off", 0, 20), A("t20", 0, 20), A("bb", 40, 60), ALU.mult)
         tt(A("do", 30, 40), w16("sgx", 50, 60), w16("sgx", 0, 10), ALU.subtract)
+        cp(A("cu", 0, 20), A("off", 0, 20))
         cp(CW, IND(IO, A("cu", 0, 20)))
         if r == 0:
             late_setup()
         for b in range(4):
             mm(A("pd", 512 * b, 512 * b + C), A("qeb", 128 * b, 128 * b + 128), A("seb", 128 * b, 128 * b + 128), QX, SX)
         small = [
-            lambda: tt(A("do", 40, 60), w16("sgx", 40, 60), w16("sgx", 20, 40), ALU.subtract),
-            lambda: ts(A("l1", 0, 60), A("bb", 0, 60), float(C), ALU.mult),
-            lambda: tt(A("eo", 0, 60), A("do", 0, 60), A("tauo", 0, 60), ALU.is_lt),
+            lambda: (ts(A("l1", 0, 60), A("bb", 0, 60), float(C), ALU.mult),
+                     tt(A("do", 40, 60), w16("sgx", 40, 60), w16("sgx", 20, 40), ALU.subtract)),
             lambda: tt(A("l2", 0, 60), A("l1", 0, 60), A("mw", 0, 60), ALU.add),
-            lambda: tt(A("ww", 0, 20), A("eo", 0, 20), A("eo", 20, 40), ALU.add),
             lambda: cp(A("lu", 0, 60), A("l2", 0, 60)),
-            lambda: tt(A("ww", 20, 40), A("eo", 40, 60), A("eo", 0, 20), ALU.subtract),
+            lambda: tt(A("eo", 0, 60), A("do", 0, 60), A("tauo", 0, 60), ALU.is_lt),
+            lambda: (tt(A("ww", 20, 40), A("eo", 40, 60), A("eo", 0, 20), ALU.subtract),
+                     tt(A("ww", 0, 20), A("eo", 0, 20), A("eo", 20, 40), ALU.add)),
             lambda: ts(A("ww", 40, 60), A("ww", 20, 40), 4.0, ALU.mult, 5.0, ALU.add),
             lambda: tt(A("t20", 0, 20), A("ww", 0, 20), A("ww", 40, 60), ALU.add),
             lambda: cp(A("cu", 0, 20), A("t20", 0, 20)),
-            lambda: (act(A("r1", 0, C), IND(IO, A("cu", 0, 20))), act(A("r2", 0, C), IND(A("r1", 0, C), POS))),
-            lambda: fill(A("win", 0, S), float(C + 1)),
-            None, None, None, None, None,
+            lambda: (act(A("r1", 0, C), IND(IO, A("cu", 0, 20))), act(A("r2", 0, C), IND(A("r1", 0, C), POS)),
+                     fill(A("win", 0, S), float(C + 1))),
+            None,
             lambda: pick(A("ex", 0, C), A("r2", 0, C), C),
             lambda: ts(A("mi", 0, 20), w16("ex", 0, 20), SCL, ALU.mult, -1.0, ALU.add),
-            lambda: ts(A("mj", 0, 20), A("mi", 0, 20), 3, ALU.bitwise_and),
-            lambda: ts(A("mj", 20, 40), A("mi", 0, 20), 12, ALU.bitwise_and),
-            lambda: ts(A("wp", 20, 40), A("mj", 0, 20), 1024.0, ALU.mult, 1024.0, ALU.add),
-            lambda: ts(A("wp", 40, 60), A("mj", 20, 40), 256.0, ALU.mult, 1024.0, ALU.add),
+            lambda: (ts(A("mj", 0, 20), A("mi", 0, 20), 3, ALU.bitwise_and),
+                     ts(A("mj", 20, 40), A("mi", 0, 20), 12, ALU.bitwise_and)),
+            lambda: (ts(A("wp", 20, 40), A("mj", 0, 20), 1024.0, ALU.mult, 1024.0, ALU.add),
+                     ts(A("wp", 40, 60), A("mj", 20, 40), 256.0, ALU.mult, 1024.0, ALU.add)),
             lambda: tt(A("t20", 0, 20), A("wp", 20, 40), A("wp", 40, 60), ALU.add),
             lambda: ts(A("wp", 60, 80), A("t20", 0, 20), -1.0, ALU.mult, 6144.0, ALU.add),
             lambda: tt(A("wm", 20, 80), A("wp", 20, 80), A("nf", 0, 60), ALU.add),
@@ -332,6 +336,7 @@ def rank_program(g, core, T, topo):
             if HOP2_S:
                 act(A("n2g", 0, C), IND(CW, M2))
             back()
+            ride()
             tt(A("sp", 0, S), A("cc", S, C), A("cc", 0, S), ALU.subtract)
             ride()
             tt(A("u1", 0, S), IND(CW, A("mu", 0, 10)), A("sp", 0, S), ALU.add)
@@ -342,44 +347,38 @@ def rank_program(g, core, T, topo):
                     tt(A("uu", a, b), A("u1", a, b), A("n2g", a, b), ALU.add)
                 else:
                     tt(A("uu", a, b), IND(CW, L("mu", 20, a, b)), A("u1", a, b), ALU.add)
-            ride()
             for a, b in parts:
                 ts(A("gg", a, b), A("uu", a, b), 1.0, ALU.min, 1.0, ALU.add)
-            ts(A("g2", 0, C), A("uu", 0, C), 1.0, ALU.min, 1.0, ALU.add)
+                ts(A("g2", a, b), A("uu", a, b), 1.0, ALU.min, 1.0, ALU.add)
             ride()
             if HOP3_S:
                 act(A("n2g", 0, C), IND(GW, M2))
-            tt(A("k1", 0, S), IND(GW, A("mu", 0, 10)), A("g2", S, C), ALU.mult)
             tt(A("k1", S, C), IND(GW, A("mu", 10, 20)), A("g2", 0, S), ALU.mult)
-            ride()
-            for a, b in parts:
+            tt(A("k1", 0, S), IND(GW, A("mu", 0, 10)), A("g2", S, C), ALU.mult)
+            for a, b in strap:
                 if HOP3_S:
                     tt(A("kw", a, b), A("k1", a, b), A("n2g", a, b), ALU.mult)
                 else:
                     tt(A("kw", a, b), IND(GW, L("mu", 20, a, b)), A("k1", a, b), ALU.mult)
-            ride()
-            for a, b in parts:
+            for a, b in strap:
                 ts(A("kw", C + a, C + b), A("kw", a, b), 0.5, ALU.mult)
-            ts(A("lo2", 0, C), A("kw", 0, C), 0.5, ALU.mult)
+                ts(A("lo2", a, b), A("kw", a, b), 0.5, ALU.mult)
             ride()
             if HOP1_S:
                 act(A("a3", 0, C), IND(KW, A("lu", 40, 60)), scale=-1.0, bias=1.25)
             back()
-            for a, b in parts:
+            for a, b in strap:
                 tt(A("a1", a, b), IND(KW, L("lu", 0, a, b)), A("lo2", a, b), ALU.subtract)
-            ride()
-            for a, b in parts:
+            for a, b in strap:
                 tt(A("a2", a, b), IND(KW, L("lu", 20, a, b)), A("a1", a, b), ALU.add)
-            ride()
             if HOP1_S:
-                for a, b in parts:
+                for a, b in strap:
                     tt(A("cc", a, b), A("a2", a, b), A("a3", a, b), ALU.is_lt)
             else:
                 for a, b in parts:
                     tt(A("a3", a, b), IND(KW, L("lu", 40, a, b)), A("a2", a, b), ALU.add)
                 for a, b in parts:
                     ts(A("cc", a, b), A("a3", a, b), 1.25, ALU.is_lt)
-            ride()
         ride(99)
         back(99)
 
@@ -397,17 +396,19 @@ def rank_program(g, core, T, topo):
         act(A("x1g", 0, C), IND(A("x1", 0, C), A("nu", 0, 20)))
         act(A("x1g", C, 2 * C), IND(A("x1", 0, C), A("nu", 20, 40)))
         ts(A("t41", 20, 40), A("t20", 0, 20), 1.0, ALU.add)
+        ts(A("t41", 40, 60), A("t41", 0, 20), 8192.0, ALU.mult)
         pick(A("exf", 0, S), A("win", 0, S), S)
         tt(A("xn", 0, 20), A("t41", 0, 20), A("t41", 20, 40), ALU.mult)
+        tt(A("tf", 0, 20), A("t41", 40, 60), A("own", 0, 20), ALU.add)
         ts(A("cposu", 0, 10), w16("exf", 0, 10), SCL, ALU.mult, -1.0, ALU.add)
         CP = A("cposu", 0, 10)
-        ts(A("t20", 0, 20), A("t41", 0, 20), 8192.0, ALU.mult)
+        pick(A("ex", 0, 2 * C), A("x1g", 0, 2 * C), 2 * C)
         for b in range(4):
             act(A("e2", S * b, S * b + S), IND(A("f2", FW * b, FW * b + C + 1), CP))
-            if b == 0:
-                tt(A("tf", 0, 20), A("t20", 0, 20), A("own", 0, 20), ALU.add)
             tt(A("et", b, 4 * S, 4), IND(A("fn", FW * b, FW * b + C + 1), CP), A("e2", S * b, S * b + S), ALU.add)
         qe, se, lq, ls = "qe%d" % r, "se%d" % r, "lq%d" % r, "ls%d" % r
+        act(A("x1g", 2 * C, 3 * C), IND(A("x1", 0, C), A("nu", 40, 60)))
+        ts(A("xn", 20, 60), w16("ex", 0, 40), SCL, ALU.mult, -1.0, ALU.add)
         quant(A(qe, 0, S), A(se, 0, S), A("et", 0, 4 * S))
         arr = T.sem["arr%d" % r]
         add("g", (lambda qe, lq, arr: lambda: g.remote_dma(T[lq][:, 0:S].bitcast(dt.uint8), T[qe][:, 0:S].bitcast(dt.uint8), arr, T.sem.sent, pid, rid, omask))(qe, lq, arr),
@@ -416,32 +417,43 @@ def rank_program(g, core, T, topo):
             [], [A(se, 0, S)], sem="remote")
         add("far", None, [A(lq, 0, S), A(ls, 0, S)], [], sem="arr%d" % r, n=2 * n_in)
 
-        act(A("x1g", 2 * C, 3 * C), IND(A("x1", 0, C), A("nu", 40, 60)))
-        pick(A("ex", 0, 3 * C), A("x1g", 0, 3 * C), 3 * C)
-        ts(A("xn", 20, 80), w16("ex", 0, 60), SCL, ALU.mult, -1.0, ALU.add)
-        ts(A("cz", 0, 80), A("xn", 0, 80), 0.0, ALU.is_gt)
-        tt(A("tp", 0, 80), A("xn", 0, 80), A("wp", 0, 80), ALU.add)
-        ts(A("l2", 0, 60), A("xn", 20, 80), 0.0, ALU.is_le)
-        tt(A("tp", 0, 80), A("tp", 0, 80), A("cz", 0, 80), ALU.mult)
-        tt(A("tf", 20, 80), A("wm", 20, 80), A("l2", 0, 60), ALU.mult)
-        tt(A("t40", 0, 40), A("tp", 0, 40), A("tp", 40, 80), ALU.max)
-        tt(A("t41", 0, 40), A("tf", 0, 40), A("tf", 40, 80), ALU.max)
-        tt(A("mi", 0, 20), A("t40", 0, 20), A("t40", 20, 40), ALU.max)
-        tt(A("mi", 20, 40), A("t41", 0, 20), A("t41", 20, 40), ALU.max)
-        ts(A("mj", 0, 40), A("mi", 0, 40), 1023, ALU.bitwise_and)
-        cp(A("s12u", 0, 40), A("mj", 0, 40))
         S1, FQ, S2 = A("s12u", 0, 20), A("s12u", 20, 40), A("mnu", 0, 20)
-        ts(A("r1", 0, C), IND(IO, S1), 1.0, ALU.add)
-        cp(A("r2", 0, C), IND(A("r1", 0, C), FQ))
-        pick(A("ex", 0, C), A("r2", 0, C), C)
-        ts(S2, w16("ex", 0, 20), SCL, ALU.mult, -1.0, ALU.add)
+        pick(A("ex", 2 * C, 3 * C), A("x1g", 2 * C, 3 * C), C)
+        ts(A("cz", 0, 60), A("xn", 0, 60), 0.0, ALU.is_gt)
+        tt(A("tp", 0, 60), A("xn", 0, 60), A("wp", 0, 60), ALU.add)
+        ts(A("xn", 60, 80), w16("ex", 40, 60), SCL, ALU.mult, -1.0, ALU.add)
+        ts(A("l2", 0, 40), A("xn", 20, 60), 0.0, ALU.is_le)
+        tt(A("tp", 0, 60), A("tp", 0, 60), A("cz", 0, 60), ALU.mult)
+        ts(A("l2", 40, 60), A("xn", 60, 80), 0.0, ALU.is_le)
+        ts(A("cz", 60, 80), A("xn", 60, 80), 0.0, ALU.is_gt)
+        tt(A("tp", 60, 80), A("xn", 60, 80), A("wp", 60, 80), ALU.add)
+        tt(A("tf", 20, 80), A("wm", 20, 80), A("l2", 0, 60), ALU.mult)
+        tt(A("tp", 60, 80), A("tp", 60, 80), A("cz", 60, 80), ALU.mult)
+        tt(A("t41", 0, 40), A("tf", 0, 40), A("tf", 40, 80), ALU.max)
+        tt(A("t40", 0, 40), A("tp", 0, 40), A("tp", 40, 80), ALU.max)
+        tt(A("mi", 20, 40), A("t41", 0, 20), A("t41", 20, 40), ALU.max)
+        tt(A("mi", 0, 20), A("t40", 0, 20), A("t40", 20, 40), ALU.max)
+        ts(A("mj", 20, 40), A("mi", 20, 40), 1023, ALU.bitwise_and)
+        ts(A("mj", 0, 20), A("mi", 0, 20), 1023, ALU.bitwise_and)
+        cp(FQ, A("mj", 20, 40))
+        cp(S1, A("mj", 0, 20))
+        for a, b in parts:
+            ts(A("r1", a, b), IND(IO, L("s12u", 0, a, b)), 1.0, ALU.add)
+        for a, b in parts:
+            cp(A("r2", a, b), IND(A("r1", 0, C), L("s12u", 20, a, b)))
+        for a, b in parts:
+            pick(A("ex", a, b), A("r2", a, b), b - a)
+        for a, b in parts:
+            ts(A("mnu", a // 16, b // 16), w16("ex", a // 16, b // 16), SCL, ALU.mult, -1.0, ALU.add)
 
         for b in range(4):
             mm(A("ph", 512 * b, 512 * b + S), A("qw", 128 * b, 128 * b + 128), A("sw", 128 * b, 128 * b + 128), A(lq, 0, S), A(ls, 0, S))
         act(A("hh", 1, S + 1), A("ph", 0, S), scale=2.0 ** -6)
-        for b in range(1, 4):
+        for b in range(1, 3):
             ts(A("hh", HW * b + 1, HW * b + S + 1), A("ph", 512 * b, 512 * b + S), 2.0 ** -6, ALU.mult)
         for b in range(4):
+            if b == 2:
+                act(A("hh", HW * 3 + 1, HW * 3 + S + 1), A("ph", 512 * 3, 512 * 3 + S), scale=2.0 ** -6)
             act(A("t2", C * b, C * b + C), IND(A("hh", HW * b, HW * b + S + 1), S1))
         for b in range(5):
             if b < 4:
@@ -478,7 +490,7 @@ def rank_program(g, core, T, topo):
                         continue
                     e = ops[j]
                     if e["q"] == o["q"] and e["sem"] is None and o["sem"] is None:
-                        need = kj == "w" and kind == "r"
+                        need = (kj == "w" or kind == "w") and not (kj == kind and nm in ("et", "xa"))
                     else:
                         need = kj == "w" or kind == "w" or ps
                     if need and e["sem"] != "remote":

@@ -6,7 +6,7 @@ C, S, ROUNDS, SWEEPS = 320, 160, 3, 8
 FW, HW = 336, 176
 BIG = 512.0
 TINY = 2.0 ** -110
-HOP1_S, HOP2_S, HOP3_S = True, False, False
+HOP1_S, HOP2_S, HOP3_S = True, True, False
 HALVES = True
 
 F32, B16, I32, U16, Q8, U8 = "float32", "bfloat16", "int32", "uint16", "float8_e4m3fn_x4", "uint8"
@@ -43,7 +43,9 @@ _sb("iota pi1 pos1", FW, F32)
 _sb("nrep posn gp exf", 2 * C, F32)
 _sb("sc prep yo", C, F32)
 _sb("sg sgx", 3 * C, F32)
-_sb("win", 3 * S, F32)
+WW = 656
+_sb("win", WW, F32)
+_sb("k3", 32, F32)
 _sb("tabp", HW, F32)
 _sb("pc", 8, F32)
 _sb("i16 own k2 off t20", 32, F32)
@@ -52,7 +54,7 @@ _sb("nf mw tau tauo dd bb do eo ww l1 l2 t40 t41", 64, F32)
 _sb("kw ci", 2 * C, B16)
 _sb("cc gg g2 lo2 a1 a2 a3 n2g u1 uu k1 x1 r1 r2", C, B16)
 _sb("sp", S, B16)
-_sb("tabx", 3 * S, B16)
+_sb("tabx", WW, B16)
 _sb("fn f2", 4 * FW, B16)
 _sb("et e2", 4 * S, B16)
 _sb("hh", 4 * HW, B16)
@@ -166,12 +168,15 @@ def rank_program(g, core, T, topo):
     ts(SCL, A("pc", 0, 1), 15.0, ALU.is_equal, 1.0 / BIG, ALU.max)
     ts(A("own", 0, 20), A("i16", 0, 20), A("pc", 0, 1), ALU.add)
     fill(A("fn", C, 4 * FW, FW), 0.0)
-    ts(A("pc", 3, 4), SCL, -BIG, ALU.mult)
+    ts(A("pc", 3, 4), A("pc", 0, 1), 15.0, ALU.not_equal, BIG, ALU.mult)
     fill(A("f2", C, 4 * FW, FW), 0.0)
     fill(A("hh", 0, 4 * HW, HW), 0.0)
-    fill(A("tabx", S, 3 * S), 1.0)
+    ts(A("k3", 0, 20), A("own", 0, 20), 2.0, ALU.mult, 2.0 * S + 2.0, ALU.add)
+    ts(A("pc", 3, 4), A("pc", 3, 4), 1.0, ALU.max)
+    fill(A("tabx", S, WW), 1.0)
     fill(A("tabp", 0, 1), -1.0)
-    ts(A("k2", 0, 20), A("own", 0, 20), float(S), ALU.add)
+    ts(A("k2", 0, 20), A("own", 0, 20), S + 2.0, ALU.add)
+    ts(A("k3", 0, 20), A("k3", 0, 20), A("pc", 3, 4), ALU.mult)
     cp(A("mw", 0, 10), A("own", 10, 20))
     cp(A("mw", 10, 20), A("own", 0, 10))
     ts(A("tabx", 0, S), A("iota", 0, S), 2.0, ALU.add)
@@ -218,31 +223,45 @@ def rank_program(g, core, T, topo):
     act(A("pos1", 0, C), IND(IO, POS), bias=1.0)
     act(A("posn", 0, C), IND(A("pos1", 0, C), A("nu", 20, 40)))
     act(A("posn", C, 2 * C), IND(A("pos1", 0, C), A("nu", 40, 60)))
+
+    def unit(b):
+        quant(A("qeb", 128 * b, 128 * b + 128), A("seb", 128 * b, 128 * b + 128), A("eb", 512 * b, 512 * b + 512))
+
+    mm(A("ph", 0, C), A("qup", 0, 128), A("sup", 0, 128), A("qx", 0, C), A("sx", 0, C))
+    act(A("sc", 0, C), A("ph", 0, C))
+    unit(0)
     pick(A("exf", 0, C), A("pi1", 0, C), C)
+    unit(1)
     ts(A("sl", 0, 20), w16("exf", 0, 20), SCL, ALU.mult, -1.0, ALU.add)
     ts(A("nw", 0, 20), w16("exf", 0, 20), SCL, ALU.mult, -1.0, ALU.add)
     PI = A("sl", 0, 20)
+    unit(2)
     cp(A("gp", 0, C), IND(A("nrep", 0, C), PI))
-    cp(A("gp", C, 2 * C), IND(A("nrep", C, 2 * C), PI))
-    act(A("sgx", 0, C), IND(A("posn", 0, C), PI))
-    act(A("sgx", C, 2 * C), IND(A("posn", C, 2 * C), PI))
+    act(A("gp", C, 2 * C), IND(A("nrep", C, 2 * C), PI))
+    act(A("nrep", 0, C), IND(A("posn", 0, C), PI))
+    act(A("pos1", 0, C), IND(A("posn", C, 2 * C), PI))
     cp(A("nw", 20, 30), A("nw", 10, 20))
     cp(A("nw", 30, 40), A("nw", 0, 10))
-    pick(A("exf", 0, 2 * C), A("gp", 0, 2 * C), 2 * C)
-    ts(A("sl", 20, 60), w16("exf", 0, 40), SCL, ALU.mult, -1.0, ALU.add)
+    pick(A("exf", 0, C), A("gp", 0, C), C)
+    pick(A("exf", C, 2 * C), A("gp", C, 2 * C), C)
+    ts(A("sl", 20, 40), w16("exf", 0, 20), SCL, ALU.mult, -1.0, ALU.add)
+    unit(3)
+    ts(A("sl", 40, 60), w16("exf", 20, 40), SCL, ALU.mult, -1.0, ALU.add)
     ts(A("nw", 40, 80), w16("exf", 0, 40), SCL, ALU.mult, -1.0, ALU.add)
-    pick(A("gp", 0, 2 * C), A("sgx", 0, 2 * C), 2 * C)
-    for k in range(3):
-        tt(A("tau", 20 * k, 20 * k + 20), A("nw", 20 * k + 20, 20 * k + 40), A("nw", 0, 20), ALU.subtract)
-    ts(A("mu", 0, 40), w16("gp", 0, 40), SCL, ALU.mult, -1.0, ALU.add)
-    ts(A("mw", 20, 60), w16("gp", 0, 40), SCL, ALU.mult, -1.0, ALU.add)
-    ts(A("tau", 0, 60), A("tau", 0, 60), TINY, ALU.mult)
+    quant(A("qv", 0, 128), A("sv", 0, 128), A("vin", 0, 512))
+
+    def mid_setup():
+        for k in range(3):
+            tt(A("tau", 20 * k, 20 * k + 20), A("nw", 20 * k + 20, 20 * k + 40), A("nw", 0, 20), ALU.subtract)
+        pick(A("gp", 0, C), A("nrep", 0, C), C)
+        ts(A("tau", 0, 60), A("tau", 0, 60), TINY, ALU.mult)
+        pick(A("gp", C, 2 * C), A("pos1", 0, C), C)
 
     def late_setup():
+        ts(A("mu", 0, 40), w16("gp", 0, 40), SCL, ALU.mult, -1.0, ALU.add)
+        ts(A("mw", 20, 60), w16("gp", 0, 40), SCL, ALU.mult, -1.0, ALU.add)
         for j, (lo, hi) in enumerate(((1, 2), (1, 3), (2, 3))):
             tt(A("tauo", 20 * j, 20 * j + 20), A("nw", 20 * hi, 20 * hi + 20), A("nw", 20 * lo, 20 * lo + 20), ALU.subtract)
-        quant(A("qeb", 0, 512), A("seb", 0, 512), A("eb", 0, 2048))
-        ts(A("tauo", 0, 60), A("tauo", 0, 60), TINY, ALU.mult)
 
     M1, M2 = A("mu", 0, 20), A("mu", 20, 40)
     QX, SX = A("qx", 0, C), A("sx", 0, C)
@@ -259,15 +278,17 @@ def rank_program(g, core, T, topo):
 
     for r in range(ROUNDS):
         last = r == ROUNDS - 1
-        mm(A("ph", 0, C), A("qup", 0, 128), A("sup", 0, 128), QX, SX)
-        if r == 0:
-            act(A("sc", 0, C), A("ph", 0, C))
-        else:
-            cp(A("sc", 0, C), A("ph", 0, C))
+        if r > 0:
+            mm(A("ph", 0, S), A("qup", 0, 128), A("sup", 0, 128), A("qx", 0, S), A("sx", 0, S))
+            mm(A("ph", 512, 512 + S), A("qup", 0, 128), A("sup", 0, 128), A("qx", S, C), A("sx", S, C))
+            cp(A("sc", 0, S), A("ph", 0, S))
+            cp(A("sc", S, C), A("ph", 512, 512 + S))
         tt(A("sg", 0, 2 * C), IND(A("sc", 0, C), A("sl", 0, 40)), A("mask", 0, 2 * C), ALU.mult)
         tt(A("sg", 2 * C, 3 * C), IND(A("sc", 0, C), A("sl", 40, 60)), A("mask", 0, C), ALU.mult)
         scan(A("sgx", 0, 2 * C), A("keep", 0, 2 * C), A("sg", 0, 2 * C), 0.0, ALU.mult, ALU.add)
         scan(A("sgx", 2 * C, 3 * C), A("keep", 0, C), A("sg", 2 * C, 3 * C), 0.0, ALU.mult, ALU.add)
+        if r == 0:
+            mid_setup()
         tt(A("dd", 0, 10), w16("sgx", 10, 20), w16("sgx", 0, 10), ALU.subtract)
         tt(A("dd", 10, 20), w16("sgx", 0, 10), w16("sgx", 10, 20), ALU.subtract)
         tt(A("dd", 20, 40), w16("sgx", 20, 40), w16("sgx", 0, 20), ALU.subtract)
@@ -281,9 +302,11 @@ def rank_program(g, core, T, topo):
         tt(A("off", 0, 20), A("t20", 0, 20), A("bb", 40, 60), ALU.mult)
         tt(A("do", 30, 40), w16("sgx", 50, 60), w16("sgx", 0, 10), ALU.subtract)
         cp(A("cu", 0, 20), A("off", 0, 20))
-        cp(CW, IND(IO, A("cu", 0, 20)))
         if r == 0:
             late_setup()
+        cp(CW, IND(IO, A("cu", 0, 20)))
+        if r == 0:
+            ts(A("tauo", 0, 60), A("tauo", 0, 60), TINY, ALU.mult)
         for b in range(4):
             mm(A("pd", 512 * b, 512 * b + C), A("qeb", 128 * b, 128 * b + 128), A("seb", 128 * b, 128 * b + 128), QX, SX)
         small = [
@@ -382,20 +405,25 @@ def rank_program(g, core, T, topo):
         ride(99)
         back(99)
 
-        ts(A("ci", 0, C), IND(CW, POS), 1.0, ALU.add)
-        scan(A("ci", C, 2 * C), A("mone", 0, C), A("ci", 0, C), 1.0, ALU.add, ALU.add)
-        pick(A("ex", 0, 2 * C), A("ci", 0, 2 * C), 2 * C)
-        ts(A("t40", 0, 20), w16("ex", 0, 20), A("pc", 3, 4), ALU.mult, 2.0 * BIG - 2.0, ALU.add)
-        ts(A("t40", 20, 40), w16("ex", 20, 40), SCL, ALU.mult)
-        tt(A("t20", 0, 20), A("t40", 0, 20), A("t40", 20, 40), ALU.add)
-        tt(A("off", 0, 20), A("t20", 0, 20), A("k2", 0, 20), ALU.min)
-        cp(A("destu", 0, 20), A("off", 0, 20))
-        ts(A("t41", 0, 20), A("t20", 0, 20), float(S), ALU.is_lt)
-        scatter(A("win", 0, 3 * S), A("destu", 0, 20), A("iota", 1, C + 1))
-        act(A("x1", 0, C), IND(A("tabx", 0, 3 * S), A("destu", 0, 20)))
+        ts(A("ci", 0, S), IND(CW, L("posu", 0, 0, S)), 1.0, ALU.add)
+        ts(A("ci", S, C), IND(CW, L("posu", 0, S, C)), 1.0, ALU.add)
+        scan(A("ci", C, C + S), A("mone", 0, S), A("ci", 0, S), 1.0, ALU.add, ALU.add)
+        pick(A("ex", 0, C), A("ci", 0, C), C)
+        last_a = A("ci", C + S - 1, C + S)
+        add("v", lambda: g.vector.tensor_tensor_scan(T.ci[:, C + S:2 * C], T.mone[:, 0:S], T.ci[:, S:C], last_a[0], ALU.add, ALU.add),
+            [A("ci", C + S, 2 * C)], [A("mone", 0, S), A("ci", S, C), last_a])
+        pick(A("ex", C, C + S), A("ci", C, C + S), S)
+        tt(A("t40", 0, 20), w16("ex", 0, 20), A("k2", 0, 20), ALU.mult)
+        pick(A("ex", C + S, 2 * C), A("ci", C + S, 2 * C), S)
+        tt(A("t40", 20, 40), A("k3", 0, 20), A("t40", 0, 20), ALU.subtract)
+        tt(A("t20", 0, 20), w16("ex", 20, 40), A("t40", 20, 40), ALU.add)
+        ts(A("destu", 0, 20), A("t20", 0, 20), SCL, ALU.mult)
+        ts(A("t41", 0, 20), A("t20", 0, 20), SCL, ALU.mult, float(S), ALU.is_lt)
+        scatter(A("win", 0, WW), A("destu", 0, 20), A("iota", 1, C + 1))
+        act(A("x1", 0, C), IND(A("tabx", 0, WW), A("destu", 0, 20)))
         act(A("x1g", 0, C), IND(A("x1", 0, C), A("nu", 0, 20)))
         act(A("x1g", C, 2 * C), IND(A("x1", 0, C), A("nu", 20, 40)))
-        ts(A("t41", 20, 40), A("t20", 0, 20), 1.0, ALU.add)
+        ts(A("t41", 20, 40), A("t20", 0, 20), SCL, ALU.mult, 1.0, ALU.add)
         ts(A("t41", 40, 60), A("t41", 0, 20), 8192.0, ALU.mult)
         pick(A("exf", 0, S), A("win", 0, S), S)
         tt(A("xn", 0, 20), A("t41", 0, 20), A("t41", 20, 40), ALU.mult)
@@ -460,14 +488,14 @@ def rank_program(g, core, T, topo):
                 tt(A("tt", C * b, C * b + C), IND(A("hh", HW * b, HW * b + S + 1), S2), A("t2", C * b, C * b + C), ALU.add)
             if b > 0:
                 a = b - 1
-                tt(A("xa", a, 4 * C, 4), A("pd", 512 * a, 512 * a + C), A("tt", C * a, C * a + C), ALU.add)
-            if last and b == 0:
-                quant(A("qv", 0, 128), A("sv", 0, 128), A("vin", 0, 512))
+                for lo, hi in ([(0, C)] if a < 3 else [(0, S), (S, C)]):
+                    tt(A("xa", 4 * lo + a, 4 * hi, 4), A("pd", 512 * a + lo, 512 * a + hi), A("tt", C * a + lo, C * a + hi), ALU.add)
         if last:
             act(A("tabp", 1, S + 1), IND(A("iota", 0, C + 1), CP))
             act(A("prep", 0, C), IND(A("tabp", 0, S + 1), S1))
             dma("s", T.op[:], T.prep[0:128:16, 0:C], [], [A("prep", 0, C)])
-        quant(QX, SX, A("xa", 0, 4 * C))
+        quant(A("qx", 0, S), A("sx", 0, S), A("xa", 0, 4 * S))
+        quant(A("qx", S, C), A("sx", S, C), A("xa", 4 * S, 4 * C))
 
     dma("y", T.oc[:], T.qx[:, 0:C].bitcast(dt.uint8), [], [QX])
     mm(A("ph", 0, S), A("qv", 0, 128), A("sv", 0, 128), A("qx", 0, S), A("sx", 0, S))

@@ -6,7 +6,7 @@ C, S, ROUNDS, SWEEPS = 320, 160, 3, 8
 FW, HW = 336, 176
 BIG = 512.0
 TINY = 2.0 ** -110
-HOP1_S, HOP2_S, HOP3_S = True, True, False
+HOP1_S, HOP2_S, HOP3_S = True, True, True
 HALVES = True
 
 F32, B16, I32, U16, Q8, U8 = "float32", "bfloat16", "int32", "uint16", "float8_e4m3fn_x4", "uint8"
@@ -52,7 +52,7 @@ _sb("i16 own k2 off t20", 32, F32)
 _sb("nw xn cz wp wm tp tf", 80, F32)
 _sb("nf mw tau tauo dd bb do eo ww l1 l2 t40 t41", 64, F32)
 _sb("kw ci", 2 * C, B16)
-_sb("cc gg g2 lo2 a1 a2 a3 n2g u1 uu k1 x1 r1 r2", C, B16)
+_sb("sh cc gg g2 lo2 a1 a2 a3 n2g u1 uu k1 x1 r1 r2", C, B16)
 _sb("sp", S, B16)
 _sb("tabx", WW, B16)
 _sb("fn f2", 4 * FW, B16)
@@ -273,8 +273,13 @@ def rank_program(g, core, T, topo):
         return A(name, base + a // 16, base + b // 16)
 
     rid, pid = topo.addr(nxt)[0], topo.addr(nxt)[1]
-    omask = topo.mask(core, nxt)
-    n_out, n_in = len(topo.engines(core, nxt)), len(topo.engines(prv, core))
+
+    def lanes(src, dst):
+        e = topo.engines(src, dst)
+        return e[::max(1, len(e) // 8)]
+
+    omask = sum(1 << e for e in lanes(core, nxt))
+    n_out, n_in = len(lanes(core, nxt)), len(lanes(prv, core))
 
     for r in range(ROUNDS):
         last = r == ROUNDS - 1
@@ -304,7 +309,8 @@ def rank_program(g, core, T, topo):
         cp(A("cu", 0, 20), A("off", 0, 20))
         if r == 0:
             late_setup()
-        cp(CW, IND(IO, A("cu", 0, 20)))
+        act(A("cc", S, C), IND(IO, A("cu", 10, 20)))
+        cp(A("cc", 0, S), IND(IO, A("cu", 0, 10)))
         if r == 0:
             ts(A("tauo", 0, 60), A("tauo", 0, 60), TINY, ALU.mult)
         for b in range(4):
@@ -320,9 +326,10 @@ def rank_program(g, core, T, topo):
             lambda: ts(A("ww", 40, 60), A("ww", 20, 40), 4.0, ALU.mult, 5.0, ALU.add),
             lambda: tt(A("t20", 0, 20), A("ww", 0, 20), A("ww", 40, 60), ALU.add),
             lambda: cp(A("cu", 0, 20), A("t20", 0, 20)),
-            lambda: (act(A("r1", 0, C), IND(IO, A("cu", 0, 20))), act(A("r2", 0, C), IND(A("r1", 0, C), POS)),
+            lambda: (bg.insert(0, lambda: act(A("r2", 0, C), IND(A("r1", 0, C), POS))),
+                     bg.insert(0, lambda: act(A("r1", 0, C), IND(IO, A("cu", 0, 20)))),
                      fill(A("win", 0, S), float(C + 1))),
-            None,
+            None, None, None, None,
             lambda: pick(A("ex", 0, C), A("r2", 0, C), C),
             lambda: ts(A("mi", 0, 20), w16("ex", 0, 20), SCL, ALU.mult, -1.0, ALU.add),
             lambda: (ts(A("mj", 0, 20), A("mi", 0, 20), 3, ALU.bitwise_and),
@@ -356,14 +363,15 @@ def rank_program(g, core, T, topo):
                     bg.pop(0)()
 
         for sw in range(1, SWEEPS):
-            if HOP2_S:
-                act(A("n2g", 0, C), IND(CW, M2))
+            act(A("sh", 0, S), IND(CW, A("mu", 10, 20)))
+            for a, b in parts:
+                act(A("n2g", a, b), IND(CW, L("mu", 20, a, b)))
             back()
             ride()
             tt(A("sp", 0, S), A("cc", S, C), A("cc", 0, S), ALU.subtract)
             ride()
             tt(A("u1", 0, S), IND(CW, A("mu", 0, 10)), A("sp", 0, S), ALU.add)
-            tt(A("u1", S, C), IND(CW, A("mu", 10, 20)), A("sp", 0, S), ALU.subtract)
+            tt(A("u1", S, C), A("sh", 0, S), A("sp", 0, S), ALU.subtract)
             ride()
             for a, b in parts:
                 if HOP2_S:
@@ -375,7 +383,8 @@ def rank_program(g, core, T, topo):
                 ts(A("g2", a, b), A("uu", a, b), 1.0, ALU.min, 1.0, ALU.add)
             ride()
             if HOP3_S:
-                act(A("n2g", 0, C), IND(GW, M2))
+                for a, b in strap:
+                    act(A("n2g", a, b), IND(GW, L("mu", 20, a, b)))
             tt(A("k1", S, C), IND(GW, A("mu", 10, 20)), A("g2", 0, S), ALU.mult)
             tt(A("k1", 0, S), IND(GW, A("mu", 0, 10)), A("g2", S, C), ALU.mult)
             for a, b in strap:
@@ -387,13 +396,14 @@ def rank_program(g, core, T, topo):
                 ts(A("kw", C + a, C + b), A("kw", a, b), 0.5, ALU.mult)
                 ts(A("lo2", a, b), A("kw", a, b), 0.5, ALU.mult)
             ride()
-            if HOP1_S:
-                act(A("a3", 0, C), IND(KW, A("lu", 40, 60)), scale=-1.0, bias=1.25)
+            act(A("sh", S, C), IND(KW, A("lu", 20, 30)))
+            for a, b in strap:
+                act(A("a3", a, b), IND(KW, L("lu", 40, a, b)), scale=-1.0, bias=1.25)
             back()
             for a, b in strap:
                 tt(A("a1", a, b), IND(KW, L("lu", 0, a, b)), A("lo2", a, b), ALU.subtract)
-            for a, b in strap:
-                tt(A("a2", a, b), IND(KW, L("lu", 20, a, b)), A("a1", a, b), ALU.add)
+            tt(A("a2", S, C), IND(KW, A("lu", 30, 40)), A("a1", S, C), ALU.add)
+            tt(A("a2", 0, S), A("sh", S, C), A("a1", 0, S), ALU.add)
             if HOP1_S:
                 for a, b in strap:
                     tt(A("cc", a, b), A("a2", a, b), A("a3", a, b), ALU.is_lt)
@@ -406,7 +416,7 @@ def rank_program(g, core, T, topo):
         back(99)
 
         ts(A("ci", 0, S), IND(CW, L("posu", 0, 0, S)), 1.0, ALU.add)
-        ts(A("ci", S, C), IND(CW, L("posu", 0, S, C)), 1.0, ALU.add)
+        act(A("ci", S, C), IND(CW, L("posu", 0, S, C)), bias=1.0)
         scan(A("ci", C, C + S), A("mone", 0, S), A("ci", 0, S), 1.0, ALU.add, ALU.add)
         pick(A("ex", 0, C), A("ci", 0, C), C)
         last_a = A("ci", C + S - 1, C + S)
@@ -465,10 +475,10 @@ def rank_program(g, core, T, topo):
         ts(A("mj", 0, 20), A("mi", 0, 20), 1023, ALU.bitwise_and)
         cp(FQ, A("mj", 20, 40))
         cp(S1, A("mj", 0, 20))
-        for a, b in parts:
-            ts(A("r1", a, b), IND(IO, L("s12u", 0, a, b)), 1.0, ALU.add)
-        for a, b in parts:
-            cp(A("r2", a, b), IND(A("r1", 0, C), L("s12u", 20, a, b)))
+        ts(A("r1", 0, S), IND(IO, L("s12u", 0, 0, S)), 1.0, ALU.add)
+        act(A("r1", S, C), IND(IO, L("s12u", 0, S, C)), bias=1.0)
+        cp(A("r2", 0, S), IND(A("r1", 0, C), L("s12u", 20, 0, S)))
+        act(A("r2", S, C), IND(A("r1", 0, C), L("s12u", 20, S, C)))
         for a, b in parts:
             pick(A("ex", a, b), A("r2", a, b), b - a)
         for a, b in parts:
@@ -476,15 +486,23 @@ def rank_program(g, core, T, topo):
 
         for b in range(4):
             mm(A("ph", 512 * b, 512 * b + S), A("qw", 128 * b, 128 * b + 128), A("sw", 128 * b, 128 * b + 128), A(lq, 0, S), A(ls, 0, S))
-        act(A("hh", 1, S + 1), A("ph", 0, S), scale=2.0 ** -6)
-        for b in range(1, 3):
-            ts(A("hh", HW * b + 1, HW * b + S + 1), A("ph", 512 * b, 512 * b + S), 2.0 ** -6, ALU.mult)
         for b in range(4):
-            if b == 2:
-                act(A("hh", HW * 3 + 1, HW * 3 + S + 1), A("ph", 512 * 3, 512 * 3 + S), scale=2.0 ** -6)
+            ts(A("hh", HW * b + 1, HW * b + S + 1), A("ph", 512 * b, 512 * b + S), 2.0 ** -6, ALU.mult)
+        for lo, hi in parts:
+            act(A("t2", lo, hi), IND(A("hh", 0, S + 1), L("s12u", 0, lo, hi)))
+        for b in range(1, 4):
             act(A("t2", C * b, C * b + C), IND(A("hh", HW * b, HW * b + S + 1), S1))
+        act(A("a1", 0, C), IND(A("hh", HW * 3, HW * 3 + S + 1), S2))
         for b in range(5):
-            if b < 4:
+            if b == 3:
+                tt(A("xa", 2, 4 * C, 4), A("pd", 1024, 1024 + C), A("tt", 2 * C, 3 * C), ALU.add)
+                for lo, hi in ((0, S), (S, C)):
+                    tt(A("tt", C * b + lo, C * b + hi), A("a1", lo, hi), A("t2", C * b + lo, C * b + hi), ALU.add)
+                continue
+            if b == 0:
+                for lo, hi in parts:
+                    tt(A("tt", lo, hi), IND(A("hh", 0, S + 1), L("mnu", 0, lo, hi)), A("t2", lo, hi), ALU.add)
+            elif b < 3:
                 tt(A("tt", C * b, C * b + C), IND(A("hh", HW * b, HW * b + S + 1), S2), A("t2", C * b, C * b + C), ALU.add)
             if b > 0:
                 a = b - 1

@@ -2,14 +2,20 @@ from concourse.mybir import dt, AluOpType, ActivationFunctionType
 
 ALU = AluOpType
 ACT = ActivationFunctionType
-C, S, ROUNDS, SWEEPS = 320, 160, 3, 8
+C, S, Q, ROUNDS, SWEEPS = 320, 160, 80, 3, 8
 FW, HW = 336, 176
 BIG = 512.0
 TINY = 2.0 ** -110
-HOP1_S, HOP2_S, HOP3_S = True, True, True
-HALVES = True
+RANK = 2 ** 18
+OWN, SURE = 2.0 ** 20, 2.0 ** 21
+WAKE, LOAD, TRIP = 185.0, 2000.0, 3500.0
+HH_ON = "vvss"
+Q_ON = ("vv", "vv", "vv", "ss")
+HI0, CC0 = "s", "d"
+FIT = 20.0
 
 F32, B16, I32, U16, Q8, U8 = "float32", "bfloat16", "int32", "uint16", "float8_e4m3fn_x4", "uint8"
+WIDTH = {F32: 4, B16: 2, I32: 4, U16: 2, Q8: 4, U8: 1}
 SCRATCH = {}
 
 
@@ -22,8 +28,9 @@ _sb("xin xa", 4 * C, B16)
 _sb("uin vin", 512, B16)
 _sb("eb", 2048, B16)
 _sb("one", 512, B16)
-_sb("mone isa inc yy jm nmask e1", C, B16)
-_sb("mask keep mx x1g ex", 3 * C, B16)
+_sb("mone isa inc jm nmask e1", C, B16)
+_sb("mask keep mx", 2 * C, B16)
+_sb("x1g ex", 4 * C, B16)
 _sb("qx", C, Q8)
 _sb("sx", C, U8)
 _sb("qu qv qup", 128, Q8)
@@ -34,31 +41,27 @@ for _r in range(ROUNDS):
     _sb("qe%d lq%d" % (_r, _r), S, Q8)
     _sb("se%d ls%d" % (_r, _r), S, U8)
 _sb("nin", 64, I32)
-_sb("pidx pmi", 8, I32)
-_sb("mi mj", 64, I32)
+_sb("pidx", 8, I32)
+_sb("mi mj wp", 80, I32)
 _sb("nu lu sl mu", 64, U16)
-_sb("upk mnu posu cu destu cposu topu", 32, U16)
-_sb("s12u", 48, U16)
+_sb("upk mnu posu cu eu ou destu cposu topu s1u fqu s2u", 32, U16)
 _sb("iota pi1 pos1", FW, F32)
 _sb("nrep posn gp exf", 2 * C, F32)
 _sb("sc prep yo", C, F32)
 _sb("sg sgx", 3 * C, F32)
 WW = 656
 _sb("win", WW, F32)
-_sb("k3", 32, F32)
 _sb("tabp", HW, F32)
 _sb("pc", 8, F32)
-_sb("i16 own k2 off t20", 32, F32)
-_sb("nw xn cz wp wm tp tf", 80, F32)
-_sb("nf mw tau tauo dd bb do eo ww l1 l2 t40 t41", 64, F32)
-_sb("kw ci", 2 * C, B16)
-_sb("sh cc gg g2 lo2 a1 a2 a3 n2g u1 uu k1 x1 r1 r2", C, B16)
-_sb("sp", S, B16)
-_sb("tabx", WW, B16)
+_sb("nw cz wm tp tq tf kk sm", 80, F32)
+_sb("eo ww kc", 64, B16)
+_sb("nf mw tau tauo dd bb do l2 t40 t41 s0", 64, F32)
+_sb("kw ci exs", 2 * C, B16)
+_sb("cc gg c2 ee a1 a2 a3 n2g u1 u2 n3g k1 sp x1 c0 r1 r2", C, B16)
 _sb("fn f2", 4 * FW, B16)
-_sb("et e2", 4 * S, B16)
+_sb("et", 4 * S, B16)
 _sb("hh", 4 * HW, B16)
-_sb("t2 tt", 4 * C, B16)
+_sb("t2 t3 tt", 4 * C, B16)
 SCRATCH["pd"] = ("psum", [128, 2048], F32)
 SCRATCH["ph"] = ("psum", [128, 2048], F32)
 
@@ -75,203 +78,203 @@ def rank_program(g, core, T, topo):
 
     def A(name, a, b, st=1):
         ap = T[name][:, a:b:st] if st != 1 else T[name][:, a:b]
-        if SCRATCH[name][0] == "psum":
+        n, ps = len(range(a, b, st)), SCRATCH[name][0] == "psum"
+        if ps:
             a, b = a // 512 * 512, (b + 511) // 512 * 512
-        return (ap, [(name, a, b)])
+        return (ap, [(name, a, b, st)], n, WIDTH[SCRATCH[name][2]], ps, False)
 
     def IND(w, o):
-        return (w[0].indirect(o[0]), w[1] + o[1])
+        return (w[0].indirect(o[0]), w[1] + o[1], 16 * o[2], w[3], False, True)
 
     def val(x):
         return x[0] if isinstance(x, tuple) else x
 
-    def add(q, fn, outs, ins, sem=None, n=1):
+    def add(q, fn, outs, ins, ns, sem=None, n=1, late=0.0):
         rd, wr = [], []
         for x in ins:
             if isinstance(x, tuple):
                 rd += x[1]
         for x in outs:
             wr += x[1]
-        ops.append({"q": q, "fn": fn, "r": rd, "w": wr, "sem": sem, "n": n, "used": False})
+        ops.append({"q": q, "fn": fn, "r": rd, "w": wr, "sem": sem, "n": n, "used": False, "ns": ns, "late": late})
+
+    def span(o, full, k=1.0):
+        if full[0][5]:
+            return 50.0 + 1.3 * o[2]
+        return 0.83 * max(64.0, o[2] * k * (0.5 if all(x[3] == 2 for x in full + [o]) else 1.0))
 
     def tt(o, a, b, op):
-        add("v", lambda: g.vector.tensor_tensor(o[0], a[0], b[0], op), [o], [a, b])
+        add("v", lambda: g.vector.tensor_tensor(o[0], a[0], b[0], op), [o], [a, b], span(o, [a, b], 1.0 if a[4] else 2.0))
 
     def ts(o, a, s1, op0, s2=None, op1=None):
         if op1 is None:
-            add("v", lambda: g.vector.tensor_scalar(o[0], a[0], val(s1), None, op0), [o], [a, s1])
+            add("v", lambda: g.vector.tensor_scalar(o[0], a[0], val(s1), None, op0), [o], [a, s1], span(o, [a]))
         else:
-            add("v", lambda: g.vector.tensor_scalar(o[0], a[0], val(s1), val(s2), op0, op1), [o], [a, s1, s2])
+            add("v", lambda: g.vector.tensor_scalar(o[0], a[0], val(s1), val(s2), op0, op1), [o], [a, s1, s2], span(o, [a]))
 
     def cp(o, a):
-        add("v", lambda: g.vector.tensor_copy(o[0], a[0]), [o], [a])
+        add("v", lambda: g.vector.tensor_copy(o[0], a[0]), [o], [a], span(o, [a]))
 
     def scatter(w, off, a):
-        add("v", lambda: g.vector.tensor_copy(w[0].indirect(off[0]), a[0]), [w], [a, off])
+        add("v", lambda: g.vector.tensor_copy(w[0].indirect(off[0]), a[0]), [w], [a, off], 50.0 + 3.2 * a[2])
 
     def fill(o, c):
-        add("v", lambda: g.vector.memset(o[0], c), [o], [])
+        add("v", lambda: g.vector.memset(o[0], c), [o], [], span(o, [o]))
 
     def scan(o, d0, d1, init, op0, op1):
-        add("v", lambda: g.vector.tensor_tensor_scan(o[0], d0[0], d1[0], init, op0, op1), [o], [d0, d1])
+        add("v", lambda: g.vector.tensor_tensor_scan(o[0], d0[0], d1[0], init, op0, op1), [o], [d0, d1], span(o, [d0, d1]))
 
-    def pick(o, d, n):
-        scan(o, A("mx", 0, n), d, 0.0, ALU.mult, ALU.max)
+    def pick(o, d):
+        scan(o, A("mx", 0, o[2]), d, 0.0, ALU.mult, ALU.max)
 
     def quant(q, s, a):
-        add("v", lambda: g.vector.quantize_mx(q[0], s[0], a[0]), [q, s], [a])
+        add("v", lambda: g.vector.quantize_mx(q[0], s[0], a[0]), [q, s], [a], 12.0 + 0.22 * a[2])
 
     def act(o, a, scale=1.0, bias=0.0):
         f = ACT.Copy if bias == 0.0 else ACT.Identity
-        add("s", lambda: g.scalar.activation(o[0], a[0], f, bias=bias, scale=scale), [o], [a])
+        add("s", lambda: g.scalar.activation(o[0], a[0], f, bias=val(bias), scale=val(scale)), [o], [a, scale, bias],
+            65.0 + 1.3 * o[2] if a[5] else 0.83 * max(64.0, o[2]))
+
+    def take(q, o, a):
+        (cp if q == "v" else act)(o, a)
 
     def mm(o, wq, ws, xq, xs):
-        add("t", lambda: g.tensor.matmul_mx(o[0], wq[0], ws[0], xq[0], xs[0], True, True), [o], [wq, ws, xq, xs])
+        add("t", lambda: g.tensor.matmul_mx(o[0], wq[0], ws[0], xq[0], xs[0], True, True), [o], [wq, ws, xq, xs], 1.25 * (o[2] + 16))
 
     def iota(o, pat, base, cm, flag):
         if flag:
-            add("g", lambda: g.iota(o[0], pat, base, cm, allow_small_or_imprecise_dtypes=True), [o], [])
+            add("g", lambda: g.iota(o[0], pat, base, cm, allow_small_or_imprecise_dtypes=True), [o], [], 130.0 + 1.66 * o[2])
         else:
-            add("g", lambda: g.iota(o[0], pat, base, cm), [o], [])
+            add("g", lambda: g.iota(o[0], pat, base, cm), [o], [], 130.0 + 1.66 * o[2])
 
     nd = [0]
 
-    def dma(q, o, a, outs, ins):
+    def dma(q, o, a, outs, ins, more=0.0):
         e = {"y": g.sync, "s": g.scalar}[q]
-        add(q, lambda: e.dma_start(o, a), outs, ins, sem="d%d" % nd[0], n=16)
+        add(q, lambda: e.dma_start(o, a), outs, ins, 60.0, sem="d%d" % nd[0], n=16, late=LOAD + more)
         nd[0] += 1
 
     def w16(name, a, b):
         return A(name, 16 * a + 15, 16 * b, 16)
 
-    SCL = A("pc", 2, 3)
+    def L(name, base, a, b):
+        return A(name, base + a // 16, base + b // 16)
+
+    PM, SCL, UNS, P15, P15R, HALF = (A("pc", k, k + 1) for k in (0, 2, 3, 4, 5, 6))
+    OWNW, K2, K3, OWNB = (A("kk", 20 * k, 20 * k + 20) for k in range(4))
+    I16, T20, OFF, T21 = (A("sm", 20 * k, 20 * k + 20) for k in range(4))
+    parts = [(0, S), (S, C)]
+    pairs = [[(h, h + Q), (h + Q, h)] for h in (0, S)]
+    cols = [(a // 16, b // 16) for p in pairs for a, b in p]
 
     for k, t in enumerate((T.n0, T.n1, T.n2)):
         dma("y", T.nin[:, 20 * k:20 * k + 20], t[:], [A("nin", 20 * k, 20 * k + 20)], [])
-    dma("s", T.xin[:], T.x[:], [A("xin", 0, 4 * C)], [])
-    dma("s", T.uin[:], T.u[:], [A("uin", 0, 512)], [])
+    dma("s", T.xin[:], T.x[:], [A("xin", 0, 4 * C)], [], 1500.0)
+    dma("s", T.uin[:], T.u[:], [A("uin", 0, 512)], [], 600.0)
 
     iota(A("pidx", 0, 1), [[1, 1]], 0, 1, False)
-    iota(A("i16", 0, 20), [[16, 20]], 0, 0, True)
+    iota(I16, [[16, 20]], 0, 0, True)
     iota(A("iota", 0, FW), [[1, FW]], 0, 0, True)
     iota(A("jm", 0, C), [[0, 20], [1, 16]], 0, 0, True)
     fill(A("one", 0, 512), 1.0)
     for b in range(4):
         o, i = A("eb", 512 * b, 512 * b + 512), A("one", 0, 512)
-        add("g", (lambda o, i, b: lambda: g.affine_select(o[0], i[0], [[-1, 512]], ALU.is_equal, 0.0, b, 4))(o, i, b), [o], [i])
-    ts(A("pmi", 0, 1), A("pidx", 0, 1), 15, ALU.bitwise_and)
+        add("g", (lambda o, i, b: lambda: g.affine_select(o[0], i[0], [[-1, 512]], ALU.is_equal, 0.0, b, 4))(o, i, b), [o], [i], 1020.0)
+    ts(A("pidx", 4, 5), A("pidx", 0, 1), 15, ALU.bitwise_and)
     fill(A("mone", 0, C), -1.0)
-    cp(A("pc", 0, 1), A("pmi", 0, 1))
-    cp(A("upk", 0, 8), A("i16", 0, 8))
-    fill(A("wp", 0, 20), 8192.0)
-    ts(A("pc", 1, 2), A("pc", 0, 1), 1.0, ALU.add)
-    ts(SCL, A("pc", 0, 1), 15.0, ALU.is_equal, 1.0 / BIG, ALU.max)
-    ts(A("own", 0, 20), A("i16", 0, 20), A("pc", 0, 1), ALU.add)
-    fill(A("fn", C, 4 * FW, FW), 0.0)
-    ts(A("pc", 3, 4), A("pc", 0, 1), 15.0, ALU.not_equal, BIG, ALU.mult)
+    cp(PM, A("pidx", 4, 5))
+    cp(A("upk", 0, 8), A("sm", 0, 8))
+    fill(A("wp", 0, 20), int(OWN))
+    ts(A("pc", 1, 2), PM, 1.0, ALU.add)
+    ts(SCL, PM, 15.0, ALU.is_equal, 1.0 / BIG, ALU.max)
+    ts(OWNW, I16, PM, ALU.add)
     fill(A("f2", C, 4 * FW, FW), 0.0)
-    fill(A("hh", 0, 4 * HW, HW), 0.0)
-    ts(A("k3", 0, 20), A("own", 0, 20), 2.0, ALU.mult, 2.0 * S + 2.0, ALU.add)
-    ts(A("pc", 3, 4), A("pc", 3, 4), 1.0, ALU.max)
-    fill(A("tabx", S, WW), 1.0)
-    fill(A("tabp", 0, 1), -1.0)
-    ts(A("k2", 0, 20), A("own", 0, 20), S + 2.0, ALU.add)
-    ts(A("k3", 0, 20), A("k3", 0, 20), A("pc", 3, 4), ALU.mult)
-    cp(A("mw", 0, 10), A("own", 10, 20))
-    cp(A("mw", 10, 20), A("own", 0, 10))
-    ts(A("tabx", 0, S), A("iota", 0, S), 2.0, ALU.add)
-
-    IO = A("iota", 0, C)
-    act(A("sc", 0, C), IO)
-    cp(A("nu", 0, 60), A("nin", 0, 60))
-    cp(A("nf", 0, 60), A("nin", 0, 60))
-    tt(A("isa", 0, C), IND(IO, A("nu", 0, 20)), A("sc", 0, C), ALU.is_gt)
-    act(A("nrep", 0, C), IND(IO, A("nu", 20, 40)), bias=1.0)
-    act(A("nrep", C, 2 * C), IND(IO, A("nu", 40, 60)), bias=1.0)
-    tt(A("t20", 0, 20), A("own", 0, 20), A("nf", 0, 20), ALU.min)
-    tt(A("off", 0, 20), A("own", 0, 20), A("nf", 0, 20), ALU.is_gt)
-    scan(A("inc", 0, C), A("one", 0, C), A("isa", 0, C), 0.0, ALU.mult, ALU.add)
-    cp(A("mnu", 0, 20), A("t20", 0, 20))
-    ts(A("nmask", 0, C), A("jm", 0, C), A("pc", 0, 1), ALU.not_equal)
+    fill(A("hh", 1, 4 * HW, HW), 0.0)
+    ts(UNS, PM, 15.0, ALU.not_equal, BIG, ALU.mult)
+    ts(UNS, UNS, 1.0, ALU.max)
+    ts(K3, OWNW, 2.0, ALU.mult, 2.0 * S + 2.0, ALU.add)
+    ts(K3, K3, UNS, ALU.mult)
+    ts(K2, OWNW, S + 2.0, ALU.add)
+    ts(OWNB, OWNW, BIG, ALU.mult)
+    fill(A("tabp", 1, 2), -1.0)
+    ts(P15, SCL, BIG, ALU.mult)
+    ts(P15R, SCL, float(RANK), ALU.mult)
+    ts(HALF, UNS, Q + 0.5, ALU.mult)
+    for k, c in enumerate((3.0, 15.0, 12.0)):
+        fill(A("kc", 20 * k, 20 * k + 20), c)
+    ts(A("nmask", 0, C), A("jm", 0, C), PM, ALU.not_equal)
     ts(A("e1", 0, C), A("jm", 0, C), A("pc", 1, 2), ALU.is_equal, BIG, ALU.mult)
-    cp(A("yy", 0, C), IND(A("inc", 0, C), A("mnu", 0, 20)))
     tt(A("mx", 0, C), A("nmask", 0, C), A("e1", 0, C), ALU.max)
-    ts(A("off", 0, 20), A("off", 0, 20), float(S), ALU.mult, -1.0, ALU.add)
     act(A("mask", 0, C), A("nmask", 0, C), scale=-1.0, bias=1.0)
-    for k in (1, 2):
-        dma("y", T.mx[:, k * C:k * C + C], T.mx[:, 0:C], [A("mx", k * C, k * C + C)], [A("mx", 0, C)])
-    pick(A("ex", 0, C), A("yy", 0, C), C)
-    quant(A("qu", 0, 128), A("su", 0, 128), A("uin", 0, 512))
     ts(A("keep", 0, C), A("jm", 0, C), 0.0, ALU.not_equal)
-    for nm in ("mask", "keep"):
-        for k in (1, 2):
-            dma("y", T[nm][:, k * C:k * C + C], T[nm][:, 0:C], [A(nm, k * C, k * C + C)], [A(nm, 0, C)])
+    for nm in ("mask", "keep", "mx"):
+        dma("y", T[nm][:, C:2 * C], T[nm][:, 0:C], [A(nm, C, 2 * C)], [A(nm, 0, C)])
     dma("y", T.qw[:].bitcast(dt.uint8), T.wc[:], [A("qw", 0, 512)], [])
     dma("y", T.sw[:], T.ws[:], [A("sw", 0, 512)], [])
     dma("y", T.vin[:], T.v[:], [A("vin", 0, 512)], [])
-    ts(A("t20", 0, 20), w16("ex", 0, 20), SCL, ALU.mult)
+    for b in range(4):
+        quant(A("qeb", 128 * b, 128 * b + 128), A("seb", 128 * b, 128 * b + 128), A("eb", 512 * b, 512 * b + 512))
+    quant(A("qv", 0, 128), A("sv", 0, 128), A("vin", 0, 512))
+    quant(A("qu", 0, 128), A("su", 0, 128), A("uin", 0, 512))
     up = A("upk", 0, 8)
     add("v", lambda: g.vector.tensor_copy(T.qup[:, 0:128].bitcast(dt.uint32), T.qu[:, 0:128].bitcast(dt.uint32).indirect(up[0])),
-        [A("qup", 0, 128)], [A("qu", 0, 128), up])
+        [A("qup", 0, 128)], [A("qu", 0, 128), up], 220.0)
     add("s", lambda: g.scalar.activation(T.sup[:, 0:128], T.su[:, 0:128].indirect(up[0]), ACT.Copy),
-        [A("sup", 0, 128)], [A("su", 0, 128), up])
-    tt(A("t20", 0, 20), A("t20", 0, 20), A("off", 0, 20), ALU.add)
+        [A("sup", 0, 128)], [A("su", 0, 128), up], 230.0)
     quant(A("qx", 0, C), A("sx", 0, C), A("xin", 0, 4 * C))
-    cp(A("posu", 0, 20), A("t20", 0, 20))
+
+    IO = A("iota", 0, C)
+    act(A("prep", 0, C), IO)
+    cp(A("nu", 0, 60), A("nin", 0, 60))
+    cp(A("nf", 0, 20), A("nin", 0, 20))
+    tt(A("isa", 0, C), IND(IO, A("nu", 0, 20)), A("prep", 0, C), ALU.is_gt)
+    act(A("nrep", 0, C), IND(IO, A("nu", 20, 40)), bias=1.0)
+    act(A("nrep", C, 2 * C), IND(IO, A("nu", 40, 60)), bias=1.0)
+    tt(T20, OWNW, A("nf", 0, 20), ALU.min)
+    tt(OFF, OWNW, A("nf", 0, 20), ALU.is_gt)
+    ts(A("nf", 0, 60), A("nin", 0, 60), BIG, ALU.mult)
+    scan(A("inc", 0, C), A("one", 0, C), A("isa", 0, C), 0.0, ALU.mult, ALU.add)
+    cp(A("mnu", 0, 20), T20)
+    for q, (a, b) in zip("vs", parts):
+        take(q, A("c0", a, b), IND(A("inc", 0, C), L("mnu", 0, a, b)))
+    ts(OFF, OFF, float(Q), ALU.mult, -1.0, ALU.add)
+    pick(A("ex", 0, C), A("c0", 0, C))
+    ts(A("t40", 0, 20), w16("ex", 0, 20), SCL, ALU.mult)
+    ts(A("t40", 20, 40), w16("ex", 0, 20), HALF, ALU.is_gt, float(Q), ALU.mult)
+    tt(A("t41", 0, 20), A("t40", 0, 20), OFF, ALU.add)
+    tt(A("t41", 20, 40), A("t41", 0, 20), A("t40", 20, 40), ALU.add)
+    cp(A("posu", 0, 20), A("t41", 20, 40))
     POS = A("posu", 0, 20)
     scatter(A("pi1", 0, C), POS, A("iota", 1, C + 1))
     act(A("pos1", 0, C), IND(IO, POS), bias=1.0)
     act(A("posn", 0, C), IND(A("pos1", 0, C), A("nu", 20, 40)))
     act(A("posn", C, 2 * C), IND(A("pos1", 0, C), A("nu", 40, 60)))
-
-    def unit(b):
-        quant(A("qeb", 128 * b, 128 * b + 128), A("seb", 128 * b, 128 * b + 128), A("eb", 512 * b, 512 * b + 512))
-
-    mm(A("ph", 0, C), A("qup", 0, 128), A("sup", 0, 128), A("qx", 0, C), A("sx", 0, C))
-    act(A("sc", 0, C), A("ph", 0, C))
-    unit(0)
-    pick(A("exf", 0, C), A("pi1", 0, C), C)
-    unit(1)
+    pick(A("exf", 0, C), A("pi1", 0, C))
     ts(A("sl", 0, 20), w16("exf", 0, 20), SCL, ALU.mult, -1.0, ALU.add)
     ts(A("nw", 0, 20), w16("exf", 0, 20), SCL, ALU.mult, -1.0, ALU.add)
     PI = A("sl", 0, 20)
-    unit(2)
     cp(A("gp", 0, C), IND(A("nrep", 0, C), PI))
     act(A("gp", C, 2 * C), IND(A("nrep", C, 2 * C), PI))
-    act(A("nrep", 0, C), IND(A("posn", 0, C), PI))
-    act(A("pos1", 0, C), IND(A("posn", C, 2 * C), PI))
-    cp(A("nw", 20, 30), A("nw", 10, 20))
-    cp(A("nw", 30, 40), A("nw", 0, 10))
-    pick(A("exf", 0, C), A("gp", 0, C), C)
-    pick(A("exf", C, 2 * C), A("gp", C, 2 * C), C)
-    ts(A("sl", 20, 40), w16("exf", 0, 20), SCL, ALU.mult, -1.0, ALU.add)
-    unit(3)
-    ts(A("sl", 40, 60), w16("exf", 20, 40), SCL, ALU.mult, -1.0, ALU.add)
-    ts(A("nw", 40, 80), w16("exf", 0, 40), SCL, ALU.mult, -1.0, ALU.add)
-    quant(A("qv", 0, 128), A("sv", 0, 128), A("vin", 0, 512))
+    act(A("win", 0, C), IND(A("posn", 0, C), PI))
+    act(A("win", C, 2 * C), IND(A("posn", C, 2 * C), PI))
+    for a, b in cols:
+        cp(A("nw", 20 + a, 25 + a), A("nw", b, b + 5))
+    for k in (0, 1):
+        pick(A("posn", C * k, C * k + C), A("gp", C * k, C * k + C))
+        ts(A("sl", 20 + 20 * k, 40 + 20 * k), w16("posn", 20 * k, 20 * k + 20), SCL, ALU.mult, -1.0, ALU.add)
+    ts(A("nw", 40, 80), w16("posn", 0, 40), SCL, ALU.mult, -1.0, ALU.add)
+    for k in (1, 2):
+        tt(A("tau", 20 * k, 20 * k + 20), A("nw", 20 * k + 20, 20 * k + 40), A("nw", 0, 20), ALU.subtract)
+        pick(A("exf", C * k - C, C * k), A("win", C * k - C, C * k))
+    ts(A("tau", 20, 60), A("tau", 20, 60), TINY, ALU.mult)
+    ts(A("mu", 0, 40), w16("exf", 0, 40), SCL, ALU.mult, -1.0, ALU.add)
+    ts(A("mw", 20, 60), A("mu", 0, 40), 1.0 / C, ALU.mult, 1.0, ALU.add)
+    for j, (lo, hi) in enumerate(((1, 2), (1, 3), (2, 3))):
+        tt(A("tauo", 20 * j, 20 * j + 20), A("nw", 20 * hi, 20 * hi + 20), A("nw", 20 * lo, 20 * lo + 20), ALU.subtract)
+    ts(A("tauo", 0, 60), A("tauo", 0, 60), TINY, ALU.mult)
 
-    def mid_setup():
-        for k in range(3):
-            tt(A("tau", 20 * k, 20 * k + 20), A("nw", 20 * k + 20, 20 * k + 40), A("nw", 0, 20), ALU.subtract)
-        pick(A("gp", 0, C), A("nrep", 0, C), C)
-        ts(A("tau", 0, 60), A("tau", 0, 60), TINY, ALU.mult)
-        pick(A("gp", C, 2 * C), A("pos1", 0, C), C)
-
-    def late_setup():
-        ts(A("mu", 0, 40), w16("gp", 0, 40), SCL, ALU.mult, -1.0, ALU.add)
-        ts(A("mw", 20, 60), w16("gp", 0, 40), SCL, ALU.mult, -1.0, ALU.add)
-        for j, (lo, hi) in enumerate(((1, 2), (1, 3), (2, 3))):
-            tt(A("tauo", 20 * j, 20 * j + 20), A("nw", 20 * hi, 20 * hi + 20), A("nw", 20 * lo, 20 * lo + 20), ALU.subtract)
-
-    M1, M2 = A("mu", 0, 20), A("mu", 20, 40)
     QX, SX = A("qx", 0, C), A("sx", 0, C)
     CW, GW, KW = A("cc", 0, C), A("gg", 0, C), A("kw", 0, 2 * C)
-    parts = [(0, S), (S, C)] if HALVES else [(0, C)]
-    strap = parts[::-1]
-
-    def L(name, base, a, b):
-        return A(name, base + a // 16, base + b // 16)
-
     rid, pid = topo.addr(nxt)[0], topo.addr(nxt)[1]
 
     def lanes(src, dst):
@@ -283,286 +286,252 @@ def rank_program(g, core, T, topo):
 
     for r in range(ROUNDS):
         last = r == ROUNDS - 1
-        if r > 0:
+        if r == 0:
+            mm(A("ph", 0, C), A("qup", 0, 128), A("sup", 0, 128), QX, SX)
+            act(A("sc", 0, C), A("ph", 0, C))
+        else:
             mm(A("ph", 0, S), A("qup", 0, 128), A("sup", 0, 128), A("qx", 0, S), A("sx", 0, S))
             mm(A("ph", 512, 512 + S), A("qup", 0, 128), A("sup", 0, 128), A("qx", S, C), A("sx", S, C))
-            cp(A("sc", 0, S), A("ph", 0, S))
+            act(A("sc", 0, S), A("ph", 0, S))
             cp(A("sc", S, C), A("ph", 512, 512 + S))
+        for b in range(4):
+            mm(A("pd", 512 * b, 512 * b + C), A("qeb", 128 * b, 128 * b + 128), A("seb", 128 * b, 128 * b + 128), QX, SX)
+            act(A("fn", FW * b, FW * b + C), A("pd", 512 * b, 512 * b + C), scale=0.5)
         tt(A("sg", 0, 2 * C), IND(A("sc", 0, C), A("sl", 0, 40)), A("mask", 0, 2 * C), ALU.mult)
         tt(A("sg", 2 * C, 3 * C), IND(A("sc", 0, C), A("sl", 40, 60)), A("mask", 0, C), ALU.mult)
         scan(A("sgx", 0, 2 * C), A("keep", 0, 2 * C), A("sg", 0, 2 * C), 0.0, ALU.mult, ALU.add)
         scan(A("sgx", 2 * C, 3 * C), A("keep", 0, C), A("sg", 2 * C, 3 * C), 0.0, ALU.mult, ALU.add)
-        if r == 0:
-            mid_setup()
-        tt(A("dd", 0, 10), w16("sgx", 10, 20), w16("sgx", 0, 10), ALU.subtract)
-        tt(A("dd", 10, 20), w16("sgx", 0, 10), w16("sgx", 10, 20), ALU.subtract)
-        tt(A("dd", 20, 40), w16("sgx", 20, 40), w16("sgx", 0, 20), ALU.subtract)
-        tt(A("dd", 40, 60), w16("sgx", 40, 60), w16("sgx", 0, 20), ALU.subtract)
-        tt(A("bb", 0, 40), A("dd", 0, 40), A("tau", 0, 40), ALU.is_lt)
-        tt(A("do", 0, 10), w16("sgx", 20, 30), w16("sgx", 10, 20), ALU.subtract)
-        tt(A("bb", 40, 60), A("dd", 40, 60), A("tau", 40, 60), ALU.is_lt)
-        tt(A("t20", 0, 20), A("bb", 0, 20), A("bb", 20, 40), ALU.mult)
-        tt(A("do", 10, 20), w16("sgx", 30, 40), w16("sgx", 0, 10), ALU.subtract)
-        tt(A("do", 20, 30), w16("sgx", 40, 50), w16("sgx", 10, 20), ALU.subtract)
-        tt(A("off", 0, 20), A("t20", 0, 20), A("bb", 40, 60), ALU.mult)
-        tt(A("do", 30, 40), w16("sgx", 50, 60), w16("sgx", 0, 10), ALU.subtract)
-        cp(A("cu", 0, 20), A("off", 0, 20))
-        if r == 0:
-            late_setup()
-        act(A("cc", S, C), IND(IO, A("cu", 10, 20)))
-        cp(A("cc", 0, S), IND(IO, A("cu", 0, 10)))
-        if r == 0:
-            ts(A("tauo", 0, 60), A("tauo", 0, 60), TINY, ALU.mult)
-        for b in range(4):
-            mm(A("pd", 512 * b, 512 * b + C), A("qeb", 128 * b, 128 * b + 128), A("seb", 128 * b, 128 * b + 128), QX, SX)
-        small = [
-            lambda: (ts(A("l1", 0, 60), A("bb", 0, 60), float(C), ALU.mult),
-                     tt(A("do", 40, 60), w16("sgx", 40, 60), w16("sgx", 20, 40), ALU.subtract)),
-            lambda: tt(A("l2", 0, 60), A("l1", 0, 60), A("mw", 0, 60), ALU.add),
-            lambda: cp(A("lu", 0, 60), A("l2", 0, 60)),
-            lambda: tt(A("eo", 0, 60), A("do", 0, 60), A("tauo", 0, 60), ALU.is_lt),
-            lambda: (tt(A("ww", 20, 40), A("eo", 40, 60), A("eo", 0, 20), ALU.subtract),
-                     tt(A("ww", 0, 20), A("eo", 0, 20), A("eo", 20, 40), ALU.add)),
-            lambda: ts(A("ww", 40, 60), A("ww", 20, 40), 4.0, ALU.mult, 5.0, ALU.add),
-            lambda: tt(A("t20", 0, 20), A("ww", 0, 20), A("ww", 40, 60), ALU.add),
-            lambda: cp(A("cu", 0, 20), A("t20", 0, 20)),
-            lambda: (bg.insert(0, lambda: act(A("r2", 0, C), IND(A("r1", 0, C), POS))),
-                     bg.insert(0, lambda: act(A("r1", 0, C), IND(IO, A("cu", 0, 20)))),
-                     fill(A("win", 0, S), float(C + 1))),
-            None, None, None, None,
-            lambda: pick(A("ex", 0, C), A("r2", 0, C), C),
-            lambda: ts(A("mi", 0, 20), w16("ex", 0, 20), SCL, ALU.mult, -1.0, ALU.add),
-            lambda: (ts(A("mj", 0, 20), A("mi", 0, 20), 3, ALU.bitwise_and),
-                     ts(A("mj", 20, 40), A("mi", 0, 20), 12, ALU.bitwise_and)),
-            lambda: (ts(A("wp", 20, 40), A("mj", 0, 20), 1024.0, ALU.mult, 1024.0, ALU.add),
-                     ts(A("wp", 40, 60), A("mj", 20, 40), 256.0, ALU.mult, 1024.0, ALU.add)),
-            lambda: tt(A("t20", 0, 20), A("wp", 20, 40), A("wp", 40, 60), ALU.add),
-            lambda: ts(A("wp", 60, 80), A("t20", 0, 20), -1.0, ALU.mult, 6144.0, ALU.add),
-            lambda: tt(A("wm", 20, 80), A("wp", 20, 80), A("nf", 0, 60), ALU.add),
-            lambda: tt(A("t20", 0, 20), A("wm", 20, 40), A("wm", 40, 60), ALU.max),
-            lambda: tt(A("mi", 0, 20), A("t20", 0, 20), A("wm", 60, 80), ALU.max),
-            lambda: ts(A("mj", 0, 20), A("mi", 0, 20), 1023, ALU.bitwise_and),
-            lambda: cp(A("topu", 0, 20), A("mj", 0, 20)),
-        ]
-        bg = []
-        for b in range(4):
-            bg.append((lambda b: lambda: act(A("fn", FW * b, FW * b + C), A("pd", 512 * b, 512 * b + C), scale=0.5))(b))
-        for b in range(4):
-            bg.append((lambda b: lambda: act(A("f2", FW * b, FW * b + C), IND(A("fn", FW * b, FW * b + C), A("topu", 0, 20))))(b))
+        for k in (1, 2):
+            tt(A("dd", 20 * k, 20 * k + 20), w16("sgx", 20 * k, 20 * k + 20), w16("sgx", 0, 20), ALU.subtract)
+            tt(A("bb", 20 * k, 20 * k + 20), A("dd", 20 * k, 20 * k + 20), A("tau", 20 * k, 20 * k + 20), ALU.is_lt)
+        for a, b in cols:
+            tt(A("bb", a, a + 5), w16("sgx", a, a + 5), w16("sgx", b, b + 5), ALU.is_ge if a < b else ALU.is_gt)
+            cp(A("s0", a, a + 5), w16("sgx", b, b + 5))
+        tt(T20, A("bb", 0, 20), A("bb", 20, 40), ALU.mult)
+        tt(OFF, T20, A("bb", 40, 60), ALU.mult)
+        cp(A("cu", 0, 20), OFF)
+        for q, (a, b) in zip("vs", parts):
+            take(q, A("cc", a, b), IND(IO, L("cu", 0, a, b)))
+        for p in pairs:
+            for a, b in p:
+                cp(A("c2", a, a + Q), A("cc", b, b + Q))
+        cp(A("eu", 0, 20), A("bb", 0, 20))
+        for a, b in parts:
+            act(A("ee", a, b), IND(IO, L("eu", 0, a, b)), scale=-0.5, bias=0.5)
+        tt(A("l2", 0, 40), A("mw", 20, 60), A("bb", 20, 60), ALU.subtract)
+        ts(A("lu", 0, 40), A("l2", 0, 40), float(C), ALU.mult)
+        act(A("win", 0, S), A("one", 0, S), scale=float(C + 1))
 
-        def ride(n=1):
-            for _ in range(n):
-                if small:
-                    step = small.pop(0)
-                    if step is not None:
-                        step()
-
-        def back(n=1):
-            for _ in range(n):
-                if bg and (len(bg) > 4 or not small):
-                    bg.pop(0)()
+        tt(A("do", 0, 20), w16("sgx", 20, 40), A("s0", 0, 20), ALU.subtract)
+        tt(A("do", 20, 40), w16("sgx", 40, 60), A("s0", 0, 20), ALU.subtract)
+        tt(A("do", 40, 60), w16("sgx", 40, 60), w16("sgx", 20, 40), ALU.subtract)
+        tt(A("eo", 0, 60), A("do", 0, 60), A("tauo", 0, 60), ALU.is_lt)
+        tt(A("ww", 0, 60), A("eo", 0, 60), A("kc", 0, 60), ALU.mult)
+        tt(A("s0", 20, 40), A("ww", 0, 20), A("ww", 20, 40), ALU.add)
+        tt(A("s0", 40, 60), A("s0", 20, 40), A("ww", 40, 60), ALU.add)
+        ts(A("ou", 0, 20), A("s0", 40, 60), -1.0, ALU.mult, 57.0, ALU.add)
+        for a, b in parts:
+            act(A("r1", a, b), IND(IO, L("ou", 0, a, b)), scale=P15R)
+        for a, b in parts:
+            act(A("r2", a, b), IND(A("r1", 0, C), L("posu", 0, a, b)))
+        for a, b in parts:
+            pick(A("ex", a, b), A("r2", a, b))
+        cp(A("mi", 0, 20), w16("ex", 0, 20))
+        ts(A("wp", 20, 40), A("mi", 0, 20), 3 * RANK, ALU.bitwise_and)
+        for k in (1, 2):
+            ts(A("wp", 20 + 20 * k, 40 + 20 * k), A("mi", 0, 20), 2 * k, ALU.logical_shift_right, 3 * RANK, ALU.bitwise_and)
+        for k in range(3):
+            tt(A("wm", 20 + 20 * k, 40 + 20 * k), A("wp", 20 + 20 * k, 40 + 20 * k), A("nf", 20 * k, 20 * k + 20), ALU.add)
+        tt(T21, A("wm", 20, 40), A("wm", 40, 60), ALU.max)
+        tt(A("mi", 20, 40), T21, A("wm", 60, 80), ALU.max)
+        ts(A("mj", 0, 20), A("mi", 20, 40), 9, ALU.logical_shift_right, int(BIG) - 1, ALU.bitwise_and)
+        cp(A("topu", 0, 20), A("mj", 0, 20))
+        for p in range(4):
+            for a, b in parts:
+                act(A("f2", FW * p + a, FW * p + b), IND(A("fn", FW * p, FW * p + C), L("topu", 0, a, b)))
+            for a in range(FW * p, FW * p + C, 64):
+                tt(A("f2", a, a + 64), A("f2", a, a + 64), A("fn", a, a + 64), ALU.add)
 
         for sw in range(1, SWEEPS):
-            act(A("sh", 0, S), IND(CW, A("mu", 10, 20)))
             for a, b in parts:
                 act(A("n2g", a, b), IND(CW, L("mu", 20, a, b)))
-            back()
-            ride()
-            tt(A("sp", 0, S), A("cc", S, C), A("cc", 0, S), ALU.subtract)
-            ride()
-            tt(A("u1", 0, S), IND(CW, A("mu", 0, 10)), A("sp", 0, S), ALU.add)
-            tt(A("u1", S, C), A("sh", 0, S), A("sp", 0, S), ALU.subtract)
-            ride()
+                tt(A("u2", a, b), IND(CW, L("mu", 0, a, b)), A("c2", a, b), ALU.max)
+                tt(A("gg", a, b), A("u2", a, b), A("n2g", a, b), ALU.max)
+            for p in pairs:
+                for a, b in p:
+                    tt(A("sp", a, a + Q), A("gg", b, b + Q), A("gg", a, a + Q), ALU.subtract)
             for a, b in parts:
-                if HOP2_S:
-                    tt(A("uu", a, b), A("u1", a, b), A("n2g", a, b), ALU.add)
-                else:
-                    tt(A("uu", a, b), IND(CW, L("mu", 20, a, b)), A("u1", a, b), ALU.add)
+                act(A("n3g", a, b), IND(GW, L("mu", 20, a, b)))
+                tt(A("k1", a, b), IND(GW, L("mu", 0, a, b)), A("sp", a, b), ALU.add)
+                tt(A("kw", a, b), A("k1", a, b), A("n3g", a, b), ALU.add)
             for a, b in parts:
-                ts(A("gg", a, b), A("uu", a, b), 1.0, ALU.min, 1.0, ALU.add)
-                ts(A("g2", a, b), A("uu", a, b), 1.0, ALU.min, 1.0, ALU.add)
-            ride()
-            if HOP3_S:
-                for a, b in strap:
-                    act(A("n2g", a, b), IND(GW, L("mu", 20, a, b)))
-            tt(A("k1", S, C), IND(GW, A("mu", 10, 20)), A("g2", 0, S), ALU.mult)
-            tt(A("k1", 0, S), IND(GW, A("mu", 0, 10)), A("g2", S, C), ALU.mult)
-            for a, b in strap:
-                if HOP3_S:
-                    tt(A("kw", a, b), A("k1", a, b), A("n2g", a, b), ALU.mult)
+                if a == 0 and HI0 == "s":
+                    act(A("kw", C + a, C + b), A("kw", a, b), bias=0.5)
                 else:
-                    tt(A("kw", a, b), IND(GW, L("mu", 20, a, b)), A("k1", a, b), ALU.mult)
-            for a, b in strap:
-                ts(A("kw", C + a, C + b), A("kw", a, b), 0.5, ALU.mult)
-                ts(A("lo2", a, b), A("kw", a, b), 0.5, ALU.mult)
-            ride()
-            act(A("sh", S, C), IND(KW, A("lu", 20, 30)))
-            for a, b in strap:
-                act(A("a3", a, b), IND(KW, L("lu", 40, a, b)), scale=-1.0, bias=1.25)
-            back()
-            for a, b in strap:
-                tt(A("a1", a, b), IND(KW, L("lu", 0, a, b)), A("lo2", a, b), ALU.subtract)
-            tt(A("a2", S, C), IND(KW, A("lu", 30, 40)), A("a1", S, C), ALU.add)
-            tt(A("a2", 0, S), A("sh", S, C), A("a1", 0, S), ALU.add)
-            if HOP1_S:
-                for a, b in strap:
-                    tt(A("cc", a, b), A("a2", a, b), A("a3", a, b), ALU.is_lt)
-            else:
-                for a, b in parts:
-                    tt(A("a3", a, b), IND(KW, L("lu", 40, a, b)), A("a2", a, b), ALU.add)
-                for a, b in parts:
-                    ts(A("cc", a, b), A("a3", a, b), 1.25, ALU.is_lt)
-        ride(99)
-        back(99)
+                    ts(A("kw", C + a, C + b), A("kw", a, b), 0.5, ALU.add)
+            for p in pairs:
+                for a, b in p:
+                    tt(A("a1", a, a + Q), A("kw", b, b + Q), A("ee", a, a + Q), ALU.add)
+            for a, b in parts:
+                act(A("a3", a, b), IND(KW, L("lu", 20, a, b)))
+                tt(A("a2", a, b), IND(KW, L("lu", 0, a, b)), A("a1", a, b), ALU.max)
+                tt(A("u1", a, b), A("a2", a, b), A("a3", a, b), ALU.max)
+                tt(A("cc", a, b), A("u1", a, b), A("kw", a, b), ALU.is_le)
+            if sw < SWEEPS - 1:
+                for h, p in enumerate(pairs):
+                    for a, b in p:
+                        if h == 0 and CC0 == "s":
+                            act(A("c2", a, a + Q), A("cc", b, b + Q))
+                        elif h == 0 and CC0 == "t":
+                            cp(A("c2", a, a + Q), A("cc", b, b + Q))
+                        else:
+                            tt(A("c2", a, a + Q), A("u1", b, b + Q), A("kw", b, b + Q), ALU.is_le)
 
         ts(A("ci", 0, S), IND(CW, L("posu", 0, 0, S)), 1.0, ALU.add)
         act(A("ci", S, C), IND(CW, L("posu", 0, S, C)), bias=1.0)
-        scan(A("ci", C, C + S), A("mone", 0, S), A("ci", 0, S), 1.0, ALU.add, ALU.add)
-        pick(A("ex", 0, C), A("ci", 0, C), C)
-        last_a = A("ci", C + S - 1, C + S)
-        add("v", lambda: g.vector.tensor_tensor_scan(T.ci[:, C + S:2 * C], T.mone[:, 0:S], T.ci[:, S:C], last_a[0], ALU.add, ALU.add),
-            [A("ci", C + S, 2 * C)], [A("mone", 0, S), A("ci", S, C), last_a])
-        pick(A("ex", C, C + S), A("ci", C, C + S), S)
-        tt(A("t40", 0, 20), w16("ex", 0, 20), A("k2", 0, 20), ALU.mult)
-        pick(A("ex", C + S, 2 * C), A("ci", C + S, 2 * C), S)
-        tt(A("t40", 20, 40), A("k3", 0, 20), A("t40", 0, 20), ALU.subtract)
-        tt(A("t20", 0, 20), w16("ex", 20, 40), A("t40", 20, 40), ALU.add)
-        ts(A("destu", 0, 20), A("t20", 0, 20), SCL, ALU.mult)
-        ts(A("t41", 0, 20), A("t20", 0, 20), SCL, ALU.mult, float(S), ALU.is_lt)
+        scan(A("ci", C, 2 * C), A("mone", 0, C), A("ci", 0, C), 1.0, ALU.add, ALU.add)
+        pick(A("exs", 0, C), A("ci", 0, C))
+        pick(A("exs", C, 2 * C), A("ci", C, 2 * C))
+        tt(A("t40", 0, 20), w16("exs", 0, 20), K2, ALU.mult)
+        tt(A("t40", 20, 40), K3, A("t40", 0, 20), ALU.subtract)
+        tt(T20, w16("exs", 20, 40), A("t40", 20, 40), ALU.add)
+        ts(A("destu", 0, 20), T20, SCL, ALU.mult)
         scatter(A("win", 0, WW), A("destu", 0, 20), A("iota", 1, C + 1))
-        act(A("x1", 0, C), IND(A("tabx", 0, WW), A("destu", 0, 20)))
-        act(A("x1g", 0, C), IND(A("x1", 0, C), A("nu", 0, 20)))
-        act(A("x1g", C, 2 * C), IND(A("x1", 0, C), A("nu", 20, 40)))
-        ts(A("t41", 20, 40), A("t20", 0, 20), SCL, ALU.mult, 1.0, ALU.add)
-        ts(A("t41", 40, 60), A("t41", 0, 20), 8192.0, ALU.mult)
-        pick(A("exf", 0, S), A("win", 0, S), S)
-        tt(A("xn", 0, 20), A("t41", 0, 20), A("t41", 20, 40), ALU.mult)
-        tt(A("tf", 0, 20), A("t41", 40, 60), A("own", 0, 20), ALU.add)
+        pick(A("exf", 0, S), A("win", 0, S))
         ts(A("cposu", 0, 10), w16("exf", 0, 10), SCL, ALU.mult, -1.0, ALU.add)
         CP = A("cposu", 0, 10)
-        pick(A("ex", 0, 2 * C), A("x1g", 0, 2 * C), 2 * C)
         for b in range(4):
-            act(A("e2", S * b, S * b + S), IND(A("f2", FW * b, FW * b + C + 1), CP))
-            tt(A("et", b, 4 * S, 4), IND(A("fn", FW * b, FW * b + C + 1), CP), A("e2", S * b, S * b + S), ALU.add)
+            take("vsvs"[b], A("et", b, 4 * S, 4), IND(A("f2", FW * b, FW * b + C + 1), CP))
         qe, se, lq, ls = "qe%d" % r, "se%d" % r, "lq%d" % r, "ls%d" % r
-        act(A("x1g", 2 * C, 3 * C), IND(A("x1", 0, C), A("nu", 40, 60)))
-        ts(A("xn", 20, 60), w16("ex", 0, 40), SCL, ALU.mult, -1.0, ALU.add)
         quant(A(qe, 0, S), A(se, 0, S), A("et", 0, 4 * S))
         arr = T.sem["arr%d" % r]
         add("g", (lambda qe, lq, arr: lambda: g.remote_dma(T[lq][:, 0:S].bitcast(dt.uint8), T[qe][:, 0:S].bitcast(dt.uint8), arr, T.sem.sent, pid, rid, omask))(qe, lq, arr),
-            [], [A(qe, 0, S)], sem="remote")
+            [], [A(qe, 0, S)], 100.0, sem="remote")
         add("g", (lambda se, ls, arr: lambda: g.remote_dma(T[ls][:, 0:S], T[se][:, 0:S], arr, T.sem.sent, pid, rid, omask))(se, ls, arr),
-            [], [A(se, 0, S)], sem="remote")
-        add("far", None, [A(lq, 0, S), A(ls, 0, S)], [], sem="arr%d" % r, n=2 * n_in)
+            [], [A(se, 0, S)], 100.0, sem="remote")
+        add("far", None, [A(lq, 0, S), A(ls, 0, S)], [A(qe, 0, S)], TRIP, sem="arr%d" % r, n=2 * n_in)
 
-        S1, FQ, S2 = A("s12u", 0, 20), A("s12u", 20, 40), A("mnu", 0, 20)
-        pick(A("ex", 2 * C, 3 * C), A("x1g", 2 * C, 3 * C), C)
-        ts(A("cz", 0, 60), A("xn", 0, 60), 0.0, ALU.is_gt)
-        tt(A("tp", 0, 60), A("xn", 0, 60), A("wp", 0, 60), ALU.add)
-        ts(A("xn", 60, 80), w16("ex", 40, 60), SCL, ALU.mult, -1.0, ALU.add)
-        ts(A("l2", 0, 40), A("xn", 20, 60), 0.0, ALU.is_le)
-        tt(A("tp", 0, 60), A("tp", 0, 60), A("cz", 0, 60), ALU.mult)
-        ts(A("l2", 40, 60), A("xn", 60, 80), 0.0, ALU.is_le)
-        ts(A("cz", 60, 80), A("xn", 60, 80), 0.0, ALU.is_gt)
-        tt(A("tp", 60, 80), A("xn", 60, 80), A("wp", 60, 80), ALU.add)
-        tt(A("tf", 20, 80), A("wm", 20, 80), A("l2", 0, 60), ALU.mult)
-        tt(A("tp", 60, 80), A("tp", 60, 80), A("cz", 60, 80), ALU.mult)
-        tt(A("t41", 0, 40), A("tf", 0, 40), A("tf", 40, 80), ALU.max)
-        tt(A("t40", 0, 40), A("tp", 0, 40), A("tp", 40, 80), ALU.max)
-        tt(A("mi", 20, 40), A("t41", 0, 20), A("t41", 20, 40), ALU.max)
-        tt(A("mi", 0, 20), A("t40", 0, 20), A("t40", 20, 40), ALU.max)
-        ts(A("mj", 20, 40), A("mi", 20, 40), 1023, ALU.bitwise_and)
-        ts(A("mj", 0, 20), A("mi", 0, 20), 1023, ALU.bitwise_and)
-        cp(FQ, A("mj", 20, 40))
-        cp(S1, A("mj", 0, 20))
-        ts(A("r1", 0, S), IND(IO, L("s12u", 0, 0, S)), 1.0, ALU.add)
-        act(A("r1", S, C), IND(IO, L("s12u", 0, S, C)), bias=1.0)
-        cp(A("r2", 0, S), IND(A("r1", 0, C), L("s12u", 20, 0, S)))
-        act(A("r2", S, C), IND(A("r1", 0, C), L("s12u", 20, S, C)))
+        S1, FQ, S2 = A("s1u", 0, 20), A("fqu", 0, 20), A("s2u", 0, 20)
+        act(A("c0", 0, C), A("ci", 0, C), bias=-1.0)
         for a, b in parts:
-            pick(A("ex", a, b), A("r2", a, b), b - a)
+            tt(A("x1", a, b), A("ci", C + a, C + b), A("c0", a, b), ALU.mult)
+        act(A("x1g", 0, C), A("x1", 0, C), scale=P15, bias=P15)
+        for k in range(3):
+            act(A("x1g", C * k + C, C * k + 2 * C), IND(A("x1", 0, C), A("nu", 20 * k, 20 * k + 20)), scale=P15, bias=P15)
+        for k in range(4):
+            a, b = 20 * k, 20 * k + 20
+            pick(A("ex", C * k, C * k + C), A("x1g", C * k, C * k + C))
+            ts(A("cz", a, b), w16("ex", a, b), 1.5 * BIG, ALU.is_gt, SURE, ALU.mult)
+            tt(A("tq", a, b), w16("ex", a, b), A("wp", a, b), ALU.add)
+            tt(A("tp", a, b), A("tq", a, b), A("cz", a, b), ALU.add)
+            if k == 0:
+                tt(A("tf", a, b), OWNB, A("cz", a, b), ALU.add)
+            else:
+                tt(A("tf", a, b), A("wm", a, b), A("cz", a, b), ALU.subtract)
+        for k, (nm, tmp, out) in enumerate((("tp", "t40", S1), ("tf", "t41", FQ))):
+            a, b = 40 + 20 * k, 60 + 20 * k
+            tt(A(tmp, 0, 20), A(nm, 0, 20), A(nm, 20, 40), ALU.max)
+            tt(A(tmp, 20, 40), A(tmp, 0, 20), A(nm, 40, 60), ALU.max)
+            tt(A("mi", a, b), A(tmp, 20, 40), A(nm, 60, 80), ALU.max)
+            ts(A("mj", a, b), A("mi", a, b), 9, ALU.logical_shift_right, int(BIG) - 1, ALU.bitwise_and)
+            cp(out, A("mj", a, b))
+        for q, (a, b) in zip("vs", parts):
+            take(q, A("r1", a, b), IND(IO, L("s1u", 0, a, b)))
+        for q, (a, b) in zip("vs", parts):
+            take(q, A("r2", a, b), IND(A("r1", 0, C), L("fqu", 0, a, b)))
         for a, b in parts:
-            ts(A("mnu", a // 16, b // 16), w16("ex", a // 16, b // 16), SCL, ALU.mult, -1.0, ALU.add)
+            pick(A("exs", a, b), A("r2", a, b))
+            ts(L("s2u", 0, a, b), w16("exs", a // 16, b // 16), SCL, ALU.mult)
 
-        for b in range(4):
-            mm(A("ph", 512 * b, 512 * b + S), A("qw", 128 * b, 128 * b + 128), A("sw", 128 * b, 128 * b + 128), A(lq, 0, S), A(ls, 0, S))
-        for b in range(4):
-            ts(A("hh", HW * b + 1, HW * b + S + 1), A("ph", 512 * b, 512 * b + S), 2.0 ** -6, ALU.mult)
-        for lo, hi in parts:
-            act(A("t2", lo, hi), IND(A("hh", 0, S + 1), L("s12u", 0, lo, hi)))
-        for b in range(1, 4):
-            act(A("t2", C * b, C * b + C), IND(A("hh", HW * b, HW * b + S + 1), S1))
-        act(A("a1", 0, C), IND(A("hh", HW * 3, HW * 3 + S + 1), S2))
-        for b in range(5):
-            if b == 3:
-                tt(A("xa", 2, 4 * C, 4), A("pd", 1024, 1024 + C), A("tt", 2 * C, 3 * C), ALU.add)
-                for lo, hi in ((0, S), (S, C)):
-                    tt(A("tt", C * b + lo, C * b + hi), A("a1", lo, hi), A("t2", C * b + lo, C * b + hi), ALU.add)
-                continue
-            if b == 0:
-                for lo, hi in parts:
-                    tt(A("tt", lo, hi), IND(A("hh", 0, S + 1), L("mnu", 0, lo, hi)), A("t2", lo, hi), ALU.add)
-            elif b < 3:
-                tt(A("tt", C * b, C * b + C), IND(A("hh", HW * b, HW * b + S + 1), S2), A("t2", C * b, C * b + C), ALU.add)
-            if b > 0:
-                a = b - 1
-                for lo, hi in ([(0, C)] if a < 3 else [(0, S), (S, C)]):
-                    tt(A("xa", 4 * lo + a, 4 * hi, 4), A("pd", 512 * a + lo, 512 * a + hi), A("tt", C * a + lo, C * a + hi), ALU.add)
+        for p in range(4):
+            mm(A("ph", 512 * p, 512 * p + S), A("qw", 128 * p, 128 * p + 128), A("sw", 128 * p, 128 * p + 128), A(lq, 0, S), A(ls, 0, S))
+            h, src = A("hh", HW * p + 3, HW * p + S + 3), A("ph", 512 * p, 512 * p + S)
+            if HH_ON[p] == "v":
+                ts(h, src, 2.0 ** -6, ALU.mult)
+            else:
+                act(h, src, scale=2.0 ** -6)
+            HP = A("hh", HW * p, HW * p + S + 3)
+            for q, (a, b) in zip(Q_ON[p], parts):
+                t2, t3, t = (A(nm, C * p + a, C * p + b) for nm in ("t2", "t3", "tt"))
+                act(t2, IND(HP, L("s1u", 0, a, b)))
+                if q == "v":
+                    tt(t, IND(HP, L("s2u", 0, a, b)), t2, ALU.add)
+                else:
+                    act(t3, IND(HP, L("s2u", 0, a, b)))
+                    tt(t, t3, t2, ALU.add)
+                tt(A("xa", 4 * a + p, 4 * b, 4), A("pd", 512 * p + a, 512 * p + b), t, ALU.add)
         if last:
-            act(A("tabp", 1, S + 1), IND(A("iota", 0, C + 1), CP))
-            act(A("prep", 0, C), IND(A("tabp", 0, S + 1), S1))
-            dma("s", T.op[:], T.prep[0:128:16, 0:C], [], [A("prep", 0, C)])
-        quant(A("qx", 0, S), A("sx", 0, S), A("xa", 0, 4 * S))
-        quant(A("qx", S, C), A("sx", S, C), A("xa", 4 * S, 4 * C))
+            act(A("tabp", 3, S + 3), IND(A("iota", 0, C + 1), CP))
+            act(A("prep", 0, C), IND(A("tabp", 0, S + 3), S1))
+            dma("y", T.op[:], T.prep[0:128:16, 0:C], [], [A("prep", 0, C)])
+        for a, b in parts:
+            quant(A("qx", a, b), A("sx", a, b), A("xa", 4 * a, 4 * b))
 
-    dma("y", T.oc[:], T.qx[:, 0:C].bitcast(dt.uint8), [], [QX])
+    dma("y", T.oc[:], T.qx[:, 0:C].bitcast(dt.uint8), [], [QX], 1000.0)
     mm(A("ph", 0, S), A("qv", 0, 128), A("sv", 0, 128), A("qx", 0, S), A("sx", 0, S))
     mm(A("ph", 512, 512 + S), A("qv", 0, 128), A("sv", 0, 128), A("qx", S, C), A("sx", S, C))
     for k in range(4):
         dma("y" if k % 2 else "s", T.osc[4 * k:4 * k + 4, :], T.sx[32 * k:32 * k + 4, 0:C], [], [SX])
-    cp(A("yo", 0, S), A("ph", 0, S))
-    act(A("yo", S, C), A("ph", 512, 512 + S))
-    dma("y", T.y[:, 0:S], T.yo[:, 0:S], [], [A("yo", 0, S)])
-    dma("s", T.y[:, S:C], T.yo[:, S:C], [], [A("yo", S, C)])
+    act(A("yo", 0, S), A("ph", 0, S))
+    cp(A("yo", S, C), A("ph", 512, 512 + S))
+    dma("s", T.y[:, 0:S], T.yo[:, 0:S], [], [A("yo", 0, S)])
+    dma("y", T.y[:, S:C], T.yo[:, S:C], [], [A("yo", S, C)])
 
     seen = {}
     for i, o in enumerate(ops):
         deps = set()
         for kind, keys in (("r", o["r"]), ("w", o["w"])):
-            for (nm, a, b) in keys:
+            for (nm, a, b, st) in keys:
                 ps = SCRATCH[nm][0] == "psum"
-                for (j, kj, aj, bj) in seen.get(nm, []):
-                    if j == i or aj >= b or a >= bj:
+                for (j, kj, aj, bj, sj) in seen.get(nm, []):
+                    if j == i or aj >= b or a >= bj or (st == sj and (a - aj) % st):
                         continue
-                    e = ops[j]
-                    if e["q"] == o["q"] and e["sem"] is None and o["sem"] is None:
-                        need = (kj == "w" or kind == "w") and not (kj == kind and nm in ("et", "xa"))
-                    else:
-                        need = kj == "w" or kind == "w" or ps
-                    if need and e["sem"] != "remote":
+                    if (kj == "w" or kind == "w" or (ps and ops[j]["q"] != o["q"])) and ops[j]["sem"] != "remote":
                         deps.add(j)
         for kind, keys in (("r", o["r"]), ("w", o["w"])):
-            for (nm, a, b) in keys:
-                seen.setdefault(nm, []).append((i, kind, a, b))
-        best = {}
-        for j in deps:
-            k = ops[j]["sem"] or ops[j]["q"]
-            best[k] = max(best.get(k, -1), j)
-        o["deps"] = sorted(best.values())
-    waited = {}
-    for o in ops:
-        keep = []
+            for (nm, a, b, st) in keys:
+                if kind == "w" and st == 1:
+                    seen[nm] = [e for e in seen.get(nm, []) if not (a <= e[2] and e[3] <= b)]
+                seen.setdefault(nm, []).append((i, kind, a, b, st))
+        o["deps"] = deps
+
+    for i in reversed(range(len(ops))):
+        o = ops[i]
+        o["tail"] = o.get("tail", 0.0) + o["ns"] + o["late"]
         for j in o["deps"]:
-            k = (o["q"], ops[j]["sem"] or ops[j]["q"])
-            if waited.get(k, -1) < j:
-                waited[k] = j
+            ops[j]["tail"] = max(ops[j].get("tail", 0.0), o["tail"] + WAKE)
+    lanes_of = {}
+    for i in sorted(range(len(ops)), key=lambda i: (-ops[i]["tail"], i)):
+        o = ops[i]
+        t = max([ops[j]["end"] + WAKE for j in o["deps"]] + [0.0])
+        line = lanes_of.setdefault(o["q"], [])
+        k = 0
+        while k < len(line) and ops[line[k]]["at0"] < t + o["ns"] - FIT:
+            t = max(t, ops[line[k]]["at0"] + ops[line[k]]["ns"])
+            k += 1
+        line.insert(k, i)
+        o["at0"], o["end"] = t, t + o["ns"] + o["late"]
+    order = sorted(range(len(ops)), key=lambda i: (ops[i]["at0"], i))
+    place = {i: k for k, i in enumerate(order)}
+
+    waited = {}
+    for i in order:
+        o, best, keep = ops[i], {}, []
+        for j in o["deps"]:
+            k = ops[j]["sem"] or ops[j]["q"]
+            if k not in best or place[j] > place[best[k]]:
+                best[k] = j
+        for k, j in sorted(best.items()):
+            if o["fn"] is not None and waited.get((o["q"], k), -1) < place[j]:
+                waited[(o["q"], k)] = place[j]
                 keep.append(j)
                 ops[j]["used"] = True
         o["deps"] = keep
     qsem = {"v": "cv", "s": "cs", "t": "ct", "g": "cg"}
     eng = {"v": g.vector, "s": g.scalar, "t": g.tensor, "g": g, "y": g.sync}
     count = {}
-    for o in ops:
+    for i in order:
+        o = ops[i]
         if o["sem"] is None:
             o["sn"] = qsem[o["q"]]
             if o["used"]:
@@ -570,7 +539,8 @@ def rank_program(g, core, T, topo):
             o["at"] = count.get(o["sn"], 0)
         else:
             o["sn"], o["at"] = o["sem"], o["n"]
-    for o in ops:
+    for i in order:
+        o = ops[i]
         if o["fn"] is None:
             continue
         for j in o["deps"]:

@@ -8,11 +8,22 @@ BIG = 512.0
 TINY = 2.0 ** -110
 RANK = 2 ** 18
 OWN, SURE = 2.0 ** 20, 2.0 ** 21
-WAKE, LOAD, TRIP = 185.0, 2000.0, 3500.0
-HH_ON = "vvss"
-Q_ON = ("vv", "vv", "vv", "ss")
-HI0, CC0 = "s", "d"
-FIT = 20.0
+WAKE, LOAD, TRIP = 185.0, 2000.0, 1400.0
+XP = 192
+LANES = 8
+EDGE, SO = 0, 45.0
+PQ_CUT = ((20, 60), (60, 80))
+R_ON = ("vs", "vs")
+WIN_CUT = ((0, 20),)
+OWN_CUT = ((0, 64), (64, 160), (160, 320))
+CI_CUT = ((0, 160), (160, 320))
+AHEAD = 300.0
+SCORE_ON = ([("s", 0, S), ("v", S, C)], [("s", 0, S), ("v", S, C)], [("s", 0, S), ("s", S, C)])
+HH_ON = "vvvv"
+P_ON = ("vs", "s", "s", "ss")
+Q_ON = ("gg", "g", "z", "zz")
+HI0, CC, OWN_ON, S0_ON = "s", "vddd", "v", "s"
+FIT, PASSES = 20.0, 4
 
 F32, B16, I32, U16, Q8, U8 = "float32", "bfloat16", "int32", "uint16", "float8_e4m3fn_x4", "uint8"
 WIDTH = {F32: 4, B16: 2, I32: 4, U16: 2, Q8: 4, U8: 1}
@@ -27,9 +38,10 @@ def _sb(names, n, d):
 _sb("xin xa", 4 * C, B16)
 _sb("uin vin", 512, B16)
 _sb("eb", 2048, B16)
-_sb("one", 512, B16)
-_sb("mone isa inc jm nmask e1", C, B16)
-_sb("mask keep mx", 2 * C, B16)
+_sb("isa inc mx mz keep", C, B16)
+_sb("m16", 96, B16)
+_sb("one", 2 * C, B16)
+_sb("mask", 3 * C, B16)
 _sb("x1g ex", 4 * C, B16)
 _sb("qx", C, Q8)
 _sb("sx", C, U8)
@@ -47,17 +59,19 @@ _sb("nu lu sl mu", 64, U16)
 _sb("upk mnu posu cu eu ou destu cposu topu s1u fqu s2u", 32, U16)
 _sb("iota pi1 pos1", FW, F32)
 _sb("nrep posn gp exf", 2 * C, F32)
-_sb("sc prep yo", C, F32)
-_sb("sg sgx", 3 * C, F32)
+_sb("prep yo", C, F32)
+_sb("sc sg sgx", 3 * C, F32)
 WW = 656
 _sb("win", WW, F32)
-_sb("tabp", HW, F32)
-_sb("pc", 8, F32)
+_sb("tabp", FW, F32)
+_sb("pc trip", 8, F32)
 _sb("nw cz wm tp tq tf kk sm", 80, F32)
-_sb("eo ww kc", 64, B16)
-_sb("nf mw tau tauo dd bb do l2 t40 t41 s0", 64, F32)
-_sb("kw ci exs", 2 * C, B16)
-_sb("cc gg c2 ee a1 a2 a3 n2g u1 u2 n3g k1 sp x1 c0 r1 r2", C, B16)
+_sb("eo ww kc", 128, B16)
+_sb("nf mw tau tauo dd bb do t40 t41 s0", 64, F32)
+_sb("l2", 100, F32)
+_sb("kw ci exs", 2 * C + 16, B16)
+_sb("cc gg c2 ee a1 a2 a3 n2g u1 u2 n3g k1 sp c0 r1 r2", C, B16)
+_sb("pu", 32, U16)
 _sb("fn f2", 4 * FW, B16)
 _sb("et", 4 * S, B16)
 _sb("hh", 4 * HW, B16)
@@ -65,7 +79,7 @@ _sb("t2 t3 tt", 4 * C, B16)
 SCRATCH["pd"] = ("psum", [128, 2048], F32)
 SCRATCH["ph"] = ("psum", [128, 2048], F32)
 
-SEMAPHORES = ["cv", "cs", "ct", "cg", "sent", "arr0", "arr1", "arr2"] + ["d%d" % _k for _k in range(24)]
+SEMAPHORES = ["cv", "cs", "ct", "cg", "sent", "arr0", "arr1", "arr2"] + ["d%d" % _k for _k in range(36)]
 
 
 def rank_program(g, core, T, topo):
@@ -122,7 +136,7 @@ def rank_program(g, core, T, topo):
         add("v", lambda: g.vector.memset(o[0], c), [o], [], span(o, [o]))
 
     def scan(o, d0, d1, init, op0, op1):
-        add("v", lambda: g.vector.tensor_tensor_scan(o[0], d0[0], d1[0], init, op0, op1), [o], [d0, d1], span(o, [d0, d1]))
+        add("v", lambda: g.vector.tensor_tensor_scan(o[0], d0[0], d1[0], val(init), op0, op1), [o], [d0, d1, init], span(o, [d0, d1]))
 
     def pick(o, d):
         scan(o, A("mx", 0, o[2]), d, 0.0, ALU.mult, ALU.max)
@@ -133,7 +147,7 @@ def rank_program(g, core, T, topo):
     def act(o, a, scale=1.0, bias=0.0):
         f = ACT.Copy if bias == 0.0 else ACT.Identity
         add("s", lambda: g.scalar.activation(o[0], a[0], f, bias=val(bias), scale=val(scale)), [o], [a, scale, bias],
-            65.0 + 1.3 * o[2] if a[5] else 0.83 * max(64.0, o[2]))
+            65.0 + 1.3 * o[2] if a[5] else SO + 0.83 * max(64.0, o[2]))
 
     def take(q, o, a):
         (cp if q == "v" else act)(o, a)
@@ -150,7 +164,7 @@ def rank_program(g, core, T, topo):
     nd = [0]
 
     def dma(q, o, a, outs, ins, more=0.0):
-        e = {"y": g.sync, "s": g.scalar}[q]
+        e = {"y": g.sync, "s": g.scalar, "g": g}[q]
         add(q, lambda: e.dma_start(o, a), outs, ins, 60.0, sem="d%d" % nd[0], n=16, late=LOAD + more)
         nd[0] += 1
 
@@ -160,31 +174,36 @@ def rank_program(g, core, T, topo):
     def L(name, base, a, b):
         return A(name, base + a // 16, base + b // 16)
 
-    PM, SCL, UNS, P15, P15R, HALF = (A("pc", k, k + 1) for k in (0, 2, 3, 4, 5, 6))
+    PM, SCL, UNS, P15, P15R, HOLD, MID = (A("pc", k, k + 1) for k in (0, 2, 3, 4, 5, 6, 7))
     OWNW, K2, K3, OWNB = (A("kk", 20 * k, 20 * k + 20) for k in range(4))
     I16, T20, OFF, T21 = (A("sm", 20 * k, 20 * k + 20) for k in range(4))
-    parts = [(0, S), (S, C)]
+    parts, xparts, thirds = [(0, S), (S, C)], [(0, XP), (XP, C)], [(0, 96), (96, 192), (192, C)]
     pairs = [[(h, h + Q), (h + Q, h)] for h in (0, S)]
     cols = [(a // 16, b // 16) for p in pairs for a, b in p]
 
     for k, t in enumerate((T.n0, T.n1, T.n2)):
-        dma("y", T.nin[:, 20 * k:20 * k + 20], t[:], [A("nin", 20 * k, 20 * k + 20)], [])
-    dma("s", T.xin[:], T.x[:], [A("xin", 0, 4 * C)], [], 1500.0)
-    dma("s", T.uin[:], T.u[:], [A("uin", 0, 512)], [], 600.0)
+        dma("y", T.nin[:, 20 * k:20 * k + 20], t[:], [A("nin", 20 * k, 20 * k + 20)], [], -700.0)
+    dma("s", T.uin[:], T.u[:], [A("uin", 0, 512)], [], 1000.0)
+    dma("s", T.xin[:], T.x[:], [A("xin", 0, 4 * C)], [], 2000.0)
+    ops[-1]["from"] = 60.0
 
     iota(A("pidx", 0, 1), [[1, 1]], 0, 1, False)
     iota(I16, [[16, 20]], 0, 0, True)
     iota(A("iota", 0, FW), [[1, FW]], 0, 0, True)
-    iota(A("jm", 0, C), [[0, 20], [1, 16]], 0, 0, True)
-    fill(A("one", 0, 512), 1.0)
-    for b in range(4):
-        o, i = A("eb", 512 * b, 512 * b + 512), A("one", 0, 512)
-        add("g", (lambda o, i, b: lambda: g.affine_select(o[0], i[0], [[-1, 512]], ALU.is_equal, 0.0, b, 4))(o, i, b), [o], [i], 1020.0)
+    J16, NOT, NXT, MX, ME, MZ = (A("m16", 16 * k, 16 * k + 16) for k in range(6))
+    iota(J16, [[1, 16]], 0, 0, True)
+    fill(A("one", 0, 2 * C), 1.0)
+
+    def select(o, pat, op, base, cm):
+        i = A("one", 0, o[2])
+        add("g", lambda: g.affine_select(o[0], i[0], pat, op, 0.0, base, cm), [o], [i], 170.0 + 1.66 * o[2])
+
+    for k in (0, 1):
+        select(A("eb", 1024 * k, 1024 * k + 514), [[-1, 514]], ALU.is_equal, 2 + k, 4)
+    select(A("keep", 0, C), [[0, 20], [1, 16]], ALU.is_gt, 0, 0)
     ts(A("pidx", 4, 5), A("pidx", 0, 1), 15, ALU.bitwise_and)
-    fill(A("mone", 0, C), -1.0)
     cp(PM, A("pidx", 4, 5))
     cp(A("upk", 0, 8), A("sm", 0, 8))
-    fill(A("wp", 0, 20), int(OWN))
     ts(A("pc", 1, 2), PM, 1.0, ALU.add)
     ts(SCL, PM, 15.0, ALU.is_equal, 1.0 / BIG, ALU.max)
     ts(OWNW, I16, PM, ALU.add)
@@ -192,40 +211,46 @@ def rank_program(g, core, T, topo):
     fill(A("hh", 1, 4 * HW, HW), 0.0)
     ts(UNS, PM, 15.0, ALU.not_equal, BIG, ALU.mult)
     ts(UNS, UNS, 1.0, ALU.max)
-    ts(K3, OWNW, 2.0, ALU.mult, 2.0 * S + 2.0, ALU.add)
-    ts(K3, K3, UNS, ALU.mult)
-    ts(K2, OWNW, S + 2.0, ALU.add)
+    ts(HOLD, PM, 15.0, ALU.not_equal, 128.0, ALU.mult)
+    ts(K2, OWNW, S + 2.0, ALU.add, UNS, ALU.mult)
+    ts(K3, OWNW, S - 1.0, ALU.add, UNS, ALU.mult)
+    ts(T21, K2, HOLD, ALU.mult)
+    tt(K3, K3, T21, ALU.add)
     ts(OWNB, OWNW, BIG, ALU.mult)
-    fill(A("tabp", 1, 2), -1.0)
+    iota(A("tabp", 0, C), [[1, C]], 0, 0, True)
+    fill(A("tabp", C, C + 1), -1.0)
+    fill(A("ci", 2 * C, 2 * C + 1), 1.0)
+    ts(MID, HOLD, 0.5, ALU.add)
     ts(P15, SCL, BIG, ALU.mult)
     ts(P15R, SCL, float(RANK), ALU.mult)
-    ts(HALF, UNS, Q + 0.5, ALU.mult)
-    for k, c in enumerate((3.0, 15.0, 12.0)):
-        fill(A("kc", 20 * k, 20 * k + 20), c)
-    ts(A("nmask", 0, C), A("jm", 0, C), PM, ALU.not_equal)
-    ts(A("e1", 0, C), A("jm", 0, C), A("pc", 1, 2), ALU.is_equal, BIG, ALU.mult)
-    tt(A("mx", 0, C), A("nmask", 0, C), A("e1", 0, C), ALU.max)
-    act(A("mask", 0, C), A("nmask", 0, C), scale=-1.0, bias=1.0)
-    ts(A("keep", 0, C), A("jm", 0, C), 0.0, ALU.not_equal)
-    for nm in ("mask", "keep", "mx"):
-        dma("y", T[nm][:, C:2 * C], T[nm][:, 0:C], [A(nm, C, 2 * C)], [A(nm, 0, C)])
-    dma("y", T.qw[:].bitcast(dt.uint8), T.wc[:], [A("qw", 0, 512)], [])
-    dma("y", T.sw[:], T.ws[:], [A("sw", 0, 512)], [])
-    dma("y", T.vin[:], T.v[:], [A("vin", 0, 512)], [])
+    fill(A("kc", 0, 128), 1.0)
+    for k, c in ((0, 0.0), (64, 0.0), (65, 1.25), (66, 4.0)):
+        fill(A("kc", k, k // 64 * 64 + 60, 3), c)
+    ts(NOT, J16, PM, ALU.not_equal)
+    ts(NXT, J16, A("pc", 1, 2), ALU.is_equal, BIG, ALU.mult)
+    tt(MX, NOT, NXT, ALU.max)
+    ts(ME, J16, PM, ALU.is_equal)
+    ts(MZ, MX, 1.5, ALU.min, -1.0, ALU.add)
+    ts(A("lu", 0, 20), A("one", 0, 20), PM, ALU.mult)
+    act(A("mx", 0, C), IND(MX, A("lu", 0, 20)))
+    act(A("r2", 0, C), IND(ME, A("lu", 0, 20)))
+    act(A("mz", 0, C), IND(MZ, A("lu", 0, 20)), scale=256.0)
     for b in range(4):
-        quant(A("qeb", 128 * b, 128 * b + 128), A("seb", 128 * b, 128 * b + 128), A("eb", 512 * b, 512 * b + 512))
-    quant(A("qv", 0, 128), A("sv", 0, 128), A("vin", 0, 512))
+        a = 1024 * (b % 2) + 2 - b // 2 * 2
+        quant(A("qeb", 128 * b, 128 * b + 128), A("seb", 128 * b, 128 * b + 128), A("eb", a, a + 512))
     quant(A("qu", 0, 128), A("su", 0, 128), A("uin", 0, 512))
     up = A("upk", 0, 8)
     add("v", lambda: g.vector.tensor_copy(T.qup[:, 0:128].bitcast(dt.uint32), T.qu[:, 0:128].bitcast(dt.uint32).indirect(up[0])),
         [A("qup", 0, 128)], [A("qu", 0, 128), up], 220.0)
     add("s", lambda: g.scalar.activation(T.sup[:, 0:128], T.su[:, 0:128].indirect(up[0]), ACT.Copy),
         [A("sup", 0, 128)], [A("su", 0, 128), up], 230.0)
-    quant(A("qx", 0, C), A("sx", 0, C), A("xin", 0, 4 * C))
+    for a, b in parts:
+        quant(A("qx", a, b), A("sx", a, b), A("xin", 4 * a, 4 * b))
 
     IO = A("iota", 0, C)
     act(A("prep", 0, C), IO)
-    cp(A("nu", 0, 60), A("nin", 0, 60))
+    cp(A("nu", 0, 20), A("nin", 0, 20))
+    cp(A("nu", 20, 60), A("nin", 20, 60))
     cp(A("nf", 0, 20), A("nin", 0, 20))
     tt(A("isa", 0, C), IND(IO, A("nu", 0, 20)), A("prep", 0, C), ALU.is_gt)
     act(A("nrep", 0, C), IND(IO, A("nu", 20, 40)), bias=1.0)
@@ -235,42 +260,45 @@ def rank_program(g, core, T, topo):
     ts(A("nf", 0, 60), A("nin", 0, 60), BIG, ALU.mult)
     scan(A("inc", 0, C), A("one", 0, C), A("isa", 0, C), 0.0, ALU.mult, ALU.add)
     cp(A("mnu", 0, 20), T20)
-    for q, (a, b) in zip("vs", parts):
-        take(q, A("c0", a, b), IND(A("inc", 0, C), L("mnu", 0, a, b)))
-    ts(OFF, OFF, float(Q), ALU.mult, -1.0, ALU.add)
+    ts(A("c0", 0, S), IND(A("inc", 0, C), L("mnu", 0, 0, S)), P15, ALU.mult)
+    act(A("c0", S, C), IND(A("inc", 0, C), L("mnu", 0, S, C)), scale=P15)
+    ts(OFF, OFF, Q * BIG, ALU.mult, -BIG, ALU.add)
     pick(A("ex", 0, C), A("c0", 0, C))
-    ts(A("t40", 0, 20), w16("ex", 0, 20), SCL, ALU.mult)
-    ts(A("t40", 20, 40), w16("ex", 0, 20), HALF, ALU.is_gt, float(Q), ALU.mult)
-    tt(A("t41", 0, 20), A("t40", 0, 20), OFF, ALU.add)
-    tt(A("t41", 20, 40), A("t41", 0, 20), A("t40", 20, 40), ALU.add)
-    cp(A("posu", 0, 20), A("t41", 20, 40))
+    tt(A("t40", 0, 20), w16("ex", 0, 20), OFF, ALU.add)
+    ts(A("t40", 20, 40), w16("ex", 0, 20), (Q + 0.5) * BIG, ALU.is_gt, Q * BIG, ALU.mult)
+    tt(A("t41", 0, 20), A("t40", 0, 20), A("t40", 20, 40), ALU.add)
+    ts(A("posu", 0, 20), A("t41", 0, 20), 1.0 / BIG, ALU.mult)
     POS = A("posu", 0, 20)
+    for nm, o, t in (("qw", T.qw[:].bitcast(dt.uint8), T.wc), ("sw", T.sw[:], T.ws), ("vin", T.vin[:], T.v)):
+        dma("y", o, t[:], [A(nm, 0, 512)], [POS], 1500.0)
+    quant(A("qv", 0, 128), A("sv", 0, 128), A("vin", 0, 512))
+    act(A("mask", 0, C), IND(A("r2", 0, C), POS))
+    for k in (1, 2):
+        act(A("mask", C * k, C * k + C), IND(A("mask", 0, C), A("nu", 20 * k, 20 * k + 20)))
     scatter(A("pi1", 0, C), POS, A("iota", 1, C + 1))
     act(A("pos1", 0, C), IND(IO, POS), bias=1.0)
-    act(A("posn", 0, C), IND(A("pos1", 0, C), A("nu", 20, 40)))
-    act(A("posn", C, 2 * C), IND(A("pos1", 0, C), A("nu", 40, 60)))
     pick(A("exf", 0, C), A("pi1", 0, C))
     ts(A("sl", 0, 20), w16("exf", 0, 20), SCL, ALU.mult, -1.0, ALU.add)
     ts(A("nw", 0, 20), w16("exf", 0, 20), SCL, ALU.mult, -1.0, ALU.add)
     PI = A("sl", 0, 20)
     cp(A("gp", 0, C), IND(A("nrep", 0, C), PI))
     act(A("gp", C, 2 * C), IND(A("nrep", C, 2 * C), PI))
-    act(A("win", 0, C), IND(A("posn", 0, C), PI))
-    act(A("win", C, 2 * C), IND(A("posn", C, 2 * C), PI))
     for a, b in cols:
-        cp(A("nw", 20 + a, 25 + a), A("nw", b, b + 5))
+        act(A("nw", 20 + a, 25 + a), A("nw", b, b + 5))
     for k in (0, 1):
         pick(A("posn", C * k, C * k + C), A("gp", C * k, C * k + C))
         ts(A("sl", 20 + 20 * k, 40 + 20 * k), w16("posn", 20 * k, 20 * k + 20), SCL, ALU.mult, -1.0, ALU.add)
     ts(A("nw", 40, 80), w16("posn", 0, 40), SCL, ALU.mult, -1.0, ALU.add)
     for k in (1, 2):
         tt(A("tau", 20 * k, 20 * k + 20), A("nw", 20 * k + 20, 20 * k + 40), A("nw", 0, 20), ALU.subtract)
-        pick(A("exf", C * k - C, C * k), A("win", C * k - C, C * k))
+        act(A("win", C * k - C, C * k), IND(A("pos1", 0, C), A("sl", 20 * k, 20 * k + 20)))
+        for a, b in parts:
+            pick(A("exf", C * k - C + a, C * k - C + b), A("win", C * k - C + a, C * k - C + b))
     ts(A("tau", 20, 60), A("tau", 20, 60), TINY, ALU.mult)
     ts(A("mu", 0, 40), w16("exf", 0, 40), SCL, ALU.mult, -1.0, ALU.add)
     ts(A("mw", 20, 60), A("mu", 0, 40), 1.0 / C, ALU.mult, 1.0, ALU.add)
-    for j, (lo, hi) in enumerate(((1, 2), (1, 3), (2, 3))):
-        tt(A("tauo", 20 * j, 20 * j + 20), A("nw", 20 * hi, 20 * hi + 20), A("nw", 20 * lo, 20 * lo + 20), ALU.subtract)
+    for j, (lo, hi) in enumerate(((1, 3), (2, 3), (1, 2))):
+        tt(A("tauo", j, 60, 3), A("nw", 20 * hi, 20 * hi + 20), A("nw", 20 * lo, 20 * lo + 20), ALU.subtract)
     ts(A("tauo", 0, 60), A("tauo", 0, 60), TINY, ALU.mult)
 
     QX, SX = A("qx", 0, C), A("sx", 0, C)
@@ -279,60 +307,55 @@ def rank_program(g, core, T, topo):
 
     def lanes(src, dst):
         e = topo.engines(src, dst)
-        return e[::max(1, len(e) // 8)]
+        return e[::max(1, len(e) // LANES)]
 
     omask = sum(1 << e for e in lanes(core, nxt))
     n_out, n_in = len(lanes(core, nxt)), len(lanes(prv, core))
 
     for r in range(ROUNDS):
         last = r == ROUNDS - 1
-        if r == 0:
-            mm(A("ph", 0, C), A("qup", 0, 128), A("sup", 0, 128), QX, SX)
-            act(A("sc", 0, C), A("ph", 0, C))
-        else:
-            mm(A("ph", 0, S), A("qup", 0, 128), A("sup", 0, 128), A("qx", 0, S), A("sx", 0, S))
-            mm(A("ph", 512, 512 + S), A("qup", 0, 128), A("sup", 0, 128), A("qx", S, C), A("sx", S, C))
-            act(A("sc", 0, S), A("ph", 0, S))
-            cp(A("sc", S, C), A("ph", 512, 512 + S))
+        for k, (a, b) in enumerate(xparts if r else [(0, C)]):
+            mm(A("ph", 512 * k, 512 * k + b - a), A("qup", 0, 128), A("sup", 0, 128), A("qx", a, b), A("sx", a, b))
+            for j in range(3):
+                tt(A("sc", C * j + a, C * j + b), A("ph", 512 * k, 512 * k + b - a), A("mask", C * j + a, C * j + b), ALU.mult)
         for b in range(4):
             mm(A("pd", 512 * b, 512 * b + C), A("qeb", 128 * b, 128 * b + 128), A("seb", 128 * b, 128 * b + 128), QX, SX)
             act(A("fn", FW * b, FW * b + C), A("pd", 512 * b, 512 * b + C), scale=0.5)
-        tt(A("sg", 0, 2 * C), IND(A("sc", 0, C), A("sl", 0, 40)), A("mask", 0, 2 * C), ALU.mult)
-        tt(A("sg", 2 * C, 3 * C), IND(A("sc", 0, C), A("sl", 40, 60)), A("mask", 0, C), ALU.mult)
-        scan(A("sgx", 0, 2 * C), A("keep", 0, 2 * C), A("sg", 0, 2 * C), 0.0, ALU.mult, ALU.add)
-        scan(A("sgx", 2 * C, 3 * C), A("keep", 0, C), A("sg", 2 * C, 3 * C), 0.0, ALU.mult, ALU.add)
-        for k in (1, 2):
-            tt(A("dd", 20 * k, 20 * k + 20), w16("sgx", 20 * k, 20 * k + 20), w16("sgx", 0, 20), ALU.subtract)
-            tt(A("bb", 20 * k, 20 * k + 20), A("dd", 20 * k, 20 * k + 20), A("tau", 20 * k, 20 * k + 20), ALU.is_lt)
+        for j in range(3):
+            for q, a, b in SCORE_ON[j]:
+                take(q, A("sg", C * j + a, C * j + b), IND(A("sc", C * j, C * j + C), L("sl", 20 * j, a, b)))
+                scan(A("sgx", C * j + a, C * j + b), A("keep", a, b), A("sg", C * j + a, C * j + b), 0.0, ALU.mult, ALU.add)
         for a, b in cols:
-            tt(A("bb", a, a + 5), w16("sgx", a, a + 5), w16("sgx", b, b + 5), ALU.is_ge if a < b else ALU.is_gt)
-            cp(A("s0", a, a + 5), w16("sgx", b, b + 5))
-        tt(T20, A("bb", 0, 20), A("bb", 20, 40), ALU.mult)
-        tt(OFF, T20, A("bb", 40, 60), ALU.mult)
-        cp(A("cu", 0, 20), OFF)
+            tt(A("bb", 3 * a, 3 * a + 15, 3), w16("sgx", a, a + 5), w16("sgx", b, b + 5), ALU.is_ge if a < b else ALU.is_gt)
+            take(S0_ON, A("s0", a, a + 5), w16("sgx", b, b + 5))
+        for a, b in WIN_CUT:
+            for k in (1, 2):
+                tt(A("dd", 20 * k + a, 20 * k + b), w16("sgx", 20 * k + a, 20 * k + b), w16("sgx", a, b), ALU.subtract)
+                tt(A("bb", 3 * a + k, 3 * b, 3), A("dd", 20 * k + a, 20 * k + b), A("tau", 20 * k + a, 20 * k + b), ALU.is_lt)
+            scan(A("l2", 40 + 3 * a, 40 + 3 * b), A("kc", 0, 3 * (b - a)), A("bb", 3 * a, 3 * b), 0.0, ALU.mult, ALU.add)
+            ts(A("cu", a, b), A("l2", 42 + 3 * a, 40 + 3 * b, 3), 2.5, ALU.is_gt)
         for q, (a, b) in zip("vs", parts):
             take(q, A("cc", a, b), IND(IO, L("cu", 0, a, b)))
         for p in pairs:
             for a, b in p:
                 cp(A("c2", a, a + Q), A("cc", b, b + Q))
-        cp(A("eu", 0, 20), A("bb", 0, 20))
+        cp(A("eu", 0, 20), A("bb", 0, 60, 3))
         for a, b in parts:
             act(A("ee", a, b), IND(IO, L("eu", 0, a, b)), scale=-0.5, bias=0.5)
-        tt(A("l2", 0, 40), A("mw", 20, 60), A("bb", 20, 60), ALU.subtract)
+        for k in (1, 2):
+            tt(A("l2", 20 * k - 20, 20 * k), A("mw", 20 * k, 20 * k + 20), A("bb", k, 60, 3), ALU.subtract)
         ts(A("lu", 0, 40), A("l2", 0, 40), float(C), ALU.mult)
         act(A("win", 0, S), A("one", 0, S), scale=float(C + 1))
 
-        tt(A("do", 0, 20), w16("sgx", 20, 40), A("s0", 0, 20), ALU.subtract)
-        tt(A("do", 20, 40), w16("sgx", 40, 60), A("s0", 0, 20), ALU.subtract)
-        tt(A("do", 40, 60), w16("sgx", 40, 60), w16("sgx", 20, 40), ALU.subtract)
+        tt(A("do", 0, 60, 3), w16("sgx", 40, 60), A("s0", 0, 20), ALU.subtract)
+        tt(A("do", 1, 60, 3), w16("sgx", 40, 60), w16("sgx", 20, 40), ALU.subtract)
+        tt(A("do", 2, 60, 3), w16("sgx", 20, 40), A("s0", 0, 20), ALU.subtract)
         tt(A("eo", 0, 60), A("do", 0, 60), A("tauo", 0, 60), ALU.is_lt)
-        tt(A("ww", 0, 60), A("eo", 0, 60), A("kc", 0, 60), ALU.mult)
-        tt(A("s0", 20, 40), A("ww", 0, 20), A("ww", 20, 40), ALU.add)
-        tt(A("s0", 40, 60), A("s0", 20, 40), A("ww", 40, 60), ALU.add)
-        ts(A("ou", 0, 20), A("s0", 40, 60), -1.0, ALU.mult, 57.0, ALU.add)
-        for a, b in parts:
+        scan(A("ww", 0, 60), A("kc", 64, 124), A("eo", 0, 60), 0.0, ALU.mult, ALU.add)
+        ts(A("ou", 0, 20), A("ww", 2, 60, 3), -3.0, ALU.mult, 57.0, ALU.add)
+        for a, b in thirds:
             act(A("r1", a, b), IND(IO, L("ou", 0, a, b)), scale=P15R)
-        for a, b in parts:
+        for a, b in thirds:
             act(A("r2", a, b), IND(A("r1", 0, C), L("posu", 0, a, b)))
         for a, b in parts:
             pick(A("ex", a, b), A("r2", a, b))
@@ -340,17 +363,18 @@ def rank_program(g, core, T, topo):
         ts(A("wp", 20, 40), A("mi", 0, 20), 3 * RANK, ALU.bitwise_and)
         for k in (1, 2):
             ts(A("wp", 20 + 20 * k, 40 + 20 * k), A("mi", 0, 20), 2 * k, ALU.logical_shift_right, 3 * RANK, ALU.bitwise_and)
-        for k in range(3):
-            tt(A("wm", 20 + 20 * k, 40 + 20 * k), A("wp", 20 + 20 * k, 40 + 20 * k), A("nf", 20 * k, 20 * k + 20), ALU.add)
+        tt(A("wm", 20, 80), A("wp", 20, 80), A("nf", 0, 60), ALU.add)
         tt(T21, A("wm", 20, 40), A("wm", 40, 60), ALU.max)
         tt(A("mi", 20, 40), T21, A("wm", 60, 80), ALU.max)
         ts(A("mj", 0, 20), A("mi", 20, 40), 9, ALU.logical_shift_right, int(BIG) - 1, ALU.bitwise_and)
         cp(A("topu", 0, 20), A("mj", 0, 20))
         for p in range(4):
-            for a, b in parts:
+            for a, b in thirds:
                 act(A("f2", FW * p + a, FW * p + b), IND(A("fn", FW * p, FW * p + C), L("topu", 0, a, b)))
-            for a in range(FW * p, FW * p + C, 64):
-                tt(A("f2", a, a + 64), A("f2", a, a + 64), A("fn", a, a + 64), ALU.add)
+            o, i = A("f2", FW * p, FW * p + C), A("fn", FW * p, FW * p + C)
+            add("g", (lambda o, i: lambda: g.dma_start(o[0], i[0], accum_op=ALU.add))(o, i), [o], [o, i], 100.0,
+                sem="d%d" % nd[0], n=16, late=LOAD + 1500.0)
+            nd[0] += 1
 
         for sw in range(1, SWEEPS):
             for a, b in parts:
@@ -376,22 +400,22 @@ def rank_program(g, core, T, topo):
                 act(A("a3", a, b), IND(KW, L("lu", 20, a, b)))
                 tt(A("a2", a, b), IND(KW, L("lu", 0, a, b)), A("a1", a, b), ALU.max)
                 tt(A("u1", a, b), A("a2", a, b), A("a3", a, b), ALU.max)
-                tt(A("cc", a, b), A("u1", a, b), A("kw", a, b), ALU.is_le)
+                if sw < SWEEPS - 1:
+                    tt(A("cc", a, b), A("u1", a, b), A("kw", a, b), ALU.is_le)
             if sw < SWEEPS - 1:
-                for h, p in enumerate(pairs):
-                    for a, b in p:
-                        if h == 0 and CC0 == "s":
-                            act(A("c2", a, a + Q), A("cc", b, b + Q))
-                        elif h == 0 and CC0 == "t":
-                            cp(A("c2", a, a + Q), A("cc", b, b + Q))
-                        else:
-                            tt(A("c2", a, a + Q), A("u1", b, b + Q), A("kw", b, b + Q), ALU.is_le)
+                for q, (a, b) in zip(CC, pairs[0] + pairs[1]):
+                    if q == "d":
+                        tt(A("c2", a, a + Q), A("u1", b, b + Q), A("kw", b, b + Q), ALU.is_le)
+                    else:
+                        take(q, A("c2", a, a + Q), A("cc", b, b + Q))
 
-        ts(A("ci", 0, S), IND(CW, L("posu", 0, 0, S)), 1.0, ALU.add)
-        act(A("ci", S, C), IND(CW, L("posu", 0, S, C)), bias=1.0)
-        scan(A("ci", C, 2 * C), A("mone", 0, C), A("ci", 0, C), 1.0, ALU.add, ALU.add)
-        pick(A("exs", 0, C), A("ci", 0, C))
-        pick(A("exs", C, 2 * C), A("ci", C, 2 * C))
+        for a, b in OWN_CUT:
+            act(A("c0", a, b), IND(A("kw", 0, C), L("posu", 0, a, b)))
+        for a, b in CI_CUT:
+            tt(A("ci", a, b), IND(A("u1", 0, C), L("posu", 0, a, b)), A("c0", a, b), ALU.is_le)
+            scan(A("ci", C + a, C + b), A("one", a, b), A("ci", a, b), A("ci", C + a - 1, C + a) if a else 2.0, ALU.mult, ALU.add)
+            scan(A("exs", a, b), A("mz", a, b), A("ci", a, b), 0.0, ALU.add, ALU.max)
+            pick(A("exs", C + a, C + b), A("ci", C + a, C + b))
         tt(A("t40", 0, 20), w16("exs", 0, 20), K2, ALU.mult)
         tt(A("t40", 20, 40), K3, A("t40", 0, 20), ALU.subtract)
         tt(T20, w16("exs", 20, 40), A("t40", 20, 40), ALU.add)
@@ -409,40 +433,38 @@ def rank_program(g, core, T, topo):
             [], [A(qe, 0, S)], 100.0, sem="remote")
         add("g", (lambda se, ls, arr: lambda: g.remote_dma(T[ls][:, 0:S], T[se][:, 0:S], arr, T.sem.sent, pid, rid, omask))(se, ls, arr),
             [], [A(se, 0, S)], 100.0, sem="remote")
-        add("far", None, [A(lq, 0, S), A(ls, 0, S)], [A(qe, 0, S)], TRIP, sem="arr%d" % r, n=2 * n_in)
+        add("far", None, [A("trip", r, r + 1)], [A(qe, 0, S)], TRIP, sem="trip")
 
-        S1, FQ, S2 = A("s1u", 0, 20), A("fqu", 0, 20), A("s2u", 0, 20)
-        act(A("c0", 0, C), A("ci", 0, C), bias=-1.0)
-        for a, b in parts:
-            tt(A("x1", a, b), A("ci", C + a, C + b), A("c0", a, b), ALU.mult)
-        act(A("x1g", 0, C), A("x1", 0, C), scale=P15, bias=P15)
-        for k in range(3):
-            act(A("x1g", C * k + C, C * k + 2 * C), IND(A("x1", 0, C), A("nu", 20 * k, 20 * k + 20)), scale=P15, bias=P15)
-        for k in range(4):
-            a, b = 20 * k, 20 * k + 20
+        PU, S1, FQ, S2 = A("pu", 0, 20), A("s1u", 0, 20), A("fqu", 0, 20), A("s2u", 0, 20)
+        for k in (1, 2, 3):
+            act(A("x1g", C * k, C * k + C), IND(A("ci", 0, C), A("nu", 20 * k - 20, 20 * k)), scale=P15, bias=P15)
             pick(A("ex", C * k, C * k + C), A("x1g", C * k, C * k + C))
+        ts(A("cz", 0, 20), w16("exs", 0, 20), MID, ALU.is_gt, SURE, ALU.mult)
+        tt(A("tf", 0, 20), OWNB, A("cz", 0, 20), ALU.add)
+        ts(A("tp", 0, 20), A("tf", 0, 20), OWN + C * BIG, ALU.max)
+        for a, b in PQ_CUT:
             ts(A("cz", a, b), w16("ex", a, b), 1.5 * BIG, ALU.is_gt, SURE, ALU.mult)
-            tt(A("tq", a, b), w16("ex", a, b), A("wp", a, b), ALU.add)
-            tt(A("tp", a, b), A("tq", a, b), A("cz", a, b), ALU.add)
-            if k == 0:
-                tt(A("tf", a, b), OWNB, A("cz", a, b), ALU.add)
-            else:
-                tt(A("tf", a, b), A("wm", a, b), A("cz", a, b), ALU.subtract)
-        for k, (nm, tmp, out) in enumerate((("tp", "t40", S1), ("tf", "t41", FQ))):
-            a, b = 40 + 20 * k, 60 + 20 * k
-            tt(A(tmp, 0, 20), A(nm, 0, 20), A(nm, 20, 40), ALU.max)
-            tt(A(tmp, 20, 40), A(tmp, 0, 20), A(nm, 40, 60), ALU.max)
-            tt(A("mi", a, b), A(tmp, 20, 40), A(nm, 60, 80), ALU.max)
-            ts(A("mj", a, b), A("mi", a, b), 9, ALU.logical_shift_right, int(BIG) - 1, ALU.bitwise_and)
-            cp(out, A("mj", a, b))
-        for q, (a, b) in zip("vs", parts):
-            take(q, A("r1", a, b), IND(IO, L("s1u", 0, a, b)))
-        for q, (a, b) in zip("vs", parts):
+            tt(A("tp", a, b), A("wm", a, b), A("cz", a, b), ALU.add)
+            tt(A("tf", a, b), A("wm", a, b), A("cz", a, b), ALU.subtract)
+        for k, nm in enumerate(("tp", "tf")):
+            a = 40 * k
+            tt(A("tq", a, a + 20), A(nm, 0, 20), A(nm, 20, 40), ALU.max)
+            tt(A("tq", a + 20, a + 40), A("tq", a, a + 20), A(nm, 40, 60), ALU.max)
+            tt(A("mi", 40 + 20 * k, 60 + 20 * k), A("tq", a + 20, a + 40), A(nm, 60, 80), ALU.max)
+        ts(A("mj", 40, 80), A("mi", 40, 80), 9, ALU.logical_shift_right, int(BIG) - 1, ALU.bitwise_and)
+        cp(PU, A("mj", 40, 60))
+        cp(FQ, A("mj", 60, 80))
+        for q, (a, b) in zip(R_ON[0], parts):
+            take(q, A("r1", a, b), IND(A("ci", C, 2 * C + 1), L("pu", 0, a, b)))
+        for q, (a, b) in zip(R_ON[1], parts):
             take(q, A("r2", a, b), IND(A("r1", 0, C), L("fqu", 0, a, b)))
-        for a, b in parts:
-            pick(A("exs", a, b), A("r2", a, b))
-            ts(L("s2u", 0, a, b), w16("exs", a // 16, b // 16), SCL, ALU.mult)
+        for src, tmp, out in (("r1", "ex", "s1u"), ("r2", "exs", "s2u")):
+            for a, b in parts:
+                pick(A(tmp, a, b), A(src, a, b))
+            ts(A(out, 0, 20), w16(tmp, 0, 20), SCL, ALU.mult)
 
+        add("far", None, [A(lq, 0, S), A(ls, 0, S)], [A("trip", r, r + 1)] + [S1, FQ, S2][:EDGE], 0.0,
+            sem="arr%d" % r, n=2 * n_in, late=-WAKE)
         for p in range(4):
             mm(A("ph", 512 * p, 512 * p + S), A("qw", 128 * p, 128 * p + 128), A("sw", 128 * p, 128 * p + 128), A(lq, 0, S), A(ls, 0, S))
             h, src = A("hh", HW * p + 3, HW * p + S + 3), A("ph", 512 * p, 512 * p + S)
@@ -451,31 +473,36 @@ def rank_program(g, core, T, topo):
             else:
                 act(h, src, scale=2.0 ** -6)
             HP = A("hh", HW * p, HW * p + S + 3)
-            for q, (a, b) in zip(Q_ON[p], parts):
+            for q, (a, b) in zip(P_ON[p], xparts if len(P_ON[p]) == 2 else [(0, C)]):
+                take(q, A("t2", C * p + a, C * p + b), IND(HP, L("s1u", 0, a, b)))
+            for q, (a, b) in zip(Q_ON[p], xparts if len(Q_ON[p]) == 2 else [(0, C)]):
                 t2, t3, t = (A(nm, C * p + a, C * p + b) for nm in ("t2", "t3", "tt"))
-                act(t2, IND(HP, L("s1u", 0, a, b)))
-                if q == "v":
+                if q == "g":
                     tt(t, IND(HP, L("s2u", 0, a, b)), t2, ALU.add)
-                else:
+                    continue
+                if q == "z":
                     act(t3, IND(HP, L("s2u", 0, a, b)))
-                    tt(t, t3, t2, ALU.add)
-                tt(A("xa", 4 * a + p, 4 * b, 4), A("pd", 512 * p + a, 512 * p + b), t, ALU.add)
+                else:
+                    take(q, t3, IND(A("t2", C * p, C * p + C), L("fqu", 0, a, b)))
+                for lo, hi in xparts:
+                    if a <= lo and hi <= b:
+                        tt(A("tt", C * p + lo, C * p + hi), A("t3", C * p + lo, C * p + hi), A("t2", C * p + lo, C * p + hi), ALU.add)
+            for a, b in xparts:
+                tt(A("xa", 4 * a + p, 4 * b, 4), A("pd", 512 * p + a, 512 * p + b), A("tt", C * p + a, C * p + b), ALU.add)
         if last:
-            act(A("tabp", 3, S + 3), IND(A("iota", 0, C + 1), CP))
-            act(A("prep", 0, C), IND(A("tabp", 0, S + 3), S1))
+            act(A("prep", 0, C), IND(A("tabp", 0, C + 1), PU))
             dma("y", T.op[:], T.prep[0:128:16, 0:C], [], [A("prep", 0, C)])
-        for a, b in parts:
+        for a, b in xparts:
             quant(A("qx", a, b), A("sx", a, b), A("xa", 4 * a, 4 * b))
+            ops[-1]["lead"] = 0.0 if a else AHEAD
 
-    dma("y", T.oc[:], T.qx[:, 0:C].bitcast(dt.uint8), [], [QX], 1000.0)
-    mm(A("ph", 0, S), A("qv", 0, 128), A("sv", 0, 128), A("qx", 0, S), A("sx", 0, S))
-    mm(A("ph", 512, 512 + S), A("qv", 0, 128), A("sv", 0, 128), A("qx", S, C), A("sx", S, C))
+    for k, (a, b) in enumerate(xparts):
+        dma("y", T.oc[:, 4 * a:4 * b], T.qx[:, a:b].bitcast(dt.uint8), [], [A("qx", a, b)], 500.0)
+        mm(A("ph", 512 * k, 512 * k + b - a), A("qv", 0, 128), A("sv", 0, 128), A("qx", a, b), A("sx", a, b))
+        take("sv"[k], A("yo", a, b), A("ph", 512 * k, 512 * k + b - a))
+        dma("sy"[k], T.y[:, a:b], T.yo[:, a:b], [], [A("yo", a, b)], 500.0)
     for k in range(4):
-        dma("y" if k % 2 else "s", T.osc[4 * k:4 * k + 4, :], T.sx[32 * k:32 * k + 4, 0:C], [], [SX])
-    act(A("yo", 0, S), A("ph", 0, S))
-    cp(A("yo", S, C), A("ph", 512, 512 + S))
-    dma("s", T.y[:, 0:S], T.yo[:, 0:S], [], [A("yo", 0, S)])
-    dma("y", T.y[:, S:C], T.yo[:, S:C], [], [A("yo", S, C)])
+        dma("s", T.osc[4 * k:4 * k + 4, :], T.sx[32 * k:32 * k + 4, 0:C], [], [SX])
 
     seen = {}
     for i, o in enumerate(ops):
@@ -495,38 +522,73 @@ def rank_program(g, core, T, topo):
                 seen.setdefault(nm, []).append((i, kind, a, b, st))
         o["deps"] = deps
 
-    for i in reversed(range(len(ops))):
-        o = ops[i]
-        o["tail"] = o.get("tail", 0.0) + o["ns"] + o["late"]
-        for j in o["deps"]:
-            ops[j]["tail"] = max(ops[j].get("tail", 0.0), o["tail"] + WAKE)
-    lanes_of = {}
-    for i in sorted(range(len(ops)), key=lambda i: (-ops[i]["tail"], i)):
-        o = ops[i]
-        t = max([ops[j]["end"] + WAKE for j in o["deps"]] + [0.0])
-        line = lanes_of.setdefault(o["q"], [])
-        k = 0
-        while k < len(line) and ops[line[k]]["at0"] < t + o["ns"] - FIT:
-            t = max(t, ops[line[k]]["at0"] + ops[line[k]]["ns"])
-            k += 1
-        line.insert(k, i)
-        o["at0"], o["end"] = t, t + o["ns"] + o["late"]
-    order = sorted(range(len(ops)), key=lambda i: (ops[i]["at0"], i))
+    every = range(len(ops))
+    ns = [o["ns"] for o in ops]
+    before = [[(j, ops[j]["late"] + WAKE) for j in o["deps"]] for o in ops]
+    after = [[] for o in ops]
+    for i in every:
+        for j, gap in before[i]:
+            after[j].append((i, gap))
+
+    def lay(rank, needs, feeds, first):
+        start, ready, left = [0.0] * len(ops), list(first), [len(n) for n in needs]
+        free, pool = {}, {}
+        for i in every:
+            if not left[i]:
+                pool.setdefault(ops[i]["q"], []).append(i)
+        for _ in every:
+            bids = []
+            for q, line in pool.items():
+                if line:
+                    now = free.get(q, 0.0)
+                    line.sort(key=lambda i: (-rank[i], i))
+                    limit, bid = None, None
+                    for i in line:
+                        t = max(now, ready[i])
+                        if limit is None or t + ns[i] <= limit + FIT:
+                            if bid is None or t < bid[0]:
+                                bid = (t, i)
+                            limit = t if limit is None else min(limit, t)
+                        if t <= now and bid[0] <= now:
+                            break
+                    bids.append(bid)
+            t, i = min(bids)
+            start[i], free[ops[i]["q"]] = t, t + ns[i]
+            pool[ops[i]["q"]].remove(i)
+            for j, gap in feeds[i]:
+                ready[j] = max(ready[j], t + ns[i] + gap)
+                left[j] -= 1
+                if not left[j]:
+                    pool.setdefault(ops[j]["q"], []).append(j)
+        return start
+
+    tail = [0.0] * len(ops)
+    for i in reversed(every):
+        tail[i] = ns[i] + ops[i].get("lead", 0.0) + max([tail[j] + gap for j, gap in after[i]] + [ops[i]["late"]])
+    urge = [[(j, gap + ops[j].get("lead", 0.0)) for j, gap in n] for n in before]
+    found = []
+    for _ in range(PASSES):
+        start = lay(tail, before, after, [o.get("from", 0.0) for o in ops])
+        found.append((max(start[i] + ns[i] + ops[i]["late"] for i in every), len(found), start))
+        back = lay([start[i] + ns[i] for i in every], after, urge, [o["late"] for o in ops])
+        tail = [back[i] + ns[i] for i in every]
+    start = min(found)[2]
+    order = sorted(every, key=lambda i: (start[i], i))
     place = {i: k for k, i in enumerate(order)}
 
-    waited = {}
+    known = {}
     for i in order:
-        o, best, keep = ops[i], {}, []
-        for j in o["deps"]:
+        o, keep = ops[i], []
+        mine = known.setdefault(o["q"], {})
+        for j in sorted(o["deps"], key=lambda j: -place[j]):
             k = ops[j]["sem"] or ops[j]["q"]
-            if k not in best or place[j] > place[best[k]]:
-                best[k] = j
-        for k, j in sorted(best.items()):
-            if o["fn"] is not None and waited.get((o["q"], k), -1) < place[j]:
-                waited[(o["q"], k)] = place[j]
+            if o["fn"] is not None and mine.get(k, -1) < place[j]:
+                mine[k] = place[j]
+                for k2, p2 in ops[j]["knew"].items():
+                    mine[k2] = max(mine.get(k2, -1), p2)
                 keep.append(j)
                 ops[j]["used"] = True
-        o["deps"] = keep
+        o["deps"], o["knew"] = keep, dict(mine)
     qsem = {"v": "cv", "s": "cs", "t": "ct", "g": "cg"}
     eng = {"v": g.vector, "s": g.scalar, "t": g.tensor, "g": g, "y": g.sync}
     count = {}

from concourse.mybir import dt, AluOpType, ActivationFunctionType

ALU = AluOpType
ACT = ActivationFunctionType
C, S, Q, ROUNDS, SWEEPS = 320, 160, 80, 3, 8
FW, HW = 336, 176
BIG = 512.0
TINY = 2.0 ** -110
RANK = 2 ** 18
OWN, SURE = 2.0 ** 20, 2.0 ** 21
WAKE, LOAD, TRIP = 185.0, 2000.0, 1400.0
XP = 192
LANES = 8
EDGE, SO = 0, 45.0
PQ_CUT = ((20, 60), (60, 80))
R_ON = ("vs", "vs")
WIN_CUT = ((0, 20),)
OWN_CUT = ((0, 64), (64, 160), (160, 320))
CI_CUT = ((0, 160), (160, 320))
AHEAD = 300.0
SCORE_ON = ([("s", 0, S), ("v", S, C)], [("s", 0, S), ("v", S, C)], [("s", 0, S), ("s", S, C)])
HH_ON = "vvvv"
P_ON = ("vs", "s", "s", "ss")
Q_ON = ("gg", "g", "z", "zz")
HI0, CC, OWN_ON, S0_ON = "s", "vddd", "v", "s"
FIT, PASSES = 20.0, 4

F32, B16, I32, U16, Q8, U8 = "float32", "bfloat16", "int32", "uint16", "float8_e4m3fn_x4", "uint8"
WIDTH = {F32: 4, B16: 2, I32: 4, U16: 2, Q8: 4, U8: 1}
SCRATCH = {}


def _sb(names, n, d):
    for k in names.split():
        SCRATCH[k] = ("sbuf", [128, n], d)


_sb("xin xa", 4 * C, B16)
_sb("uin vin", 512, B16)
_sb("eb", 2048, B16)
_sb("isa inc mx mz keep", C, B16)
_sb("m16", 96, B16)
_sb("one", 2 * C, B16)
_sb("mask", 3 * C, B16)
_sb("x1g ex", 4 * C, B16)
_sb("qx", C, Q8)
_sb("sx", C, U8)
_sb("qu qv qup", 128, Q8)
_sb("su sv sup", 128, U8)
_sb("qw qeb", 512, Q8)
_sb("sw seb", 512, U8)
for _r in range(ROUNDS):
    _sb("qe%d lq%d" % (_r, _r), S, Q8)
    _sb("se%d ls%d" % (_r, _r), S, U8)
_sb("nin", 64, I32)
_sb("pidx", 8, I32)
_sb("mi mj wp", 80, I32)
_sb("nu lu sl mu", 64, U16)
_sb("upk mnu posu cu eu ou destu cposu topu s1u fqu s2u", 32, U16)
_sb("iota pi1 pos1", FW, F32)
_sb("nrep posn gp exf", 2 * C, F32)
_sb("prep yo", C, F32)
_sb("sc sg sgx", 3 * C, F32)
WW = 656
_sb("win", WW, F32)
_sb("tabp", FW, F32)
_sb("pc trip", 8, F32)
_sb("nw cz wm tp tq tf kk sm", 80, F32)
_sb("eo ww kc", 128, B16)
_sb("nf mw tau tauo dd bb do t40 t41 s0", 64, F32)
_sb("l2", 100, F32)
_sb("kw ci exs", 2 * C + 16, B16)
_sb("cc gg c2 ee a1 a2 a3 n2g u1 u2 n3g k1 sp c0 r1 r2", C, B16)
_sb("pu", 32, U16)
_sb("fn f2", 4 * FW, B16)
_sb("et", 4 * S, B16)
_sb("hh", 4 * HW, B16)
_sb("t2 t3 tt", 4 * C, B16)
SCRATCH["pd"] = ("psum", [128, 2048], F32)
SCRATCH["ph"] = ("psum", [128, 2048], F32)

SEMAPHORES = ["cv", "cs", "ct", "cg", "sent", "arr0", "arr1", "arr2"] + ["d%d" % _k for _k in range(36)]


def rank_program(g, core, T, topo):
    rank = T.rank_of(core)
    if rank is None:
        return
    nr = len(T.cores)
    nxt, prv = T.cores[(rank + 1) % nr], T.cores[(rank - 1) % nr]
    ops = []

    def A(name, a, b, st=1):
        ap = T[name][:, a:b:st] if st != 1 else T[name][:, a:b]
        n, ps = len(range(a, b, st)), SCRATCH[name][0] == "psum"
        if ps:
            a, b = a // 512 * 512, (b + 511) // 512 * 512
        return (ap, [(name, a, b, st)], n, WIDTH[SCRATCH[name][2]], ps, False)

    def IND(w, o):
        return (w[0].indirect(o[0]), w[1] + o[1], 16 * o[2], w[3], False, True)

    def val(x):
        return x[0] if isinstance(x, tuple) else x

    def add(q, fn, outs, ins, ns, sem=None, n=1, late=0.0):
        rd, wr = [], []
        for x in ins:
            if isinstance(x, tuple):
                rd += x[1]
        for x in outs:
            wr += x[1]
        ops.append({"q": q, "fn": fn, "r": rd, "w": wr, "sem": sem, "n": n, "used": False, "ns": ns, "late": late})

    def span(o, full, k=1.0):
        if full[0][5]:
            return 50.0 + 1.3 * o[2]
        return 0.83 * max(64.0, o[2] * k * (0.5 if all(x[3] == 2 for x in full + [o]) else 1.0))

    def tt(o, a, b, op):
        add("v", lambda: g.vector.tensor_tensor(o[0], a[0], b[0], op), [o], [a, b], span(o, [a, b], 1.0 if a[4] else 2.0))

    def ts(o, a, s1, op0, s2=None, op1=None):
        if op1 is None:
            add("v", lambda: g.vector.tensor_scalar(o[0], a[0], val(s1), None, op0), [o], [a, s1], span(o, [a]))
        else:
            add("v", lambda: g.vector.tensor_scalar(o[0], a[0], val(s1), val(s2), op0, op1), [o], [a, s1, s2], span(o, [a]))

    def cp(o, a):
        add("v", lambda: g.vector.tensor_copy(o[0], a[0]), [o], [a], span(o, [a]))

    def scatter(w, off, a):
        add("v", lambda: g.vector.tensor_copy(w[0].indirect(off[0]), a[0]), [w], [a, off], 50.0 + 3.2 * a[2])

    def fill(o, c):
        add("v", lambda: g.vector.memset(o[0], c), [o], [], span(o, [o]))

    def scan(o, d0, d1, init, op0, op1):
        add("v", lambda: g.vector.tensor_tensor_scan(o[0], d0[0], d1[0], val(init), op0, op1), [o], [d0, d1, init], span(o, [d0, d1]))

    def pick(o, d):
        scan(o, A("mx", 0, o[2]), d, 0.0, ALU.mult, ALU.max)

    def quant(q, s, a):
        add("v", lambda: g.vector.quantize_mx(q[0], s[0], a[0]), [q, s], [a], 12.0 + 0.22 * a[2])

    def act(o, a, scale=1.0, bias=0.0):
        f = ACT.Copy if bias == 0.0 else ACT.Identity
        add("s", lambda: g.scalar.activation(o[0], a[0], f, bias=val(bias), scale=val(scale)), [o], [a, scale, bias],
            65.0 + 1.3 * o[2] if a[5] else SO + 0.83 * max(64.0, o[2]))

    def take(q, o, a):
        (cp if q == "v" else act)(o, a)

    def mm(o, wq, ws, xq, xs):
        add("t", lambda: g.tensor.matmul_mx(o[0], wq[0], ws[0], xq[0], xs[0], True, True), [o], [wq, ws, xq, xs], 1.25 * (o[2] + 16))

    def iota(o, pat, base, cm, flag):
        if flag:
            add("g", lambda: g.iota(o[0], pat, base, cm, allow_small_or_imprecise_dtypes=True), [o], [], 130.0 + 1.66 * o[2])
        else:
            add("g", lambda: g.iota(o[0], pat, base, cm), [o], [], 130.0 + 1.66 * o[2])

    nd = [0]

    def dma(q, o, a, outs, ins, more=0.0):
        e = {"y": g.sync, "s": g.scalar, "g": g}[q]
        add(q, lambda: e.dma_start(o, a), outs, ins, 60.0, sem="d%d" % nd[0], n=16, late=LOAD + more)
        nd[0] += 1

    def w16(name, a, b):
        return A(name, 16 * a + 15, 16 * b, 16)

    def L(name, base, a, b):
        return A(name, base + a // 16, base + b // 16)

    PM, SCL, UNS, P15, P15R, HOLD, MID = (A("pc", k, k + 1) for k in (0, 2, 3, 4, 5, 6, 7))
    OWNW, K2, K3, OWNB = (A("kk", 20 * k, 20 * k + 20) for k in range(4))
    I16, T20, OFF, T21 = (A("sm", 20 * k, 20 * k + 20) for k in range(4))
    parts, xparts, thirds = [(0, S), (S, C)], [(0, XP), (XP, C)], [(0, 96), (96, 192), (192, C)]
    pairs = [[(h, h + Q), (h + Q, h)] for h in (0, S)]
    cols = [(a // 16, b // 16) for p in pairs for a, b in p]

    for k, t in enumerate((T.n0, T.n1, T.n2)):
        dma("y", T.nin[:, 20 * k:20 * k + 20], t[:], [A("nin", 20 * k, 20 * k + 20)], [], -700.0)
    dma("s", T.uin[:], T.u[:], [A("uin", 0, 512)], [], 1000.0)
    dma("s", T.xin[:], T.x[:], [A("xin", 0, 4 * C)], [], 2000.0)
    ops[-1]["from"] = 60.0

    iota(A("pidx", 0, 1), [[1, 1]], 0, 1, False)
    iota(I16, [[16, 20]], 0, 0, True)
    iota(A("iota", 0, FW), [[1, FW]], 0, 0, True)
    J16, NOT, NXT, MX, ME, MZ = (A("m16", 16 * k, 16 * k + 16) for k in range(6))
    iota(J16, [[1, 16]], 0, 0, True)
    fill(A("one", 0, 2 * C), 1.0)

    def select(o, pat, op, base, cm):
        i = A("one", 0, o[2])
        add("g", lambda: g.affine_select(o[0], i[0], pat, op, 0.0, base, cm), [o], [i], 170.0 + 1.66 * o[2])

    for k in (0, 1):
        select(A("eb", 1024 * k, 1024 * k + 514), [[-1, 514]], ALU.is_equal, 2 + k, 4)
    select(A("keep", 0, C), [[0, 20], [1, 16]], ALU.is_gt, 0, 0)
    ts(A("pidx", 4, 5), A("pidx", 0, 1), 15, ALU.bitwise_and)
    cp(PM, A("pidx", 4, 5))
    cp(A("upk", 0, 8), A("sm", 0, 8))
    ts(A("pc", 1, 2), PM, 1.0, ALU.add)
    ts(SCL, PM, 15.0, ALU.is_equal, 1.0 / BIG, ALU.max)
    ts(OWNW, I16, PM, ALU.add)
    fill(A("f2", C, 4 * FW, FW), 0.0)
    fill(A("hh", 1, 4 * HW, HW), 0.0)
    ts(UNS, PM, 15.0, ALU.not_equal, BIG, ALU.mult)
    ts(UNS, UNS, 1.0, ALU.max)
    ts(HOLD, PM, 15.0, ALU.not_equal, 128.0, ALU.mult)
    ts(K2, OWNW, S + 2.0, ALU.add, UNS, ALU.mult)
    ts(K3, OWNW, S - 1.0, ALU.add, UNS, ALU.mult)
    ts(T21, K2, HOLD, ALU.mult)
    tt(K3, K3, T21, ALU.add)
    ts(OWNB, OWNW, BIG, ALU.mult)
    iota(A("tabp", 0, C), [[1, C]], 0, 0, True)
    fill(A("tabp", C, C + 1), -1.0)
    fill(A("ci", 2 * C, 2 * C + 1), 1.0)
    ts(MID, HOLD, 0.5, ALU.add)
    ts(P15, SCL, BIG, ALU.mult)
    ts(P15R, SCL, float(RANK), ALU.mult)
    fill(A("kc", 0, 128), 1.0)
    for k, c in ((0, 0.0), (64, 0.0), (65, 1.25), (66, 4.0)):
        fill(A("kc", k, k // 64 * 64 + 60, 3), c)
    ts(NOT, J16, PM, ALU.not_equal)
    ts(NXT, J16, A("pc", 1, 2), ALU.is_equal, BIG, ALU.mult)
    tt(MX, NOT, NXT, ALU.max)
    ts(ME, J16, PM, ALU.is_equal)
    ts(MZ, MX, 1.5, ALU.min, -1.0, ALU.add)
    ts(A("lu", 0, 20), A("one", 0, 20), PM, ALU.mult)
    act(A("mx", 0, C), IND(MX, A("lu", 0, 20)))
    act(A("r2", 0, C), IND(ME, A("lu", 0, 20)))
    act(A("mz", 0, C), IND(MZ, A("lu", 0, 20)), scale=256.0)
    for b in range(4):
        a = 1024 * (b % 2) + 2 - b // 2 * 2
        quant(A("qeb", 128 * b, 128 * b + 128), A("seb", 128 * b, 128 * b + 128), A("eb", a, a + 512))
    quant(A("qu", 0, 128), A("su", 0, 128), A("uin", 0, 512))
    up = A("upk", 0, 8)
    add("v", lambda: g.vector.tensor_copy(T.qup[:, 0:128].bitcast(dt.uint32), T.qu[:, 0:128].bitcast(dt.uint32).indirect(up[0])),
        [A("qup", 0, 128)], [A("qu", 0, 128), up], 220.0)
    add("s", lambda: g.scalar.activation(T.sup[:, 0:128], T.su[:, 0:128].indirect(up[0]), ACT.Copy),
        [A("sup", 0, 128)], [A("su", 0, 128), up], 230.0)
    for a, b in parts:
        quant(A("qx", a, b), A("sx", a, b), A("xin", 4 * a, 4 * b))

    IO = A("iota", 0, C)
    act(A("prep", 0, C), IO)
    cp(A("nu", 0, 20), A("nin", 0, 20))
    cp(A("nu", 20, 60), A("nin", 20, 60))
    cp(A("nf", 0, 20), A("nin", 0, 20))
    tt(A("isa", 0, C), IND(IO, A("nu", 0, 20)), A("prep", 0, C), ALU.is_gt)
    act(A("nrep", 0, C), IND(IO, A("nu", 20, 40)), bias=1.0)
    act(A("nrep", C, 2 * C), IND(IO, A("nu", 40, 60)), bias=1.0)
    tt(T20, OWNW, A("nf", 0, 20), ALU.min)
    tt(OFF, OWNW, A("nf", 0, 20), ALU.is_gt)
    ts(A("nf", 0, 60), A("nin", 0, 60), BIG, ALU.mult)
    scan(A("inc", 0, C), A("one", 0, C), A("isa", 0, C), 0.0, ALU.mult, ALU.add)
    cp(A("mnu", 0, 20), T20)
    ts(A("c0", 0, S), IND(A("inc", 0, C), L("mnu", 0, 0, S)), P15, ALU.mult)
    act(A("c0", S, C), IND(A("inc", 0, C), L("mnu", 0, S, C)), scale=P15)
    ts(OFF, OFF, Q * BIG, ALU.mult, -BIG, ALU.add)
    pick(A("ex", 0, C), A("c0", 0, C))
    tt(A("t40", 0, 20), w16("ex", 0, 20), OFF, ALU.add)
    ts(A("t40", 20, 40), w16("ex", 0, 20), (Q + 0.5) * BIG, ALU.is_gt, Q * BIG, ALU.mult)
    tt(A("t41", 0, 20), A("t40", 0, 20), A("t40", 20, 40), ALU.add)
    ts(A("posu", 0, 20), A("t41", 0, 20), 1.0 / BIG, ALU.mult)
    POS = A("posu", 0, 20)
    for nm, o, t in (("qw", T.qw[:].bitcast(dt.uint8), T.wc), ("sw", T.sw[:], T.ws), ("vin", T.vin[:], T.v)):
        dma("y", o, t[:], [A(nm, 0, 512)], [POS], 1500.0)
    quant(A("qv", 0, 128), A("sv", 0, 128), A("vin", 0, 512))
    act(A("mask", 0, C), IND(A("r2", 0, C), POS))
    for k in (1, 2):
        act(A("mask", C * k, C * k + C), IND(A("mask", 0, C), A("nu", 20 * k, 20 * k + 20)))
    scatter(A("pi1", 0, C), POS, A("iota", 1, C + 1))
    act(A("pos1", 0, C), IND(IO, POS), bias=1.0)
    pick(A("exf", 0, C), A("pi1", 0, C))
    ts(A("sl", 0, 20), w16("exf", 0, 20), SCL, ALU.mult, -1.0, ALU.add)
    ts(A("nw", 0, 20), w16("exf", 0, 20), SCL, ALU.mult, -1.0, ALU.add)
    PI = A("sl", 0, 20)
    cp(A("gp", 0, C), IND(A("nrep", 0, C), PI))
    act(A("gp", C, 2 * C), IND(A("nrep", C, 2 * C), PI))
    for a, b in cols:
        act(A("nw", 20 + a, 25 + a), A("nw", b, b + 5))
    for k in (0, 1):
        pick(A("posn", C * k, C * k + C), A("gp", C * k, C * k + C))
        ts(A("sl", 20 + 20 * k, 40 + 20 * k), w16("posn", 20 * k, 20 * k + 20), SCL, ALU.mult, -1.0, ALU.add)
    ts(A("nw", 40, 80), w16("posn", 0, 40), SCL, ALU.mult, -1.0, ALU.add)
    for k in (1, 2):
        tt(A("tau", 20 * k, 20 * k + 20), A("nw", 20 * k + 20, 20 * k + 40), A("nw", 0, 20), ALU.subtract)
        act(A("win", C * k - C, C * k), IND(A("pos1", 0, C), A("sl", 20 * k, 20 * k + 20)))
        for a, b in parts:
            pick(A("exf", C * k - C + a, C * k - C + b), A("win", C * k - C + a, C * k - C + b))
    ts(A("tau", 20, 60), A("tau", 20, 60), TINY, ALU.mult)
    ts(A("mu", 0, 40), w16("exf", 0, 40), SCL, ALU.mult, -1.0, ALU.add)
    ts(A("mw", 20, 60), A("mu", 0, 40), 1.0 / C, ALU.mult, 1.0, ALU.add)
    for j, (lo, hi) in enumerate(((1, 3), (2, 3), (1, 2))):
        tt(A("tauo", j, 60, 3), A("nw", 20 * hi, 20 * hi + 20), A("nw", 20 * lo, 20 * lo + 20), ALU.subtract)
    ts(A("tauo", 0, 60), A("tauo", 0, 60), TINY, ALU.mult)

    QX, SX = A("qx", 0, C), A("sx", 0, C)
    CW, GW, KW = A("cc", 0, C), A("gg", 0, C), A("kw", 0, 2 * C)
    rid, pid = topo.addr(nxt)[0], topo.addr(nxt)[1]

    def lanes(src, dst):
        e = topo.engines(src, dst)
        return e[::max(1, len(e) // LANES)]

    omask = sum(1 << e for e in lanes(core, nxt))
    n_out, n_in = len(lanes(core, nxt)), len(lanes(prv, core))

    for r in range(ROUNDS):
        last = r == ROUNDS - 1
        for k, (a, b) in enumerate(xparts if r else [(0, C)]):
            mm(A("ph", 512 * k, 512 * k + b - a), A("qup", 0, 128), A("sup", 0, 128), A("qx", a, b), A("sx", a, b))
            for j in range(3):
                tt(A("sc", C * j + a, C * j + b), A("ph", 512 * k, 512 * k + b - a), A("mask", C * j + a, C * j + b), ALU.mult)
        for b in range(4):
            mm(A("pd", 512 * b, 512 * b + C), A("qeb", 128 * b, 128 * b + 128), A("seb", 128 * b, 128 * b + 128), QX, SX)
            act(A("fn", FW * b, FW * b + C), A("pd", 512 * b, 512 * b + C), scale=0.5)
        for j in range(3):
            for q, a, b in SCORE_ON[j]:
                take(q, A("sg", C * j + a, C * j + b), IND(A("sc", C * j, C * j + C), L("sl", 20 * j, a, b)))
                scan(A("sgx", C * j + a, C * j + b), A("keep", a, b), A("sg", C * j + a, C * j + b), 0.0, ALU.mult, ALU.add)
        for a, b in cols:
            tt(A("bb", 3 * a, 3 * a + 15, 3), w16("sgx", a, a + 5), w16("sgx", b, b + 5), ALU.is_ge if a < b else ALU.is_gt)
            take(S0_ON, A("s0", a, a + 5), w16("sgx", b, b + 5))
        for a, b in WIN_CUT:
            for k in (1, 2):
                tt(A("dd", 20 * k + a, 20 * k + b), w16("sgx", 20 * k + a, 20 * k + b), w16("sgx", a, b), ALU.subtract)
                tt(A("bb", 3 * a + k, 3 * b, 3), A("dd", 20 * k + a, 20 * k + b), A("tau", 20 * k + a, 20 * k + b), ALU.is_lt)
            scan(A("l2", 40 + 3 * a, 40 + 3 * b), A("kc", 0, 3 * (b - a)), A("bb", 3 * a, 3 * b), 0.0, ALU.mult, ALU.add)
            ts(A("cu", a, b), A("l2", 42 + 3 * a, 40 + 3 * b, 3), 2.5, ALU.is_gt)
        for q, (a, b) in zip("vs", parts):
            take(q, A("cc", a, b), IND(IO, L("cu", 0, a, b)))
        for p in pairs:
            for a, b in p:
                cp(A("c2", a, a + Q), A("cc", b, b + Q))
        cp(A("eu", 0, 20), A("bb", 0, 60, 3))
        for a, b in parts:
            act(A("ee", a, b), IND(IO, L("eu", 0, a, b)), scale=-0.5, bias=0.5)
        for k in (1, 2):
            tt(A("l2", 20 * k - 20, 20 * k), A("mw", 20 * k, 20 * k + 20), A("bb", k, 60, 3), ALU.subtract)
        ts(A("lu", 0, 40), A("l2", 0, 40), float(C), ALU.mult)
        act(A("win", 0, S), A("one", 0, S), scale=float(C + 1))

        tt(A("do", 0, 60, 3), w16("sgx", 40, 60), A("s0", 0, 20), ALU.subtract)
        tt(A("do", 1, 60, 3), w16("sgx", 40, 60), w16("sgx", 20, 40), ALU.subtract)
        tt(A("do", 2, 60, 3), w16("sgx", 20, 40), A("s0", 0, 20), ALU.subtract)
        tt(A("eo", 0, 60), A("do", 0, 60), A("tauo", 0, 60), ALU.is_lt)
        scan(A("ww", 0, 60), A("kc", 64, 124), A("eo", 0, 60), 0.0, ALU.mult, ALU.add)
        ts(A("ou", 0, 20), A("ww", 2, 60, 3), -3.0, ALU.mult, 57.0, ALU.add)
        for a, b in thirds:
            act(A("r1", a, b), IND(IO, L("ou", 0, a, b)), scale=P15R)
        for a, b in thirds:
            act(A("r2", a, b), IND(A("r1", 0, C), L("posu", 0, a, b)))
        for a, b in parts:
            pick(A("ex", a, b), A("r2", a, b))
        cp(A("mi", 0, 20), w16("ex", 0, 20))
        ts(A("wp", 20, 40), A("mi", 0, 20), 3 * RANK, ALU.bitwise_and)
        for k in (1, 2):
            ts(A("wp", 20 + 20 * k, 40 + 20 * k), A("mi", 0, 20), 2 * k, ALU.logical_shift_right, 3 * RANK, ALU.bitwise_and)
        tt(A("wm", 20, 80), A("wp", 20, 80), A("nf", 0, 60), ALU.add)
        tt(T21, A("wm", 20, 40), A("wm", 40, 60), ALU.max)
        tt(A("mi", 20, 40), T21, A("wm", 60, 80), ALU.max)
        ts(A("mj", 0, 20), A("mi", 20, 40), 9, ALU.logical_shift_right, int(BIG) - 1, ALU.bitwise_and)
        cp(A("topu", 0, 20), A("mj", 0, 20))
        for p in range(4):
            for a, b in thirds:
                act(A("f2", FW * p + a, FW * p + b), IND(A("fn", FW * p, FW * p + C), L("topu", 0, a, b)))
            o, i = A("f2", FW * p, FW * p + C), A("fn", FW * p, FW * p + C)
            add("g", (lambda o, i: lambda: g.dma_start(o[0], i[0], accum_op=ALU.add))(o, i), [o], [o, i], 100.0,
                sem="d%d" % nd[0], n=16, late=LOAD + 1500.0)
            nd[0] += 1

        for sw in range(1, SWEEPS):
            for a, b in parts:
                act(A("n2g", a, b), IND(CW, L("mu", 20, a, b)))
                tt(A("u2", a, b), IND(CW, L("mu", 0, a, b)), A("c2", a, b), ALU.max)
                tt(A("gg", a, b), A("u2", a, b), A("n2g", a, b), ALU.max)
            for p in pairs:
                for a, b in p:
                    tt(A("sp", a, a + Q), A("gg", b, b + Q), A("gg", a, a + Q), ALU.subtract)
            for a, b in parts:
                act(A("n3g", a, b), IND(GW, L("mu", 20, a, b)))
                tt(A("k1", a, b), IND(GW, L("mu", 0, a, b)), A("sp", a, b), ALU.add)
                tt(A("kw", a, b), A("k1", a, b), A("n3g", a, b), ALU.add)
            for a, b in parts:
                if a == 0 and HI0 == "s":
                    act(A("kw", C + a, C + b), A("kw", a, b), bias=0.5)
                else:
                    ts(A("kw", C + a, C + b), A("kw", a, b), 0.5, ALU.add)
            for p in pairs:
                for a, b in p:
                    tt(A("a1", a, a + Q), A("kw", b, b + Q), A("ee", a, a + Q), ALU.add)
            for a, b in parts:
                act(A("a3", a, b), IND(KW, L("lu", 20, a, b)))
                tt(A("a2", a, b), IND(KW, L("lu", 0, a, b)), A("a1", a, b), ALU.max)
                tt(A("u1", a, b), A("a2", a, b), A("a3", a, b), ALU.max)
                if sw < SWEEPS - 1:
                    tt(A("cc", a, b), A("u1", a, b), A("kw", a, b), ALU.is_le)
            if sw < SWEEPS - 1:
                for q, (a, b) in zip(CC, pairs[0] + pairs[1]):
                    if q == "d":
                        tt(A("c2", a, a + Q), A("u1", b, b + Q), A("kw", b, b + Q), ALU.is_le)
                    else:
                        take(q, A("c2", a, a + Q), A("cc", b, b + Q))

        for a, b in OWN_CUT:
            act(A("c0", a, b), IND(A("kw", 0, C), L("posu", 0, a, b)))
        for a, b in CI_CUT:
            tt(A("ci", a, b), IND(A("u1", 0, C), L("posu", 0, a, b)), A("c0", a, b), ALU.is_le)
            scan(A("ci", C + a, C + b), A("one", a, b), A("ci", a, b), A("ci", C + a - 1, C + a) if a else 2.0, ALU.mult, ALU.add)
            scan(A("exs", a, b), A("mz", a, b), A("ci", a, b), 0.0, ALU.add, ALU.max)
            pick(A("exs", C + a, C + b), A("ci", C + a, C + b))
        tt(A("t40", 0, 20), w16("exs", 0, 20), K2, ALU.mult)
        tt(A("t40", 20, 40), K3, A("t40", 0, 20), ALU.subtract)
        tt(T20, w16("exs", 20, 40), A("t40", 20, 40), ALU.add)
        ts(A("destu", 0, 20), T20, SCL, ALU.mult)
        scatter(A("win", 0, WW), A("destu", 0, 20), A("iota", 1, C + 1))
        pick(A("exf", 0, S), A("win", 0, S))
        ts(A("cposu", 0, 10), w16("exf", 0, 10), SCL, ALU.mult, -1.0, ALU.add)
        CP = A("cposu", 0, 10)
        for b in range(4):
            take("vsvs"[b], A("et", b, 4 * S, 4), IND(A("f2", FW * b, FW * b + C + 1), CP))
        qe, se, lq, ls = "qe%d" % r, "se%d" % r, "lq%d" % r, "ls%d" % r
        quant(A(qe, 0, S), A(se, 0, S), A("et", 0, 4 * S))
        arr = T.sem["arr%d" % r]
        add("g", (lambda qe, lq, arr: lambda: g.remote_dma(T[lq][:, 0:S].bitcast(dt.uint8), T[qe][:, 0:S].bitcast(dt.uint8), arr, T.sem.sent, pid, rid, omask))(qe, lq, arr),
            [], [A(qe, 0, S)], 100.0, sem="remote")
        add("g", (lambda se, ls, arr: lambda: g.remote_dma(T[ls][:, 0:S], T[se][:, 0:S], arr, T.sem.sent, pid, rid, omask))(se, ls, arr),
            [], [A(se, 0, S)], 100.0, sem="remote")
        add("far", None, [A("trip", r, r + 1)], [A(qe, 0, S)], TRIP, sem="trip")

        PU, S1, FQ, S2 = A("pu", 0, 20), A("s1u", 0, 20), A("fqu", 0, 20), A("s2u", 0, 20)
        for k in (1, 2, 3):
            act(A("x1g", C * k, C * k + C), IND(A("ci", 0, C), A("nu", 20 * k - 20, 20 * k)), scale=P15, bias=P15)
            pick(A("ex", C * k, C * k + C), A("x1g", C * k, C * k + C))
        ts(A("cz", 0, 20), w16("exs", 0, 20), MID, ALU.is_gt, SURE, ALU.mult)
        tt(A("tf", 0, 20), OWNB, A("cz", 0, 20), ALU.add)
        ts(A("tp", 0, 20), A("tf", 0, 20), OWN + C * BIG, ALU.max)
        for a, b in PQ_CUT:
            ts(A("cz", a, b), w16("ex", a, b), 1.5 * BIG, ALU.is_gt, SURE, ALU.mult)
            tt(A("tp", a, b), A("wm", a, b), A("cz", a, b), ALU.add)
            tt(A("tf", a, b), A("wm", a, b), A("cz", a, b), ALU.subtract)
        for k, nm in enumerate(("tp", "tf")):
            a = 40 * k
            tt(A("tq", a, a + 20), A(nm, 0, 20), A(nm, 20, 40), ALU.max)
            tt(A("tq", a + 20, a + 40), A("tq", a, a + 20), A(nm, 40, 60), ALU.max)
            tt(A("mi", 40 + 20 * k, 60 + 20 * k), A("tq", a + 20, a + 40), A(nm, 60, 80), ALU.max)
        ts(A("mj", 40, 80), A("mi", 40, 80), 9, ALU.logical_shift_right, int(BIG) - 1, ALU.bitwise_and)
        cp(PU, A("mj", 40, 60))
        cp(FQ, A("mj", 60, 80))
        for q, (a, b) in zip(R_ON[0], parts):
            take(q, A("r1", a, b), IND(A("ci", C, 2 * C + 1), L("pu", 0, a, b)))
        for q, (a, b) in zip(R_ON[1], parts):
            take(q, A("r2", a, b), IND(A("r1", 0, C), L("fqu", 0, a, b)))
        for src, tmp, out in (("r1", "ex", "s1u"), ("r2", "exs", "s2u")):
            for a, b in parts:
                pick(A(tmp, a, b), A(src, a, b))
            ts(A(out, 0, 20), w16(tmp, 0, 20), SCL, ALU.mult)

        add("far", None, [A(lq, 0, S), A(ls, 0, S)], [A("trip", r, r + 1)] + [S1, FQ, S2][:EDGE], 0.0,
            sem="arr%d" % r, n=2 * n_in, late=-WAKE)
        for p in range(4):
            mm(A("ph", 512 * p, 512 * p + S), A("qw", 128 * p, 128 * p + 128), A("sw", 128 * p, 128 * p + 128), A(lq, 0, S), A(ls, 0, S))
            h, src = A("hh", HW * p + 3, HW * p + S + 3), A("ph", 512 * p, 512 * p + S)
            if HH_ON[p] == "v":
                ts(h, src, 2.0 ** -6, ALU.mult)
            else:
                act(h, src, scale=2.0 ** -6)
            HP = A("hh", HW * p, HW * p + S + 3)
            for q, (a, b) in zip(P_ON[p], xparts if len(P_ON[p]) == 2 else [(0, C)]):
                take(q, A("t2", C * p + a, C * p + b), IND(HP, L("s1u", 0, a, b)))
            for q, (a, b) in zip(Q_ON[p], xparts if len(Q_ON[p]) == 2 else [(0, C)]):
                t2, t3, t = (A(nm, C * p + a, C * p + b) for nm in ("t2", "t3", "tt"))
                if q == "g":
                    tt(t, IND(HP, L("s2u", 0, a, b)), t2, ALU.add)
                    continue
                if q == "z":
                    act(t3, IND(HP, L("s2u", 0, a, b)))
                else:
                    take(q, t3, IND(A("t2", C * p, C * p + C), L("fqu", 0, a, b)))
                for lo, hi in xparts:
                    if a <= lo and hi <= b:
                        tt(A("tt", C * p + lo, C * p + hi), A("t3", C * p + lo, C * p + hi), A("t2", C * p + lo, C * p + hi), ALU.add)
            for a, b in xparts:
                tt(A("xa", 4 * a + p, 4 * b, 4), A("pd", 512 * p + a, 512 * p + b), A("tt", C * p + a, C * p + b), ALU.add)
        if last:
            act(A("prep", 0, C), IND(A("tabp", 0, C + 1), PU))
            dma("y", T.op[:], T.prep[0:128:16, 0:C], [], [A("prep", 0, C)])
        for a, b in xparts:
            quant(A("qx", a, b), A("sx", a, b), A("xa", 4 * a, 4 * b))
            ops[-1]["lead"] = 0.0 if a else AHEAD

    for k, (a, b) in enumerate(xparts):
        dma("y", T.oc[:, 4 * a:4 * b], T.qx[:, a:b].bitcast(dt.uint8), [], [A("qx", a, b)], 500.0)
        mm(A("ph", 512 * k, 512 * k + b - a), A("qv", 0, 128), A("sv", 0, 128), A("qx", a, b), A("sx", a, b))
        take("sv"[k], A("yo", a, b), A("ph", 512 * k, 512 * k + b - a))
        dma("sy"[k], T.y[:, a:b], T.yo[:, a:b], [], [A("yo", a, b)], 500.0)
    for k in range(4):
        dma("s", T.osc[4 * k:4 * k + 4, :], T.sx[32 * k:32 * k + 4, 0:C], [], [SX])

    seen = {}
    for i, o in enumerate(ops):
        deps = set()
        for kind, keys in (("r", o["r"]), ("w", o["w"])):
            for (nm, a, b, st) in keys:
                ps = SCRATCH[nm][0] == "psum"
                for (j, kj, aj, bj, sj) in seen.get(nm, []):
                    if j == i or aj >= b or a >= bj or (st == sj and (a - aj) % st):
                        continue
                    if (kj == "w" or kind == "w" or (ps and ops[j]["q"] != o["q"])) and ops[j]["sem"] != "remote":
                        deps.add(j)
        for kind, keys in (("r", o["r"]), ("w", o["w"])):
            for (nm, a, b, st) in keys:
                if kind == "w" and st == 1:
                    seen[nm] = [e for e in seen.get(nm, []) if not (a <= e[2] and e[3] <= b)]
                seen.setdefault(nm, []).append((i, kind, a, b, st))
        o["deps"] = deps

    every = range(len(ops))
    ns = [o["ns"] for o in ops]
    before = [[(j, ops[j]["late"] + WAKE) for j in o["deps"]] for o in ops]
    after = [[] for o in ops]
    for i in every:
        for j, gap in before[i]:
            after[j].append((i, gap))

    def lay(rank, needs, feeds, first):
        start, ready, left = [0.0] * len(ops), list(first), [len(n) for n in needs]
        free, pool = {}, {}
        for i in every:
            if not left[i]:
                pool.setdefault(ops[i]["q"], []).append(i)
        for _ in every:
            bids = []
            for q, line in pool.items():
                if line:
                    now = free.get(q, 0.0)
                    line.sort(key=lambda i: (-rank[i], i))
                    limit, bid = None, None
                    for i in line:
                        t = max(now, ready[i])
                        if limit is None or t + ns[i] <= limit + FIT:
                            if bid is None or t < bid[0]:
                                bid = (t, i)
                            limit = t if limit is None else min(limit, t)
                        if t <= now and bid[0] <= now:
                            break
                    bids.append(bid)
            t, i = min(bids)
            start[i], free[ops[i]["q"]] = t, t + ns[i]
            pool[ops[i]["q"]].remove(i)
            for j, gap in feeds[i]:
                ready[j] = max(ready[j], t + ns[i] + gap)
                left[j] -= 1
                if not left[j]:
                    pool.setdefault(ops[j]["q"], []).append(j)
        return start

    tail = [0.0] * len(ops)
    for i in reversed(every):
        tail[i] = ns[i] + ops[i].get("lead", 0.0) + max([tail[j] + gap for j, gap in after[i]] + [ops[i]["late"]])
    urge = [[(j, gap + ops[j].get("lead", 0.0)) for j, gap in n] for n in before]
    found = []
    for _ in range(PASSES):
        start = lay(tail, before, after, [o.get("from", 0.0) for o in ops])
        found.append((max(start[i] + ns[i] + ops[i]["late"] for i in every), len(found), start))
        back = lay([start[i] + ns[i] for i in every], after, urge, [o["late"] for o in ops])
        tail = [back[i] + ns[i] for i in every]
    start = min(found)[2]
    order = sorted(every, key=lambda i: (start[i], i))
    place = {i: k for k, i in enumerate(order)}

    known = {}
    for i in order:
        o, keep = ops[i], []
        mine = known.setdefault(o["q"], {})
        for j in sorted(o["deps"], key=lambda j: -place[j]):
            k = ops[j]["sem"] or ops[j]["q"]
            if o["fn"] is not None and mine.get(k, -1) < place[j]:
                mine[k] = place[j]
                for k2, p2 in ops[j]["knew"].items():
                    mine[k2] = max(mine.get(k2, -1), p2)
                keep.append(j)
                ops[j]["used"] = True
        o["deps"], o["knew"] = keep, dict(mine)
    qsem = {"v": "cv", "s": "cs", "t": "ct", "g": "cg"}
    eng = {"v": g.vector, "s": g.scalar, "t": g.tensor, "g": g, "y": g.sync}
    count = {}
    for i in order:
        o = ops[i]
        if o["sem"] is None:
            o["sn"] = qsem[o["q"]]
            if o["used"]:
                count[o["sn"]] = count.get(o["sn"], 0) + 1
            o["at"] = count.get(o["sn"], 0)
        else:
            o["sn"], o["at"] = o["sem"], o["n"]
    for i in order:
        o = ops[i]
        if o["fn"] is None:
            continue
        for j in o["deps"]:
            eng[o["q"]].wait_ge(T.sem[ops[j]["sn"]], ops[j]["at"])
        ins = o["fn"]()
        if o["sem"] is None:
            if o["used"]:
                ins.then_inc(T.sem[o["sn"]], 1)
        elif o["sem"] != "remote":
            ins.then_inc(T.sem[o["sem"]], 16)
    g.wait_ge(T.sem.sent, 2 * ROUNDS * n_out)
    for o in ops:
        if o["fn"] is not None and o["sem"] not in (None, "remote") and not o["used"]:
            g.wait_ge(T.sem[o["sem"]], 16)
